import numpy as np, ml_dtypes
CORES = [2,6,10,14,18,22,26,30]
N = 8
BF = ml_dtypes.bfloat16
V, G, W, CAP, QA, QB, RO = 1024, 512, 2048, 96, 4, 4, 4
def deal(rng, a):
    return np.stack([rng.permutation(np.resize(np.array(a), 8)) for q in range(N)])
def parts(rng):
    sh = (N, 8, 16, V)
    mid = rng.integers(20, 236, (N, 8, 16, 16)); kin = rng.integers(0, 16, (N, 8, 1, V))
    x = np.take_along_axis(mid, kin, 3) + rng.integers(-20, 21, sh)
    low = deal(rng, [0.003, 0.01, 0.03])[:, :, None, None]; flat = deal(rng, [0, 1])[:, :, None, None] == 1
    r = np.where(flat, 255, rng.integers(130, 256, sh)); r = np.where(rng.random(sh) < low, rng.integers(1, 130, sh), r)
    p = np.where(rng.random(sh) < 0.15, rng.integers(1, 130, sh), 0)
    keep = deal(rng, [0.4, 0.7, 0.9])[:, :, None, None]
    s = np.where(rng.random(sh) < keep, np.arange(V), rng.integers(0, W, sh))
    c = np.where(rng.random(sh) < 0.5, rng.integers(0, V, sh), rng.integers(0, W, sh))
    h = deal(rng, [180, 230, 500, 1000, 1200]) + rng.integers(0, 32, (N, 8))
    return x, r, p, c, s, h
def pack(x, r, p, c, s, h):
    v = {"x": x, "reach": r, "past": p}
    d = {k: np.ascontiguousarray(v[k].reshape(N, 128, V)).astype(np.float32).astype(BF) for k in v}
    d["cand"] = np.ascontiguousarray(c.reshape(N, 128, V)).astype(np.int32); d["succ"] = np.ascontiguousarray(s.reshape(N, 128, V)).astype(np.int32)
    d["th"] = h.reshape(N, 8, 1).astype(np.int32)
    return d
def setup_inputs(rng):
    return pack(*parts(rng))
def setup_inputs_ends(rng):
    sh = (N, 8, 16, V); one = (N, 8, 1, V)
    x = 255 * np.where(rng.random(one) < 0.7, rng.integers(0, 2, one), rng.integers(0, 2, sh))
    x = np.where((rng.random(one) < 0.2) & (rng.random(sh) < 0.3), x + np.where(x == 0, 1, -1), x)
    k = rng.random(one); r = np.where(k < 0.5, 255, np.where(k < 0.6, 1, np.where(rng.random(sh) < 0.5, 1, 255)))
    p = 255 * ((rng.random(one) < 0.25) & (rng.random(sh) < 0.2)).astype(np.int64)
    c = np.where(rng.random(sh) < 0.65, (W - 1) * rng.integers(0, 2, sh), rng.integers(0, W, sh))
    s = np.where((rng.random(one) < 0.5) | (rng.random(sh) < 0.65), (W - 1) * rng.integers(0, 2, sh), rng.integers(0, W, sh))
    h = 4095 * rng.integers(0, 2, (N, 8)); h[:, 0] = 0; h[:, 4] = 4095; h[:, 7] = 4095
    for a in (0, 1, V - QA, V - 1, G - 1): p[..., a] = 0; r[..., a] = 255
    p[..., 2] = 255; r[..., 2] = 1; x[..., 0] = 0; x[..., V - QA] = 0
    for a in (1, V - 1): x[:, 1::2, :, a] = 255; x[:, ::2, :, a] = 0
    c[..., 0] = 2; c[:, :, 15, 0] = V - 1
    c[..., V - QA] = 2; c[:, :, 14, V - QA] = V - 1; c[:, :, 15, V - QA] = 1
    s[..., 0] = 0; s[..., G - 1] = W - 1
    return pack(x, r, p, c, s, h)
def setup_inputs_corners(rng):
    x, r, p, c, s, h = parts(rng); act = np.arange(0, G, QB); here = np.arange(V); ptr = np.array([0, V - 1, V, V + G - 1, V + G, W - 1])
    for q in range(N):
        for g in range(8):
            k = (g + q) % 8
            if k < 6:
                n = (0, 1, CAP - 1, CAP, CAP + 1, len(act))[k]; a = rng.permutation(act)[:n]
                h[q, g] = 0; x[q, g] = x[q, g][:, rng.integers(0, 16, V)]; r[q, g] = 200; r[q, g, :, V - 1] = 5
                p[q, g] = np.where(rng.random((16, V)) < 0.05, 10, 0)
                w = np.tile(here, (16, 1)); w[rng.integers(0, 16, n), a] = V - 1; s[q, g] = w
            elif k == 6:
                h[q, g] = 4095; p[q, g] = 0; c[q, g] = here - here % QA + (here + QA - 1) % QA
            else:
                h[q, g] = 4095; full = rng.random(V) < 0.5; full[0] = True; full[V - 1] = False; m = rng.random(V) < 0.5; n = int(np.count_nonzero(m))
                w = p[q, g].copy(); w[:, full] = 255; p[q, g] = w
                w = np.where(rng.random((16, V)) < 0.5, rng.integers(V, W, (16, V)), (here + QA * rng.integers(0, V // QA, (16, V))) % V)
                w[:, m] = rng.choice(here[full], (16, n)); w[15, m] = rng.integers(0, V, n); c[q, g] = w
                s[q, g] = np.where(rng.random((16, V)) < 0.3, here, ptr[rng.integers(0, 6, (16, V))])
    return pack(x, r, p, c, s, h)
def setup_inputs_ties(rng):
    x, r, p, c, s, h = parts(rng); sh = (N, 8, 16, V)
    x = 8 * rng.integers(0, 2, sh); pool = rng.integers(0, V, (N, 8, 1, 24)); pool[..., 0] = 0; pool[..., 1] = V - 1; pool[..., 2] = V; pool[..., 3] = W - 1
    few = np.take_along_axis(pool, rng.integers(0, 24, sh), 3); c[:, ::2] = few[:, ::2]
    m = np.arange(16)[:, None] == rng.integers(0, 16, (N, 8, 1, 1))
    r = np.where(m, rng.integers(100, 102, sh), rng.integers(101, 256, sh)); p = np.where(m, rng.integers(99, 101, sh), 0)
    h = deal(rng, [24, 32, 40, 48, 64])
    return pack(x, r, p, c, s, h)
def setup_inputs_border(rng):
    x, r, p, c, s, h = parts(rng); x = rng.integers(0, 256, x.shape); h = rng.integers(1, 33, h.shape); s[...] = np.arange(V)
    goal = np.zeros((N, 8, 3), np.int64); e, y, w = G - 1, V - 3, V - 2
    for q in range(N):
        for g in range(8):
            n, turn = ((0, 0), (0, int(rng.integers(1, 3))), (CAP - 1, 0), (CAP, 0), (CAP + 1, 0), (G, 0))[(g + q) % 6]
            o = [4 * rng.permutation(G // 4 - 1) + i for i in range(4)]
            v = o[turn][0]; j = o[0][1]; v1 = o[1][1]; u = o[1][2]; b = o[3][1]; z = o[3][2]
            for a in (v, e, j, y, v1, w, u, b): s[q, g, :, a] = z; c[q, g, :, a] = rng.integers(V, W, 16)
            for a in (v, v1, u): r[q, g, :, a] = rng.integers(140, 200, 16); p[q, g, :, a] = rng.integers(0, 41, 16)
            for a in (e, j): r[q, g, :, a] = rng.integers(200, 255, 16); p[q, g, :, a] = 0
            for a in (y, w): r[q, g, :, a] = 255; p[q, g, :, a] = 0
            r[q, g, :, z] = 255; r[q, g, :, V - 1] = 1
            i, k = rng.integers(0, 16, 2); d = int(rng.integers(1, 41))
            r[q, g, :, b] = r[q, g, :, u]; p[q, g, :, b] = p[q, g, :, u]; r[q, g, i, b] -= d; p[q, g, k, b] += d
            for a, f in ((v, e), (j, y), (v1, y), (w, y), (u, b)): x[q, g, :, a] = x[q, g, :, f]
            for a, f in ((v, e), (j, y), (v1, j), (w, y), (u, b)): c[q, g, int(rng.integers(0, 16)), a] = f
            a = rng.permutation(np.setdiff1d(np.arange(0, G, QB), np.array([v, j])))[:n]
            s[q, g][rng.integers(0, 16, len(a)), a] = V - 1
            goal[q, g] = (e, u, j)
    k = np.arange(G, V - 3)
    for q in range(N):
        for g in range(8):
            see = np.concatenate([V + goal[(q + 1) % N, g], V + G + goal[(q - 1) % N, g]])
            r[q, g, :, G:V - 3] = 255; p[q, g, :, G:V - 3] = 0
            s[q, g][rng.integers(0, 16, len(k)), k] = see[((k - G) // 4) % 6]
    return pack(x, r, p, c, s, h)
def setup_inputs_spread(rng):
    sh = (N, 8, 16, V); one = (N, 8, 1, V)
    def uneven(): return np.floor(np.exp2(8 * rng.random(one)) * rng.random(sh)).astype(np.int64)
    def lean():
        e = deal(rng, [1.0, 2.0, 4.0])[:, :, None, None]; v = np.minimum((W * rng.random(sh) ** e).astype(np.int64), W - 1)
        return np.where(deal(rng, [0, 0, 1])[:, :, None, None] == 1, W - 1 - v, v)
    x = uneven(); r = np.maximum(255 - uneven(), 1); p = np.where(rng.random(one) < 0.3, uneven(), 0)
    c = lean(); s = np.where(rng.random(one) < rng.random(sh), np.arange(V), lean())
    h = np.minimum(np.floor(np.exp2(12 * rng.random((N, 8)))).astype(np.int64), 4095)
    return pack(x, r, p, c, s, h)
def check_inputs(d):
    bad = []
    for k, lo, hi in (("x", 0, 255), ("reach", 1, 255), ("past", 0, 255), ("cand", 0, W - 1), ("succ", 0, W - 1), ("th", 0, 4095)):
        a = np.asarray(d[k]).astype(np.float64)
        if not (np.all(a >= lo) and np.all(a <= hi)): bad.append("range of " + k)
        elif not np.all(a == np.floor(a)): bad.append("whole numbers in " + k)
    return bad
def at(a, ix):
    return np.take_along_axis(a, ix[:, :, None, :], 3)
def reference(x, reach, past, cand, succ, th):
    X = x.astype(np.float32).astype(np.int32).reshape(N, 8, 16, V)
    R = reach.astype(np.float32).astype(np.int32).reshape(N, 8, 16, V); P = past.astype(np.float32).astype(np.int32).reshape(N, 8, 16, V)
    R = np.concatenate([R, np.roll(R[..., :G], -1, axis=0), np.roll(R[..., :G], 1, axis=0)], axis=3)
    P = np.concatenate([P, np.roll(P[..., :G], -1, axis=0), np.roll(P[..., :G], 1, axis=0)], axis=3)
    C = cand.astype(np.int64).reshape(N, 8, 16, V); S = succ.astype(np.int64).reshape(N, 8, 16, V); H = th.astype(np.int64).reshape(N, 8)
    F = np.zeros((N, 8, W), np.int64) + np.arange(W); M = np.zeros(N, np.int64); odd = (np.arange(16) % 2 == 1)[:, None]; NONE = 2 ** 20
    qi, gi = np.arange(N)[:, None, None], np.arange(8)[None, :, None]
    for t in range(RO):
        r_old, p_old, f_old = R[..., :G].copy(), P[..., :G].copy(), F[..., :G].copy()
        a = slice(t % QA, V, QA); v = np.arange(t % QA, V, QA); L = len(v)
        c = np.take_along_axis(F, C[..., a].reshape(N, 8, 16 * L), 2)
        xc, rc, pc = [at(w, i).reshape(N, 8, 16, 16, L) for w, i in ((X, np.minimum(c, V - 1)), (R, c), (P, c))]
        xv, rv, pv = [w[..., a][:, :, :, None, :] for w in (X, R, P)]
        c = c.reshape(N, 8, 16, L); ordered = np.any((rv <= pc) | (rc <= pv), axis=2)
        fit = ~ordered & (c < V) & (c % QA != t % QA)
        D = np.where(fit, np.add.reduce(np.abs(xc - xv), axis=2), NONE)
        k = np.argmin(D, axis=2)[:, :, None, :]
        b = np.take_along_axis(c, k, 2)[:, :, 0]; D = np.take_along_axis(D, k, 2)[:, :, 0].astype(np.int64); has = D < NONE; b = np.where(has, b, 0)
        C[..., a] = np.where(ordered & has[:, :, None, :], at(C, b), C[..., a])
        asks = has & (D < H[:, :, None] + (M & 31)[:, None, None]); key = np.where(asks, D * V + v, 2 ** 40)
        best = np.full((N, 8, V), 2 ** 40, np.int64); np.minimum.at(best, (qi, gi, b), key)
        win = asks & (np.take_along_axis(best, b, 2) == key); m = win[:, :, None, :]
        xb, rb, pb, sb = at(X, b), at(R, b), at(P, b), at(S, b)
        X[..., a] = np.where(m, (X[..., a] + xb) >> 1, X[..., a])
        R[..., a] = np.where(m, np.minimum(R[..., a], rb), R[..., a]); P[..., a] = np.where(m, np.maximum(P[..., a], pb), P[..., a])
        S[..., a] = np.where(m & odd, sb, S[..., a])
        i, j, l = np.nonzero(win); F[i, j, b[i, j, l]] = v[l]
        M = np.add.reduce(win.astype(np.int64).reshape(N, -1), axis=1)
        a = slice(t % QB, V, QB); L = len(range(t % QB, V, QB))
        c = np.take_along_axis(F, S[..., a].reshape(N, 8, 16 * L), 2)
        low = np.min(at(R, c).reshape(N, 8, 16, 16, L), axis=3); R[..., a] = np.minimum(R[..., a], low)
        ch = np.any(R[..., :G] != r_old, axis=2) | np.any(P[..., :G] != p_old, axis=2) | (F[..., :G] != f_old)
        go = ch & (np.add.accumulate(ch.astype(np.int64), axis=2) <= CAP)
        for turn, o in ((-1, V), (1, V + G)):
            w = np.roll(go, turn, axis=0); m = w[:, :, None, :]; f = np.roll(F[..., :G], turn, axis=0)
            R[..., o:o + G] = np.where(m, np.roll(R[..., :G], turn, axis=0), R[..., o:o + G])
            P[..., o:o + G] = np.where(m, np.roll(P[..., :G], turn, axis=0), P[..., o:o + G])
            F[..., o:o + G] = np.where(w & (f < G), f + o, F[..., o:o + G])
    return {"yx": X.reshape(N, 128, V).astype(np.float32).astype(BF), "yr": np.ascontiguousarray(R[..., :V]).reshape(N, 128, V).astype(np.float32).astype(BF), "yc": C.reshape(N, 128, V).astype(np.float32)}

@@ -1,0 +1,618 @@
+from concourse.bass import DstId, RemoteDMATransfer
+from concourse.mybir import AluOpType, AxisListType, ActivationFunctionType as AF
+
+V, G5, RO, CAP = 1024, 512, 4, 96
+DUM, GH, RAW, WID = 256, 1280, 2304, 3328
+PEN = 16384.0
+B10 = 10.0 * 2 ** 20
+TESTS = (("P", 0, 2, "V"), ("P", 2, 2, "V"), ("P", 4, 2, "V"), ("P", 6, 2, "V"), ("R", 0, 2, "V"), ("R", 2, 1, "V"), ("R", 3, 1, "S"), ("R", 4, 2, "S"), ("R", 6, 2, "S"))
+TESTS0 = tuple((k, i, n, "S" if (k, i) == ("R", 6) else "V") for k, i, n, _ in TESTS)
+SUCC = ((0, 1024), (1024, 2048), (2048, 3072), (3072, 4096))
+PAIRS = "SVSVSVSVSVSVSVSV"
+
+SCRATCH, PLACE = {}, {}
+SIZE = {"bfloat16": 2, "uint16": 2, "float32": 4, "int32": 4}
+
+
+def _b(names, cols, dtype, where="sbuf"):
+    for name in names.split():
+        if where == "sbuf" and cols <= 512:
+            pool = "pool_" + dtype
+            at = SCRATCH.get(pool, (where, [128, 0], dtype))[1][1]
+            step = 32 // SIZE[dtype]
+            SCRATCH[pool] = (where, [128, at + -(-cols // step) * step], dtype)
+            PLACE[name] = (pool, at, cols)
+        else:
+            SCRATCH[name] = (where, [128, cols], dtype)
+            PLACE[name] = (name, 0, cols)
+
+
+_b("xb rb pb", WID, "bfloat16")
+_b("fl vi nv", DUM + V, "float32"); _b("idf", 128, "float32")
+_b("ci si", V, "int32")
+_b("cb sb", V, "float32")
+for _t in range(RO):
+    _b("rr%d pr%d" % (_t, _t), 1024, "bfloat16")
+    _b("ct%d" % _t, 256, "uint16"); _b("ca%d" % _t, 256, "float32")
+    _b("xa%d rn%d pn%d" % (_t, _t, _t), 256, "bfloat16"); _b("z%d" % _t, 32, "uint16")
+    _b("lra%d lrb%d lpa%d lpb%d" % (_t, _t, _t, _t), 128, "bfloat16")
+    _b("lz%d" % _t, 64, "uint16")
+_b("xg ad tp tr sg sc gp", 4096, "bfloat16")
+_b("rwa rwb pwa pwb", 1024, "bfloat16")
+_b("rva rvb pva pvb", 512, "bfloat16")
+_b("wm", 2048, "bfloat16"); _b("em", 2048, "float32")
+_b("idm ngm bom ltm sb2m onm", 128, "bfloat16"); _b("b8", 128, "float32")
+_b("sc10 sc13 sw " + " ".join("se%d" % r for r in range(10, 16)), 1, "float32"); _b("ic", 256, "float32")
+_b("ia ib", 256, "int32"); _b("id_ ie ig ih ij ik in_", 128, "int32"); _b("iq", 1024, "int32")
+_b("pc", 8, "int32"); _b("cc", 48, "float32"); _b("g8", 8, "bfloat16"); _b("lh", 128, "bfloat16"); _b("lw", 16, "float32")
+_b("dg", 512, "bfloat16"); _b("thr sg1", 256, "float32"); _b("smx", 1024, "bfloat16")
+_b("kc cll clr", 256, "bfloat16"); _b("rq", 96, "bfloat16"); _b("one", 32, "float32")
+_b("o2 ofin oq omx", 16, "uint16"); _b("oke", 32, "uint16")
+_b("in12 tr12", 512, "float32")
+_b("key", 256, "int32"); _b("k8", 128, "int32"); _b("k4", 64, "int32"); _b("k2", 32, "int32"); _b("mk", 16, "int32")
+_b("eq prd", 256, "float32"); _b("s8", 128, "float32"); _b("s4", 64, "float32"); _b("s2", 32, "float32")
+_b("s1 has ask nli bc pen", 16, "float32"); _b("nl bcu", 16, "uint16"); _b("fsh fbt", 256, "int32")
+_b("bits fev fod fr junk we os", 256, "bfloat16"); _b("bm bs cd od sx sev", 256, "float32"); _b("kl", 32, "int32"); _b("ke", 512, "bfloat16")
+_b("mx", 16, "float32"); _b("nb3 d3 t3", 48, "float32"); _b("l3", 48, "uint16"); _b("v3", 192, "float32"); _b("so", 256, "uint16")
+_b("xs xh", 256, "int32"); _b("r2 nsm0 nsm1", 256, "bfloat16")
+_b("wn", 16, "bfloat16"); _b("mt", 2, "float32"); _b("mi", 2, "int32"); _b("thi", 8, "int32"); _b("thf", 8, "float32")
+_b("dr dp", 128, "bfloat16")
+_b("fvs e5 flt dfl c96 go ge gf zf", 32, "float32"); _b("fli", 32, "int32"); _b("chf ch scq", 32, "bfloat16")
+_b("zi fi ei jl", 64, "int32"); _b("fu eu", 64, "uint16")
+_b("p0 p1 p2 p3 p4 p5 p6 p7", 512, "float32", "psum")
+SEMAPHORES = ["qV", "qS", "qP", "qG", "inA", "inB"] + ["d%d" % i for i in range(24)] + ["ls%d" % i for i in range(12)] + \
+    ["%s%s%d" % (a, s, t) for a in ("ar", "ap", "az") for s in "AB" for t in range(RO - 1)]
+
+
+def rank_program(g, core, T, topo):
+    rank = T.rank_of(core)
+    if rank is None:
+        return
+    O = AluOpType
+    queues = {"V": g.vector, "S": g.scalar, "P": g.tensor, "G": g, "D": g.sync}
+    cnt = {"qV": 0, "qS": 0, "qP": 0, "qG": 0}
+    know = {q: {} for q in queues}
+    snap, hist, free = {}, {}, {"d": 0, "ls": 0}
+
+    def A(name, a=None, b=None, s=1, p0=0, p1=128):
+        buf, at, cols = PLACE[name]
+        t = T[buf]
+        a = 0 if a is None else a
+        b = cols if b is None else b
+        return {"n": name, "a": a, "b": b, "s": s, "ap": t[p0:p1, at + a:at + b:s] if s != 1 else t[p0:p1, at + a:at + b]}
+
+    def wait(q, sem, val):
+        if know[q].get(sem, 0) < val:
+            queues[q].wait_ge(T.sem[sem], val)
+            for k, v in snap.get((sem, val), {}).items():
+                if know[q].get(k, 0) < v: know[q][k] = v
+            know[q][sem] = val
+
+    def deps(q, reads, writes):
+        need = {}
+        for acc, w in [(r, False) for r in reads] + [(r, True) for r in writes]:
+            ps = SCRATCH[PLACE[acc["n"]][0]][0] == "psum"
+            for e in hist.get(acc["n"], ()):
+                if e[3] == q and ps and q == "P": continue
+                if (w or e[2] or (ps and e[3] != q)) and (ps or (acc["a"] < e[1] and e[0] < acc["b"])):
+                    if need.get(e[4], 0) < e[5]: need[e[4]] = e[5]
+        for s in sorted(need): wait(q, s, need[s])
+
+    def note(q, sem, val, reads, writes):
+        snap[(sem, val)] = dict(know[q])
+        for acc, w in [(r, False) for r in reads] + [(r, True) for r in writes]:
+            h = hist.setdefault(acc["n"], [])
+            if w and acc["s"] == 1:
+                h[:] = [e for e in h if not (acc["a"] <= e[0] and e[1] <= acc["b"])]
+            else:
+                h[:] = [e for e in h if not (e[4] == sem and e[2] == w and e[0] == acc["a"] and e[1] == acc["b"])]
+            h.append((acc["a"], acc["b"], w, q, sem, val))
+
+    def run(q, fn, writes, reads):
+        deps(q, reads, writes)
+        s = "q" + q
+        cnt[s] += 1
+        fn().then_inc(T.sem[s], 1)
+        note(q, s, cnt[s], reads, writes)
+
+    def dma(q, out, in_, reads, writes):
+        deps(q, reads, writes)
+        s = "d%d" % free["d"]; free["d"] += 1
+        queues[q].dma_start(out, in_).then_inc(T.sem[s], 16)
+        note(q, s, 16, reads, writes)
+
+    def ind(win, off): return {"ap": win["ap"].indirect(off["ap"]), "w": win, "o": off}
+    def rd(x): return [x["w"], x["o"]] if "w" in x else [x]
+    def cp(out, in_): run("V", lambda: g.vector.tensor_copy(out["ap"], in_["ap"]), [out], rd(in_))
+    def scat(win, off, in_): run("V", lambda: g.vector.tensor_copy(win["ap"].indirect(off["ap"]), in_["ap"]), [win], [off, in_])
+    def tt(out, a, b, op): run("V", lambda: g.vector.tensor_tensor(out["ap"], a["ap"], b["ap"], op), [out], rd(a) + [b])
+    def ts(out, a, s1, op0, s2=None, op1=None):
+        r = rd(a) + [s for s in (s1, s2) if isinstance(s, dict)]
+        v1 = s1["ap"] if isinstance(s1, dict) else s1
+        v2 = s2["ap"] if isinstance(s2, dict) else s2
+        if op1 is None: run("V", lambda: g.vector.tensor_scalar(out["ap"], a["ap"], v1, None, op0), [out], r)
+        else: run("V", lambda: g.vector.tensor_scalar(out["ap"], a["ap"], v1, v2, op0, op1), [out], r)
+    def scan(out, d0, d1, init, op0, op1): run("V", lambda: g.vector.tensor_tensor_scan(out["ap"], d0["ap"], d1["ap"], init, op0, op1), [out], [d0, d1])
+    def fill(out, v): run("V", lambda: g.vector.memset(out["ap"], v), [out], [])
+    def reduce(out, in_, op): run("V", lambda: g.vector.tensor_reduce(out["ap"], in_["ap"], AxisListType.X, op), [out], [in_])
+    def act(out, in_, func=AF.Copy, bias=0.0, scale=1.0, acc=None):
+        r = rd(in_) + [k for k in (bias, scale) if isinstance(k, dict)]
+        sc = scale["ap"] if isinstance(scale, dict) else scale
+        bi = bias["ap"] if isinstance(bias, dict) else bias
+        if acc is None: run("S", lambda: g.scalar.activation(out["ap"], in_["ap"], func, bias=bi, scale=sc), [out], r)
+        else: run("S", lambda: g.scalar.activation(out["ap"], in_["ap"], func, bias=bias, scale=sc, accum_out=acc["ap"]), [out, acc], r)
+    def mm(out, l, r, start, stop): run("P", lambda: g.tensor.matmul(out["ap"], l["ap"], r["ap"], start, stop), [out], [l, r])
+    def iota(out, pat, base=0, cm=0): run("G", lambda: g.iota(out["ap"], pat, base, cm), [out], [])
+    def iotf(out, pat, base=0, cm=0): run("G", lambda: g.iota(out["ap"], pat, base, cm, allow_small_or_imprecise_dtypes=True), [out], [])
+
+    nxt, prv = T.cores[(rank + 1) % 8], T.cores[(rank - 1) % 8]
+    far = [d for d in (nxt, prv) if topo.chip(d) != topo.chip(core)]
+    eng = {}
+    for d in (nxt, prv):
+        e = topo.engines(core, d)
+        if d not in far: e = [i for i in e if not far or i not in topo.engines(core, far[0])] or e
+        elif len(far) == 2: e = e[:len(e) // 2] if d == far[0] else e[len(e) // 2:]
+        eng[d] = e
+
+    def send(pairs, sems, n):
+        s = "ls%d" % free["ls"]; free["ls"] += 1
+        deps("G", [p[0] for p in pairs], [])
+        tr = []
+        for side, d in (("A", prv), ("B", nxt)):
+            rid, pid, _ = topo.addr(d)
+            for i, p in enumerate(pairs):
+                tr.append(RemoteDMATransfer(dst_ids=[DstId(rid=rid, pnc=pid)], dma_engine_mask=sum(1 << e for e in eng[d][i * n:i * n + n]),
+                                            remote_sem=T.sem[sems[i] % side], src=p[0]["ap"], dst=p[1 if side == "A" else 2]["ap"]))
+        g.remote_dma_fused(tr, local_sem=T.sem[s])
+        note("G", s, n * len(tr), [p[0] for p in pairs], [])
+
+    def arrive(sem, val, writes):
+        snap[(sem, val)] = {}
+        for w in writes: hist.setdefault(w["n"], []).append((w["a"], w["b"], True, "R", sem, val))
+
+    RWb = lambda n: A(n, RAW, RAW + V)
+    own = lambda n: A(n, DUM, GH)
+    gA, gB = (GH, GH + G5), (GH + G5, GH + 2 * G5)
+    dma("D", RWb("rb")["ap"], T.reach[:], [], [RWb("rb")])
+    dma("S", RWb("pb")["ap"], T.past[:], [], [RWb("pb")])
+    dma("D", A("ci")["ap"], T.cand[:], [], [A("ci")])
+    dma("S", own("xb")["ap"], T.x[:], [], [own("xb")])
+    dma("D", RWb("xb")["ap"], T.x[:], [], [RWb("xb")])
+    dma("D", own("rb")["ap"], T.reach[:], [], [own("rb")])
+    dma("D", own("pb")["ap"], T.past[:], [], [own("pb")])
+    dma("D", A("si")["ap"], T.succ[:], [], [A("si")])
+    dma("D", A("thi", 0, 1, p1=8)["ap"], T.th[:], [], [A("thi")])
+    c = lambda i: A("cc", i, i + 1)
+    ROW, P16, PF, ODD, SCL, RS, RG0, RG1, C1L, C1R, M12, M15, TH16, NG, LIM, EVR, W0, W1, W2, W3, W4 = range(21)
+    NRS, PM = 24, 28
+    rw, pp = A("pc", 1, 2), A("pc", 0, 1)
+    iota(pp, [[0, 1]], 0, 1)
+    iota(A("id_", 0, 16), [[32, 8], [-16, 2]], 16, 1)
+    iota(A("id_", 16, 32), [[1, 16]])
+    iota(A("ie"), [[1, 128]])
+    iota(A("ig", 0, 8), [[1, 8]])
+    iota(A("ia"), [[1, 16], [0, 16]])
+    iotf(A("xb", GH, RAW), [[0, RAW - GH]], int(PEN))
+    send([(A("rb", RAW, RAW + G5), A("rb", *gA), A("rb", *gB)), (A("pb", RAW, RAW + G5), A("pb", *gA), A("pb", *gB))], ["in%s", "in%s"], 4)
+    for n in ("rb", "pb"):
+        arrive("inA", 8, [A(n, *gA)]); arrive("inB", 8, [A(n, *gB)])
+    ts(rw, pp, 15, O.bitwise_and)
+    ts(A("pc", 2, 3), pp, 4, O.arith_shift_right)
+    ts(A("pc", 3, 4), pp, 4, O.arith_shift_right, 1, O.bitwise_and)
+    ts(A("pc", 4, 5), rw, 1, O.arith_shift_right)
+    ts(A("pc", 5, 6), rw, 1, O.bitwise_and)
+    cp(c(ROW), rw); cp(c(P16), A("pc", 2, 3)); cp(c(PF), pp); cp(c(RG1), A("pc", 3, 4)); cp(c(W0), A("pc", 4, 5)); cp(c(ODD), A("pc", 5, 6))
+    ts(c(RG0), c(RG1), -1.0, O.mult, 1.0, O.add)
+    ts(c(EVR), c(ODD), -1.0, O.mult, 1.0, O.add)
+    ts(c(NG), c(P16), -16.0, O.mult)
+    ts(A("o2"), A("id_", 0, 16), c(NG), O.add)
+    tt(c(W1), c(ODD), c(RG1), O.not_equal)
+    ts(c(W2), c(W0), 32.0, O.mult)
+    ts(c(W1), c(W1), 256.0, O.mult, c(W2), O.add)
+    ts(c(W2), c(RG1), 16.0, O.mult, c(W1), O.add)
+    ts(A("ofin"), A("id_", 16, 32), c(W2), O.add)
+    def tables():
+        ts(A("g8"), A("ig", 0, 8), c(P16), O.is_equal)
+        fill(A("wm"), 0.0)
+        for m in range(16): act(A("wm", 128 * m + m, 128 * m + 128, 16), A("g8"))
+        ts(A("idm"), A("ie"), c(PF), O.is_equal)
+        ts(A("ngm"), A("idm"), -1.0, O.mult)
+        ts(A("kc"), A("ia"), 2.0 ** -23, O.mult)
+        fill(A("smx"), 0.0); fill(A("smx", 0, 1024, 16), 255.0)
+        fill(A("sg1"), 1.0); fill(A("sg1", 0, 256, 16), 0.0)
+        fill(A("nsm0"), 0.0)
+
+    def row_tables():
+        fill(c(SCL), 1.0)
+        for b in range(4):
+            ts(A("pc", 7, 8), rw, b, O.arith_shift_right, 1, O.bitwise_and)
+            ts(c(W3), A("pc", 7, 8), 2.0 ** -(2 ** b) - 1.0, O.mult, 1.0, O.add)
+            tt(c(SCL), c(SCL), c(W3), O.mult)
+        eq, lt = {}, {}
+        for lim in (10, 13):
+            lt[lim] = A("sc%d" % lim)
+            act(A("sw"), c(ROW), AF.Sign, bias=lim - 0.5, scale=-1.0)
+            act(lt[lim], A("sw"), AF.Relu)
+        for r in (10, 11, 12, 13, 14, 15):
+            eq[r] = A("se%d" % r)
+            act(A("sw"), c(ROW), AF.Abs, bias=-float(r))
+            act(eq[r], A("sw"), AF.Relu, bias=1.0, scale=-1.0)
+
+        def total(i, parts):
+            for n, (m, v) in enumerate(parts):
+                act(c(i), m, AF.Identity, bias=c(i) if n else 0.0, scale=float(v))
+        total(RS, [(lt[10], 2 ** 20), (eq[10], 2 ** 14), (eq[11], 2 ** 8), (eq[12], 1), (eq[13], -2 ** 14), (eq[14], -2 ** 8), (eq[15], -1)])
+        total(C1L, [(lt[10], -1), (eq[13], 1), (eq[14], 1), (eq[15], 1)])
+        total(C1R, [(lt[10], -2), (lt[13], 1)])
+        act(c(W4), lt[10], scale=2.0)
+        act(A("cll"), A("ic"), AF.Identity, bias=c(C1L), scale=eq[12])
+        act(A("clr"), A("ic"), AF.Identity, bias=c(C1R), scale=eq[15])
+        act(A("sb2m"), A("idm"), scale=c(W4))
+        act(A("idf"), A("idm"))
+
+    def turn_a(t):
+        cp(A("in12", 0, 256), A("ci", t, V, 4))
+        act(A("in12", 256, 512), ind(A("in12", 0, 256), A("o2")))
+
+    def turn_v(t): run("V", lambda: g.vector.transpose(A("tr12")["ap"], A("in12")["ap"]), [A("tr12")], [A("in12")])
+
+    def turn_s(t): act(A("ca%d" % t), ind(A("tr12"), A("ofin")))
+
+    def list_b(t): cp(A("ct%d" % t), A("ca%d" % t))
+
+    def copies(t, f):
+        f(A("xa%d" % t), A("xb", RAW + t, RAW + V, 4))
+        for n in ("r", "p"):
+            for i in range(4): f(A("%sr%d" % (n, t), 256 * i, 256 * i + 256), A(n + "b", RAW + t, RAW + V, 4))
+
+    def squeeze(n, i, w, last):
+        for m in range(16):
+            mm(A("p4", 32 * i, 32 * (i + w)), A("wm", 128 * m, 128 * m + 128), A(n, 512 * i + m, 512 * (i + w), 16), False, last and m == 15)
+
+    def x_gather(t, i): act(A("xg", 1024 * i, 1024 * i + 1024), ind(A("xb", DUM, RAW), A("ct%d" % t, 64 * i, 64 * i + 64)))
+
+    def x_sub(t, i):
+        for h in (2 * i, 2 * i + 1):
+            p = "p%d" % (h % 4)
+            mm(A(p), A("idm"), A("xg", 512 * h, 512 * h + 512), True, False)
+            mm(A(p, 0, 256), A("ngm"), A("xa%d" % t), False, False)
+            mm(A(p, 256, 512), A("ngm"), A("xa%d" % t), False, True)
+
+    def distances(t):
+        mm(A("p4", 0, 256), A("idm"), A("kc"), True, False)
+        x_sub(t, 0)
+        for i in range(4):
+            if i < 3: x_sub(t, i + 1)
+            for h in (2 * i, 2 * i + 1): act(A("ad", 512 * h, 512 * h + 512), A("p%d" % (h % 4)), AF.Abs, scale=2.0 ** -19)
+            squeeze("ad", 2 * i, 2, False)
+
+    def tests(t):
+        todo, tv, tg = [], 0.0, 0.0
+        plan = TESTS if t else TESTS0
+        for kind, i, n, who in plan:
+            if who == "V":
+                todo.append((tv, 0, kind, i, n)); tv += 0.8 * n; todo.append((tv, 3, kind, i, n))
+            else:
+                todo.append((tg, 1, kind, i, n)); tg += 0.8 * n
+        for kind, i, n, who in plan:
+            if who == "S":
+                todo.append((tg, 2, kind, i, n)); tg += 0.65 * n; todo.append((tg, 3, kind, i, n))
+        left = len(plan)
+        for _, step, kind, i, w in sorted(todo):
+            win = A("pb" if kind == "P" else "rb", DUM, RAW)
+            mine = ("rr%d" if kind == "P" else "pr%d") % t
+            n = {"P": "tp", "R": "tr"}[kind]
+            off = A("ct%d" % t, 32 * i, 32 * (i + w))
+            if step == 0:
+                tt(A(n, 512 * i, 512 * (i + w)), ind(win, off), A(mine, 0, 512 * w), O.is_ge if kind == "P" else O.is_le)
+            elif step == 1:
+                act(A("gp", 512 * i, 512 * (i + w)), ind(win, off))
+            elif step == 2:
+                for h in range(i, i + w):
+                    p = "p%d" % (h % 4)
+                    mm(A(p), A("idm"), A("gp", 512 * h, 512 * h + 512), True, False)
+                    mm(A(p), A("ngm"), A(mine, 0, 512), False, True)
+                    act(A(n, 512 * h, 512 * h + 512), A(p), AF.Relu, bias=1.0, scale=1.0 if kind == "P" else -1.0)
+            else:
+                left -= 1
+                squeeze(n, i, w, left == 0)
+
+    def tree(srcs, op):
+        for i in range(len(srcs) - 1):
+            w = 128 >> i
+            tt(A(srcs[i + 1]), A(srcs[i], 0, w), A(srcs[i], w, 2 * w), op)
+
+    def partner(t):
+        ts(A("key"), A("p4", 0, 256), 2.0 ** 23, O.mult, 2.0 ** 22, O.min)
+        tree(("key", "k8", "k4", "k2", "mk"), O.min)
+        tt(A("eq"), ind(A("mk"), A("oq")), A("key"), O.is_equal)
+        tt(A("prd"), A("eq"), A("ca%d" % t), O.mult)
+        ts(A("has"), A("mk"), 65536.0, O.is_lt)
+        tree(("prd", "s8", "s4", "s2", "s1"), O.add)
+        tt(A("nli"), A("s1"), A("has"), O.mult)
+        cp(A("nl"), A("nli"))
+        fw = A("fl", DUM, DUM + V)
+        ts(A("fsh"), ind(fw, A("nl")), c(SCL), O.mult, -0.5 + 2.0 ** -11, O.add)
+        ts(A("kl", 0, 16), A("mk"), 10, O.arith_shift_right, 63, O.bitwise_and)
+        ts(A("fbt"), A("fsh"), 1, O.bitwise_and)
+        ts(A("pen"), A("mk"), c(LIM), O.is_ge, 128.0, O.mult)
+        ts(A("kl", 16, 32), A("mk"), 4, O.arith_shift_right, 63, O.bitwise_and)
+        cp(A("bits"), A("fbt"))
+        tt(A("kl", 0, 16), A("kl", 0, 16), A("pen"), O.add)
+        tt(A("ke"), ind(A("kl"), A("oke")), A("dg"), O.mult)
+        for p, cl in (("p6", "clr"), ("p5", "cll")): mm(A(p, 0, 256), A("idm"), A(cl), True, False)
+        for p in ("p6", "p5"): mm(A(p, 0, 256), A("sb2m"), A("bits"), False, False)
+        for p, r in (("p6", 13), ("p5", 10)):
+            mm(A(p, 0, 256), A("wm", 128 * r, 128 * r + 128), A("ke", 0, 256), False, False)
+            mm(A(p, 0, 256), A("wm", 128 * r + 128, 128 * r + 256), A("ke", 256, 512), False, True)
+        act(A("fr"), A("p6", 0, 256), scale=c(RS))
+        act(A("fev"), A("p5", 0, 256), scale=c(RG0))
+        act(A("fod"), A("p5", 0, 256), scale=c(RG1))
+        tt(A("bm"), ind(fw, A("nl")), A("dg", 0, 256), O.mult)
+        scan(A("bs"), A("sg1"), A("bm"), 0.0, O.mult, O.add)
+        v3 = A("v3", 48 * t, 48 * t + 48)
+        cp(A("nb3", 0, 16), A("nli"))
+        ts(A("nb3", 16, 32), A("bs", 15, 256, 16), float(DUM), O.add)
+        cp(A("nb3", 32, 48), A("bs", 15, 256, 16))
+        tt(A("d3"), A("nb3"), v3, O.subtract)
+        ts(A("ask"), A("mk"), c(LIM), O.is_lt)
+        tt(A("bc"), A("d3", 32, 48), A("has"), O.mult)
+        tt(A("bc"), A("bc"), A("v3", 48 * t + 32, 48 * t + 48), O.add)
+        for i in range(3): tt(A("d3", 16 * i, 16 * i + 16), A("d3", 16 * i, 16 * i + 16), A("ask"), O.mult)
+        cp(A("bcu"), A("bc"))
+        if t + 1 < RO: list_b(t + 1)
+        seen = {"V": 0, "S": 0}
+        for a in range(16):
+            gr, h, who = a // 2, a % 2, PAIRS[a]
+            p = {"V": ("p0", "p2", "p5"), "S": ("p1", "p3", "p6")}[who][seen[who] % 3]
+            seen[who] += 1
+            lo = 32 * (gr // 2)
+            mm(A(p, 0, 256), A("fod" if gr % 2 else "fev", 128 * h, 128 * h + 128, p0=lo, p1=lo + 32), A("fr", p0=lo, p1=lo + 32), True, True)
+            if who == "V": reduce(A("mx", a, a + 1), A(p, 0, 256), O.max)
+            else: act(A("junk"), A(p, 0, 256), AF.Relu, bias=-B10, acc=A("mx", a, a + 1))
+        tt(A("we"), ind(A("mx"), A("omx")), A("thr"), O.is_le)
+        for h in range(2): mm(A("p7", 0, 48), A("we", 128 * h, 128 * h + 128), A("rq", 48 * h, 48 * h + 48), h == 0, h == 1)
+        tt(A("t3"), A("p7", 0, 48), A("d3"), O.mult)
+        tt(A("t3"), A("t3"), v3, O.add)
+        cp(A("l3"), A("t3"))
+
+    nl2, sc, sl = A("l3", 0, 16), A("l3", 16, 32), A("l3", 32, 48)
+
+    def selfmark(n, t, new, p, sign, op):
+        w = A(n, DUM + t, GH, 4)
+        mm(A(p, 0, 256), A("idm"), new, True, False)
+        mm(A(p, 0, 256), A(sign), A("nsm%d" % (t % 2)), False, True)
+        tt(w, w, A(p, 0, 256), op)
+
+    def merge(t):
+        tt(A("r2"), ind(A("rb", DUM, WID), nl2), A("rr%d" % t, 0, 256), O.min)
+        ts(A("sx"), ind(A("sb"), sl), c(ODD), O.mult)
+        scat(A("rb", 0, GH), sc, A("r2"))
+        tt(A("sb", t, V, 4), A("sx"), A("sev"), O.add)
+        cp(A("so"), A("sb", t, V, 4))
+        selfmark("rb", t, A("r2"), "p1", "idm", O.min)
+
+    def succ_gather(chunks):
+        for a, b in chunks: act(A("sg", a, b), ind(A("rb", DUM, RAW), A("so", a // 16, b // 16)))
+
+    def succ_min(t):
+        for a, b in SUCC: scan(A("sc", a, b), A("smx", 0, b - a), A("sg", a, b), 255.0, O.max, O.min)
+        tt(A("rn%d" % t), A("sc", 15, 4096, 16), A("r2"), O.min)
+
+    def pmerge(t): tt(A("pn%d" % t), ind(A("pb", DUM, WID), nl2), A("pr%d" % t, 0, 256), O.max)
+
+    def xmerge(t):
+        tt(A("xs"), ind(A("xb", DUM, WID), nl2), A("xa%d" % t), O.add)
+        ts(A("xh"), A("xs"), 1, O.arith_shift_right)
+        cp(A("xb", RAW + t, RAW + V, 4), A("xh"))
+
+    def c_flags():
+        for k in range(16): mm(A("p5", 0, 256), A("wm", 128 * k, 128 * k + 128), A("tp", 256 * k, 256 * k + 256), k == 0, False)
+        for k in range(16): mm(A("p5", 0, 256), A("wm", 128 * k, 128 * k + 128), A("tr", 256 * k, 256 * k + 256), False, k == 15)
+        act(A("os"), A("p5", 0, 256), AF.Sign)
+
+    def c_update(t):
+        tt(A("cd"), ind(A("cb"), A("bcu")), A("ci", t, V, 4), O.subtract)
+        tt(A("od"), A("os"), A("cd"), O.mult)
+        tt(A("cb", t, V, 4), A("cb", t, V, 4), A("od"), O.add)
+
+    def marks(u):
+        ns = A("nsm%d" % (u % 2))
+        mm(A("p2", 0, 256), A("idf"), A("fl", DUM + u, DUM + V, 4), True, False)
+        mm(A("p2", 0, 256), A("idf"), A("nv", DUM + u, DUM + V, 4), False, True)
+        act(ns, A("p2", 0, 256), AF.Abs, scale=PEN)
+        act(A("p3", 0, 256), ns, AF.Relu, bias=PEN, scale=-1.0)
+
+    def windows(t):
+        xr, u = A("xb", RAW + t, RAW + V, 4), t + 1
+        scat(A("xb", 0, GH), sc, xr)
+        selfmark("xb", t, xr, "p0", "idm", O.min)
+        f_changes(t)
+        tt(A("xb", DUM + u, GH, 4), A("xb", DUM + u, GH, 4), A("p3", 0, 256), O.max)
+
+    def f_list(t):
+        for m in range(16): mm(A("p6", 0, 32), A("em", 128 * m, 128 * m + 128), A("fl", DUM + m, DUM + G5, 16), m == 0, m == 15)
+
+    def f_changes(t):
+        cp(A("fli"), A("p6", 0, 32))
+        tt(A("dp"), A("pn%d" % t, 0, 128), A("pr%d" % t, 0, 128), O.not_equal)
+        ts(A("flt"), A("p6", 0, 32), float(G5), O.is_lt)
+        ts(A("fli"), A("fli"), 3, O.bitwise_and)
+        tt(A("dfl"), A("p6", 0, 32), A("fvs"), O.subtract)
+        ts(A("chf"), A("fli"), float(t), O.is_equal, c(NRS + t), O.mult)
+        tt(A("dfl"), A("dfl"), A("flt"), O.mult)
+        mm(A("p7", 128, 160), A("idm"), A("chf"), True, False)
+        changed("dp", t, False)
+
+    def changed(n, t, last):
+        for a in range(4):
+            m = 4 * a + t
+            mm(A("p7", 128, 160), A("wm", 128 * m, 128 * m + 128), A(n, a, 128, 4), False, last and a == 3)
+
+    def publish(t):
+        tt(A("dr"), A("rn%d" % t, 0, 128), A("rr%d" % t, 0, 128), O.not_equal)
+        changed("dr", t, True)
+        ts(A("ch"), A("p7", 128, 160), 0.0, O.is_gt)
+        scan(A("scq"), A("one"), A("ch"), 0.0, O.mult, O.add)
+        ts(A("c96"), A("ch"), float(CAP + 1), O.mult, -1.0, O.add)
+        mm(A("p7", 192, 224), A("ltm"), A("ch"), True, False)
+        mm(A("p7", 192, 224), A("bom"), A("scq"), False, True)
+        tt(A("go"), A("p7", 192, 224), A("c96"), O.is_le)
+        ts(A("ge"), A("go"), c(PM + t), O.mult)
+        tt(A("gf"), A("go"), A("dfl"), O.mult)
+        tt(A("e5"), A("e5"), A("ge"), O.max)
+        tt(A("fvs"), A("fvs"), A("gf"), O.add)
+        tt(A("zf"), A("e5"), A("fvs"), O.add)
+        cp(A("z%d" % t), A("zf"))
+        send([(A("z%d" % t), A("lz%d" % t, 0, 32), A("lz%d" % t, 32, 64))], ["az%%s%d" % t], 2)
+
+    def pwin(t):
+        scat(A("pb", 0, GH), sc, A("pn%d" % t))
+        selfmark("pb", t, A("pn%d" % t), "p2", "ngm", O.max)
+
+    def rwin(t):
+        scat(A("rb", 0, GH), sc, A("rn%d" % t))
+        selfmark("rb", t, A("rn%d" % t), "p1", "idm", O.min)
+        ts(A("sev"), A("si", t + 1, V, 4), c(EVR), O.mult)
+        act(A("rb", RAW + t, RAW + V, 4), A("rn%d" % t))
+
+    def count(t):
+        tt(A("wn"), A("p7", 0, 16), A("ask"), O.mult)
+        mm(A("p7", 256, 272), A("onm"), A("wn"), True, True)
+        reduce(A("mt", 0, 1), A("p7", 256, 272), O.add)
+        cp(A("mi", 0, 1), A("mt", 0, 1))
+        ts(A("mi", 1, 2), A("mi", 0, 1), 31, O.bitwise_and)
+        ts(c(LIM), A("mi", 1, 2), 16.0, O.mult, c(TH16), O.add)
+
+    def block(kind, t):
+        n = "%sn%d" % (kind, t)
+        send([(A(n, 0, 128), A("l%sa%d" % (kind, t)), A("l%sb%d" % (kind, t)))], ["a%s%%s%d" % (kind, t)], 2)
+        for s, S in (("a", "A"), ("b", "B")): arrive("a%s%s%d" % (kind, S, t), 2, [A("l%s%s%d" % (kind, s, t))])
+
+    def ghosts(t):
+        arrive("azA%d" % t, 2, [A("lz%d" % t, 0, 32)]); arrive("azB%d" % t, 2, [A("lz%d" % t, 32, 64)])
+        for s in "ab":
+            cp(A("rw" + s, G5 + t, 2 * G5, 4), A("lr%s%d" % (s, t)))
+            act(A("pw" + s, G5 + t, 2 * G5, 4), A("lp%s%d" % (s, t)))
+        cp(A("zi"), A("lz%d" % t))
+        ts(A("ei"), A("zi"), 512, O.bitwise_and)
+        ts(A("fi"), A("zi"), 511, O.bitwise_and)
+        tt(A("ei"), A("ei"), A("jl"), O.add)
+        cp(A("fu"), A("fi"))
+        cp(A("eu"), A("ei"))
+        for i, s in enumerate("ab"):
+            act(A("pv" + s), ind(A("pw" + s), A("eu", 32 * i, 32 * i + 32)))
+            cp(A("rv" + s), ind(A("rw" + s), A("eu", 32 * i, 32 * i + 32)))
+        for i, (s, w) in enumerate((("a", gA), ("b", gB))):
+            act(A("pb", *w), ind(A("pv" + s), A("fu", 32 * i, 32 * i + 32)))
+            cp(A("rb", *w), ind(A("rv" + s), A("fu", 32 * i, 32 * i + 32)))
+
+    turn_a(0)
+    tables()
+    turn_v(0)
+    turn_s(0)
+    fill(A("xb", DUM, GH, 4), PEN)
+    list_b(0)
+    turn_a(1)
+    copies(0, cp)
+    turn_v(1)
+    iota(A("ik"), [[1, 8], [0, 16]])
+    ts(A("b8"), A("ik"), c(PF), O.is_equal)
+    cp(A("thf", 0, 1, p1=8), A("thi", 0, 1, p1=8))
+    mm(A("p7", 0, 1), A("b8", p1=8), A("thf", 0, 1, p1=8), True, True)
+    ts(c(TH16), A("p7", 0, 1), 16.0, O.mult)
+    cp(c(LIM), c(TH16))
+    for i in range(4): x_gather(0, i)
+    distances(0)
+    iota(A("ib"), [[0, 16], [1, 16]])
+    iotf(A("ic"), [[1, 256]])
+    iota(A("ih", 0, 16), [[1, 2], [2, 8]]); iota(A("ih", 16, 48), [[1, 32]])
+    iota(A("ij", 0, 16), [[0, 16]], 0, 1); iota(A("ij", 16, 32), [[16, 16]], 0, 1)
+    iotf(A("vi"), [[1, DUM + V]], -DUM); iotf(A("fl"), [[1, DUM + V]], -DUM); iotf(A("nv"), [[-1, DUM + V]], DUM)
+    iota(A("in_", 0, 96), [[-8, 2], [0, 3], [1, 16]])
+    iota(A("id_", 32, 96), [[0, 2], [16, 32]], 0, 1)
+    iotf(A("em"), [[0, 2048]])
+    ts(A("dg", 0, 256), A("ib"), c(ROW), O.is_equal); ts(A("dg", 256, 512), A("ib"), c(ROW), O.is_equal)
+    cp(A("oke"), A("ih", 16, 48)); cp(A("omx"), A("ih", 0, 16))
+    ts(A("oq"), A("ij", 0, 16), c(NG), O.add)
+    for a in range(16):
+        o = 128 * (a % 2) + 16 * (a // 2)
+        if a == 0: ts(A("thr"), A("dg", 0, 256), 1e9 + 0.5, O.mult, -1e9, O.add)
+        if PAIRS[a] == "V": ts(A("thr", o, o + 16), A("dg", 0, 16), 1e9 + B10, O.mult, -1e9, O.add)
+    ts(A("rq"), A("in_", 0, 96), c(P16), O.is_equal)
+    ts(A("lw"), A("ij", 16, 32), c(NG), O.add)
+    for t in range(RO):
+        o = 48 * t
+        ts(A("v3", o, o + 16), A("lw"), 4.0, O.mult, float(2048 + t), O.add)
+        cp(A("v3", o + 16, o + 32), A("lw"))
+        ts(A("v3", o + 32, o + 48), A("lw"), 4.0, O.mult, float(t), O.add)
+    cp(A("sb"), A("si"))
+    ts(A("sev"), A("si", 0, V, 4), c(EVR), O.mult)
+    for n in ("r", "p"):
+        for s, w in (("a", gA), ("b", gB)):
+            for o in (0, G5):
+                dma("D", A(n + "w" + s, o, o + G5)["ap"], A(n + "b", *w)["ap"], [A(n + "b", *w)], [A(n + "w" + s, o, o + G5)])
+
+    def border():
+        for m in range(16): act(A("em", 128 * m + m, 128 * m + 128, 16), A("idm", m, 128, 16))
+        ts(A("bom"), A("ik"), c(P16), O.is_equal)
+        ts(A("lh"), A("ie"), c(PF), O.is_lt, -1.0, O.mult)
+        tt(A("ltm"), A("lh"), A("bom"), O.mult)
+        ts(A("jl"), A("id_", 32, 96), c(NG), O.add)
+        cp(A("fvs"), A("jl", 0, 32)); fill(A("e5"), 0.0)
+        fill(A("one"), 1.0); fill(A("onm"), 1.0)
+        ts(A("pc", 7, 8), rw, 3, O.bitwise_and)
+        cp(c(W3), A("pc", 7, 8))
+        for t in range(RO - 1):
+            ts(c(NRS + t), c(W3), float(t), O.not_equal)
+            ts(c(PM + t), c(W3), float(t), O.is_le, 512.0, O.mult)
+
+    for t in range(RO):
+        last = t == RO - 1
+        tests(t)
+        if t == 0: row_tables()
+        c_flags()
+        if not last:
+            turn_s(t + 1)
+            copies(t + 1, act)
+        if t == 0: border()
+        partner(t)
+        merge(t)
+        if last:
+            succ_gather(SUCC[:3])
+            for a, b in SUCC[3:]: cp(A("sg", a, b), ind(A("rb", DUM, RAW), A("so", a // 16, b // 16)))
+        else:
+            scat(A("fl", 0, DUM + V), sc, A("vi", DUM + t, DUM + V, 4))
+            if t + 2 < RO: turn_a(t + 2)
+            succ_gather(SUCC[:2])
+            marks(t + 1)
+            succ_gather(SUCC[2:])
+            pmerge(t)
+            block("p", t)
+            f_list(t)
+        xmerge(t)
+        if last:
+            dma("D", T.yx[:], RWb("xb")["ap"], [RWb("xb")], [])
+            c_update(t)
+            dma("D", T.yc[:], A("cb")["ap"], [A("cb")], [])
+            succ_min(t)
+            cp(A("rb", RAW + t, RAW + V, 4), A("rn%d" % t))
+            dma("D", T.yr[:], RWb("rb")["ap"], [RWb("rb")], [])
+            continue
+        windows(t)
+        for i in range(4): x_gather(t + 1, i)
+        succ_min(t)
+        block("r", t)
+        publish(t)
+        pwin(t)
+        rwin(t)
+        distances(t + 1)
+        if t == 0: cp(A("cb"), A("ci"))
+        c_update(t)
+        if t + 2 < RO: turn_v(t + 2)
+        ghosts(t)
+        count(t)
+    for i in range(free["ls"]):
+        for (s, v) in [k for k in snap if k[0] == "ls%d" % i]: wait("G", s, v)
+    for s in sorted(cnt): wait("G", s, cnt[s])
+    for i in range(free["d"]): wait("D", "d%d" % i, 16)

@@ -2,15 +2,18 @@ from concourse.bass import DstId, RemoteDMATransfer
 from concourse.mybir import AluOpType, AxisListType, ActivationFunctionType as AF
 
 V, G5, RO, CAP = 1024, 512, 4, 96
-DUM, GH, RAW, WID = 256, 1280, 2304, 3328
+DUM = 256
 PEN = 16384.0
 B10 = 10.0 * 2 ** 20
-TESTS = (("P", 0, 2, "V"), ("P", 2, 2, "V"), ("P", 4, 2, "V"), ("P", 6, 2, "V"), ("R", 0, 2, "V"), ("R", 2, 1, "V"), ("R", 3, 1, "S"), ("R", 4, 2, "S"), ("R", 6, 2, "S"))
-TESTS0 = tuple((k, i, n, "S" if (k, i) == ("R", 6) else "V") for k, i, n, _ in TESTS)
-SUCC = ((0, 1024), (1024, 2048), (2048, 3072), (3072, 4096))
+MAGIC = 1.5 * 2 ** 23
+TESTS = {"P": "VVVVVVVV", "R": "VVVSVVSS"}
+TESTS0 = {"P": "VVVVVVVV", "R": "VVVVVVVS"}
+AGAIN = {"x": "S", "p": "S", "r": "S"}
+GHOST = {"pa": "S", "pb": "V", "ra": "S", "rb": "V"}
 PAIRS = "SVSVSVSVSVSVSVSV"
+CYC, GA, SC, HOP, SELF, LOOK, SWEEPS = 0.9e-3, 1.56, 3.8, 0.1, 0.05, 1.0, 4
 
-SCRATCH, PLACE = {}, {}
+SCRATCH, PLACE, ORDER = {}, {}, {}
 SIZE = {"bfloat16": 2, "uint16": 2, "float32": 4, "int32": 4}
 
 
@@ -27,41 +30,78 @@ def _b(names, cols, dtype, where="sbuf"):
             PLACE[name] = (name, 0, cols)
 
 
-_b("xb rb pb", WID, "bfloat16")
-_b("fl vi nv", DUM + V, "float32"); _b("idf", 128, "float32")
-_b("ci si", V, "int32")
-_b("cb sb", V, "float32")
+_b("rb bw", DUM + 2 * V, "bfloat16")
+_b("pb xw rq pq xq", 2 * V, "bfloat16")
+_b("bs", V, "bfloat16")
+_b("ci si", V, "int32"); _b("cb sb", V, "float32")
 for _t in range(RO):
-    _b("rr%d pr%d" % (_t, _t), 1024, "bfloat16")
-    _b("ct%d" % _t, 256, "uint16"); _b("ca%d" % _t, 256, "float32")
-    _b("xa%d rn%d pn%d" % (_t, _t, _t), 256, "bfloat16"); _b("z%d" % _t, 32, "uint16")
-    _b("lra%d lrb%d lpa%d lpb%d" % (_t, _t, _t, _t), 128, "bfloat16")
-    _b("lz%d" % _t, 64, "uint16")
-_b("xg ad tp tr sg sc gp", 4096, "bfloat16")
-_b("rwa rwb pwa pwb", 1024, "bfloat16")
-_b("rva rvb pva pvb", 512, "bfloat16")
-_b("wm", 2048, "bfloat16"); _b("em", 2048, "float32")
-_b("idm ngm bom ltm sb2m onm", 128, "bfloat16"); _b("b8", 128, "float32")
-_b("sc10 sc13 sw " + " ".join("se%d" % r for r in range(10, 16)), 1, "float32"); _b("ic", 256, "float32")
-_b("ia ib", 256, "int32"); _b("id_ ie ig ih ij ik in_", 128, "int32"); _b("iq", 1024, "int32")
-_b("pc", 8, "int32"); _b("cc", 48, "float32"); _b("g8", 8, "bfloat16"); _b("lh", 128, "bfloat16"); _b("lw", 16, "float32")
-_b("dg", 512, "bfloat16"); _b("thr sg1", 256, "float32"); _b("smx", 1024, "bfloat16")
-_b("kc cll clr", 256, "bfloat16"); _b("rq", 96, "bfloat16"); _b("one", 32, "float32")
-_b("o2 ofin oq omx", 16, "uint16"); _b("oke", 32, "uint16")
+    _b("ct%d" % _t, 256, "uint16"); _b("ca%d" % _t, 256, "float32"); _b("lb%d" % _t, 128, "uint16")
+    _b("rn%d pn%d" % (_t, _t), 256, "bfloat16"); _b("z%d" % _t, 32, "uint16"); _b("lz%d" % _t, 64, "uint16")
+_b("xg ad tp tr gp", 4096, "bfloat16"); _b("sga sgb sc", 2048, "bfloat16")
+_b("rwa rwb pwa pwb", 896, "bfloat16")
+_b("wm wm2 wt", 2048, "bfloat16"); _b("smx", 1024, "bfloat16")
+_b("idm ngm hm bgm nbm zm bom ltm s10 onm lh", 128, "bfloat16"); _b("idf b8 la0 la1 lb_0 lb_1", 128, "float32")
+_b("ic thr sg1", 256, "float32"); _b("ib", 256, "int32"); _b("id_ ie ig ih ij ik in_", 128, "int32")
+_b("pc", 8, "int32"); _b("cc", 40, "float32"); _b("g8", 8, "bfloat16"); _b("lw wv wx", 16, "float32")
+_b("pat", 224, "bfloat16"); _b("tc", 32, "bfloat16"); _b("ta", 32, "float32"); _b("pa pb_ pc_ dig dt dgt", 512, "bfloat16")
+_b("dg", 512, "bfloat16"); _b("kc cll clr mh", 256, "bfloat16"); _b("rs", 96, "bfloat16"); _b("one", 32, "float32")
+_b("o2 ofin omx kqu cu bcu", 16, "uint16"); _b("oke", 32, "uint16")
 _b("in12 tr12", 512, "float32")
-_b("key", 256, "int32"); _b("k8", 128, "int32"); _b("k4", 64, "int32"); _b("k2", 32, "int32"); _b("mk", 16, "int32")
-_b("eq prd", 256, "float32"); _b("s8", 128, "float32"); _b("s4", 64, "float32"); _b("s2", 32, "float32")
-_b("s1 has ask nli bc pen", 16, "float32"); _b("nl bcu", 16, "uint16"); _b("fsh fbt", 256, "int32")
-_b("bits fev fod fr junk we os", 256, "bfloat16"); _b("bm bs cd od sx sev", 256, "float32"); _b("kl", 32, "int32"); _b("ke", 512, "bfloat16")
-_b("mx", 16, "float32"); _b("nb3 d3 t3", 48, "float32"); _b("l3", 48, "uint16"); _b("v3", 192, "float32"); _b("so", 256, "uint16")
-_b("xs xh", 256, "int32"); _b("r2 nsm0 nsm1", 256, "bfloat16")
+_b("klo k8", 128, "float32"); _b("k4", 64, "float32"); _b("k2", 32, "float32"); _b("k1 has ask bc pen", 16, "float32"); _b("mk kq", 16, "int32")
+_b("cm cs sx cx cy", 256, "float32"); _b("bits fev fod fr junk we os xp r2", 256, "bfloat16"); _b("kl", 32, "int32"); _b("ke", 512, "bfloat16")
+_b("mx", 16, "float32"); _b("d3 t3", 48, "float32"); _b("l3", 48, "uint16"); _b("v3 vm", 192, "float32"); _b("la", 128, "uint16")
 _b("wn", 16, "bfloat16"); _b("mt", 2, "float32"); _b("mi", 2, "int32"); _b("thi", 8, "int32"); _b("thf", 8, "float32")
 _b("dr dp", 128, "bfloat16")
-_b("fvs e5 flt dfl c96 go ge gf zf", 32, "float32"); _b("fli", 32, "int32"); _b("chf ch scq", 32, "bfloat16")
-_b("zi fi ei jl", 64, "int32"); _b("fu eu", 64, "uint16")
+_b("fvs flo flt dfl c96 gf", 32, "float32"); _b("e5 ge go chf ch scq", 32, "bfloat16"); _b("fu", 32, "uint16"); _b("flu", 64, "uint16")
 _b("p0 p1 p2 p3 p4 p5 p6 p7", 512, "float32", "psum")
-SEMAPHORES = ["qV", "qS", "qP", "qG", "inA", "inB"] + ["d%d" % i for i in range(24)] + ["ls%d" % i for i in range(12)] + \
+SEMAPHORES = ["qV", "qS", "qP", "qG", "inA", "inB"] + ["d%d" % i for i in range(28)] + ["ls%d" % i for i in range(12)] + \
     ["%s%s%d" % (a, s, t) for a in ("ar", "ap", "az") for s in "AB" for t in range(RO - 1)]
+
+
+def plan(nodes):
+    n = len(nodes)
+    after = [[] for _ in nodes]
+    for i, d in enumerate(nodes):
+        for j in d["deps"]: after[j].append(i)
+    hop = lambda j, i: 0.0 if not nodes[i]["deps"][j] else SELF if nodes[j]["q"] == nodes[i]["q"] else HOP
+    far = [0.0] * n
+    for i in range(n - 1, -1, -1):
+        run, most = {}, 0.0
+        for k in sorted(after[i], key=lambda k: nodes[k]["cost"] - far[k]):
+            q = nodes[k]["q"]
+            most = max(most, run.get(q, 0.0) + far[k] + hop(i, k))
+            run[q] = run.get(q, 0.0) + nodes[k]["cost"]
+        far[i] = nodes[i]["cost"] + nodes[i]["lat"] + most
+    before = [list(d["deps"]) for d in nodes]
+
+    def sweep(far, back):
+        pre, post = (after, before) if back else (before, after)
+        left = [len(p) for p in pre]
+        end, est, free, ready, order = [0.0] * n, [0.0] * n, {}, {}, []
+        for i in range(n):
+            if back: est[i] = nodes[i]["lat"]
+            if not left[i]: ready.setdefault(nodes[i]["q"], []).append(i)
+        while len(order) < n:
+            t, q = min((max(free.get(q, 0.0), min(est[i] for i in r)), q) for q, r in ready.items() if r)
+            a = max((i for i in ready[q] if est[i] <= t), key=lambda i: (far[i], -i))
+            for b in ready[q]:
+                if t < est[b] < t + nodes[a]["cost"] and far[b] > far[a]:
+                    if max(est[b] + far[b], est[b] + nodes[b]["cost"] + far[a]) + LOOK * (est[b] - t) < max(t + nodes[a]["cost"] + far[b], t + far[a]):
+                        a, t = b, est[b]
+            ready[q].remove(a); order.append(a)
+            if q != "R": free[q] = t + nodes[a]["cost"]
+            end[a] = t + nodes[a]["cost"] + (0.0 if back else nodes[a]["lat"])
+            for k in post[a]:
+                est[k] = max(est[k], end[a] + (hop(k, a) + nodes[k]["lat"] if back else hop(a, k))); left[k] -= 1
+                if not left[k]: ready.setdefault(nodes[k]["q"], []).append(k)
+        return order, end
+
+    best = None
+    for _ in range(SWEEPS):
+        order, end = sweep(far, False)
+        if best is None or max(end) < best[0]: best = (max(end), order)
+        far = sweep(end, True)[1]
+    return best[1]
 
 
 def rank_program(g, core, T, topo):
@@ -69,138 +109,142 @@ def rank_program(g, core, T, topo):
     if rank is None:
         return
     O = AluOpType
-    queues = {"V": g.vector, "S": g.scalar, "P": g.tensor, "G": g, "D": g.sync}
-    cnt = {"qV": 0, "qS": 0, "qP": 0, "qG": 0}
-    know = {q: {} for q in queues}
-    snap, hist, free = {}, {}, {"d": 0, "ls": 0}
+    nodes, hist, free = [], {}, {"d": 0, "ls": 0}
 
     def A(name, a=None, b=None, s=1, p0=0, p1=128):
         buf, at, cols = PLACE[name]
         t = T[buf]
         a = 0 if a is None else a
         b = cols if b is None else b
-        return {"n": name, "a": a, "b": b, "s": s, "ap": t[p0:p1, at + a:at + b:s] if s != 1 else t[p0:p1, at + a:at + b]}
+        return {"n": name, "a": a, "b": b, "s": s, "k": len(range(a, b, s)), "w": SIZE[SCRATCH[buf][2]], "ps": SCRATCH[buf][0] == "psum",
+                "ap": t[p0:p1, at + a:at + b:s] if s != 1 else t[p0:p1, at + a:at + b]}
 
-    def wait(q, sem, val):
-        if know[q].get(sem, 0) < val:
-            queues[q].wait_ge(T.sem[sem], val)
-            for k, v in snap.get((sem, val), {}).items():
-                if know[q].get(k, 0) < v: know[q][k] = v
-            know[q][sem] = val
-
-    def deps(q, reads, writes):
-        need = {}
-        for acc, w in [(r, False) for r in reads] + [(r, True) for r in writes]:
-            ps = SCRATCH[PLACE[acc["n"]][0]][0] == "psum"
-            for e in hist.get(acc["n"], ()):
-                if e[3] == q and ps and q == "P": continue
-                if (w or e[2] or (ps and e[3] != q)) and (ps or (acc["a"] < e[1] and e[0] < acc["b"])):
-                    if need.get(e[4], 0) < e[5]: need[e[4]] = e[5]
-        for s in sorted(need): wait(q, s, need[s])
-
-    def note(q, sem, val, reads, writes):
-        snap[(sem, val)] = dict(know[q])
-        for acc, w in [(r, False) for r in reads] + [(r, True) for r in writes]:
-            h = hist.setdefault(acc["n"], [])
-            if w and acc["s"] == 1:
-                h[:] = [e for e in h if not (acc["a"] <= e[0] and e[1] <= acc["b"])]
+    def node(q, calls, cost, writes, reads, lat=0.0, sem=None, grp=None, extra=()):
+        me, deps = len(nodes), {j: False for j in extra}
+        acc = [(r, False) for r in reads] + [(r, True) for r in writes]
+        for x, w in acc:
+            h = hist.setdefault(x["n"], [])
+            if x["ps"]:
+                keep = []
+                for e in h:
+                    if e[3] == me: continue
+                    o = nodes[e[3]]
+                    if grp is not None and o["grp"] is grp and e[3] != grp["first"]: keep.append(e)
+                    elif o["q"] == q and not (w or e[2]): keep.append(e)
+                    else:
+                        deps[e[3]] = deps.get(e[3], False) or not (q == o["q"] == "P")
+                        if (grp is not None and o["grp"] is grp) or (e[2] and not w): keep.append(e)
+                h[:] = keep + [(0, 512, w or any(e[2] for e in h if e[3] == me), me)]
             else:
-                h[:] = [e for e in h if not (e[4] == sem and e[2] == w and e[0] == acc["a"] and e[1] == acc["b"])]
-            h.append((acc["a"], acc["b"], w, q, sem, val))
+                for e in h:
+                    if e[3] != me and (w or e[2]) and x["a"] < e[1] and e[0] < x["b"]: deps[e[3]] = True
+        for x, w in acc:
+            if not x["ps"]:
+                h = hist[x["n"]]
+                if w and x["s"] == 1: h[:] = [e for e in h if not (x["a"] <= e[0] and e[1] <= x["b"])]
+                h.append((x["a"], x["b"], w, me))
+        nodes.append({"q": q, "calls": calls, "cost": cost, "lat": lat, "deps": deps, "sem": sem, "grp": grp})
+        return me
 
-    def run(q, fn, writes, reads):
-        deps(q, reads, writes)
-        s = "q" + q
-        cnt[s] += 1
-        fn().then_inc(T.sem[s], 1)
-        note(q, s, cnt[s], reads, writes)
-
-    def dma(q, out, in_, reads, writes):
-        deps(q, reads, writes)
-        s = "d%d" % free["d"]; free["d"] += 1
-        queues[q].dma_start(out, in_).then_inc(T.sem[s], 16)
-        note(q, s, 16, reads, writes)
-
-    def ind(win, off): return {"ap": win["ap"].indirect(off["ap"]), "w": win, "o": off}
-    def rd(x): return [x["w"], x["o"]] if "w" in x else [x]
-    def cp(out, in_): run("V", lambda: g.vector.tensor_copy(out["ap"], in_["ap"]), [out], rd(in_))
-    def scat(win, off, in_): run("V", lambda: g.vector.tensor_copy(win["ap"].indirect(off["ap"]), in_["ap"]), [win], [off, in_])
-    def tt(out, a, b, op): run("V", lambda: g.vector.tensor_tensor(out["ap"], a["ap"], b["ap"], op), [out], rd(a) + [b])
+    def price(q, out, in_, rate):
+        if "o" in in_: return 0.06 + 16 * in_["o"]["k"] * GA * CYC
+        return max(64, in_["k"] * rate) * CYC
+    def half(*x): return 0.5 if all(i["w"] == 2 for i in x) else 1.0
+    def ind(win, off): return {"ap": win["ap"].indirect(off["ap"]), "win": win, "o": off, "w": win["w"], "ps": False}
+    def rd(x): return [x["win"], x["o"]] if "o" in x else [x]
+    def ap(x): return x["ap"] if isinstance(x, dict) else x
+    def cols(*x): return [i for i in x if isinstance(i, dict)]
+    def cp(out, in_): node("V", [lambda: g.vector.tensor_copy(out["ap"], in_["ap"])], price("V", out, in_, half(out, in_)), [out], rd(in_))
+    def scat(win, off, in_): node("V", [lambda: g.vector.tensor_copy(win["ap"].indirect(off["ap"]), in_["ap"])], 0.05 + in_["k"] * SC * CYC, [win], [off, in_])
+    def tt(out, a, b, op):
+        rate = 1.0 if a["ps"] or b["ps"] else 2.0 * half(out, a, b)
+        node("V", [lambda: g.vector.tensor_tensor(out["ap"], a["ap"], b["ap"], op)], price("V", out, a, rate), [out], rd(a) + [b])
     def ts(out, a, s1, op0, s2=None, op1=None):
-        r = rd(a) + [s for s in (s1, s2) if isinstance(s, dict)]
-        v1 = s1["ap"] if isinstance(s1, dict) else s1
-        v2 = s2["ap"] if isinstance(s2, dict) else s2
-        if op1 is None: run("V", lambda: g.vector.tensor_scalar(out["ap"], a["ap"], v1, None, op0), [out], r)
-        else: run("V", lambda: g.vector.tensor_scalar(out["ap"], a["ap"], v1, v2, op0, op1), [out], r)
-    def scan(out, d0, d1, init, op0, op1): run("V", lambda: g.vector.tensor_tensor_scan(out["ap"], d0["ap"], d1["ap"], init, op0, op1), [out], [d0, d1])
-    def fill(out, v): run("V", lambda: g.vector.memset(out["ap"], v), [out], [])
-    def reduce(out, in_, op): run("V", lambda: g.vector.tensor_reduce(out["ap"], in_["ap"], AxisListType.X, op), [out], [in_])
+        f = (lambda: g.vector.tensor_scalar(out["ap"], a["ap"], ap(s1), None, op0)) if op1 is None else \
+            (lambda: g.vector.tensor_scalar(out["ap"], a["ap"], ap(s1), ap(s2), op0, op1))
+        node("V", [f], price("V", out, a, half(out, a)), [out], rd(a) + cols(s1, s2))
+    def scan(out, d0, d1, init, op0, op1):
+        node("V", [lambda: g.vector.tensor_tensor_scan(out["ap"], d0["ap"], d1["ap"], init, op0, op1)], price("V", out, d1, half(out, d0, d1)), [out], [d0, d1])
+    def fill(out, v): node("V", [lambda: g.vector.memset(out["ap"], v)], price("V", out, out, half(out)), [out], [])
+    def reduce(out, in_, op): node("V", [lambda: g.vector.tensor_reduce(out["ap"], in_["ap"], AxisListType.X, op)], price("V", out, in_, 1.0), [out], [in_])
+    def turn32(out, in_): node("V", [lambda: g.vector.transpose(out["ap"], in_["ap"])], price("V", out, in_, 1.0), [out], [in_])
     def act(out, in_, func=AF.Copy, bias=0.0, scale=1.0, acc=None):
-        r = rd(in_) + [k for k in (bias, scale) if isinstance(k, dict)]
-        sc = scale["ap"] if isinstance(scale, dict) else scale
-        bi = bias["ap"] if isinstance(bias, dict) else bias
-        if acc is None: run("S", lambda: g.scalar.activation(out["ap"], in_["ap"], func, bias=bi, scale=sc), [out], r)
-        else: run("S", lambda: g.scalar.activation(out["ap"], in_["ap"], func, bias=bias, scale=sc, accum_out=acc["ap"]), [out, acc], r)
-    def mm(out, l, r, start, stop): run("P", lambda: g.tensor.matmul(out["ap"], l["ap"], r["ap"], start, stop), [out], [l, r])
-    def iota(out, pat, base=0, cm=0): run("G", lambda: g.iota(out["ap"], pat, base, cm), [out], [])
-    def iotf(out, pat, base=0, cm=0): run("G", lambda: g.iota(out["ap"], pat, base, cm, allow_small_or_imprecise_dtypes=True), [out], [])
+        r = rd(in_) + cols(bias, scale)
+        if acc is None: node("S", [lambda: g.scalar.activation(out["ap"], in_["ap"], func, bias=ap(bias), scale=ap(scale))], price("S", out, in_, 1.0), [out], r)
+        else: node("S", [lambda: g.scalar.activation(out["ap"], in_["ap"], func, bias=bias, scale=ap(scale), accum_out=acc["ap"])], price("S", out, in_, 1.0) + 0.02, [out, acc], r)
+    def copy(who, out, in_): (cp if who == "V" else act)(out, in_)
+    def mms(parts, grp=None):
+        first = grp is None or "first" not in grp
+        if grp is not None:
+            if first: grp["first"] = len(nodes); grp["n"] = 0
+            grp["n"] += 1
+        calls = [(o["ap"], l["ap"], r["ap"], first and i == 0) for i, (o, l, r) in enumerate(parts)]
+        cost = sum(max(64, r["k"]) * (4 if r["w"] == 4 else 1) * CYC / 2 for o, l, r in parts)
+        node("P", calls, cost, [parts[0][0]], [x for o, l, r in parts for x in (l, r)], grp=grp)
+    def iota(out, pat, base=0, cm=0):
+        if out["w"] == 4 and PLACE[out["n"]][0].endswith("int32"): f = lambda: g.iota(out["ap"], pat, base, cm)
+        else: f = lambda: g.iota(out["ap"], pat, base, cm, allow_small_or_imprecise_dtypes=True)
+        node("G", [f], 0.13 + 2 * out["k"] * CYC, [out], [])
+    def dma(out, in_, reads, writes, kb, q="D"):
+        s = "d%d" % free["d"]; free["d"] += 1
+        f = g.sync if q == "D" else g.scalar
+        node("D", [lambda: f.dma_start(out, in_)], kb / 200.0, writes, reads, lat=2.0, sem=(s, 16))
 
-    nxt, prv = T.cores[(rank + 1) % 8], T.cores[(rank - 1) % 8]
-    far = [d for d in (nxt, prv) if topo.chip(d) != topo.chip(core)]
-    eng = {}
-    for d in (nxt, prv):
-        e = topo.engines(core, d)
-        if d not in far: e = [i for i in e if not far or i not in topo.engines(core, far[0])] or e
-        elif len(far) == 2: e = e[:len(e) // 2] if d == far[0] else e[len(e) // 2:]
-        eng[d] = e
+    def sides(c):
+        r = T.rank_of(c)
+        two = (T.cores[(r - 1) % 8], T.cores[(r + 1) % 8])
+        far = [d for d in two if topo.chip(d) != topo.chip(c)]
+        out = []
+        for d in two:
+            e = topo.engines(c, d)
+            if d not in far: e = [i for i in e if not far or i not in topo.engines(c, far[0])] or e
+            elif len(far) == 2: e = e[:len(e) // 2] if d == far[0] else e[len(e) // 2:]
+            out.append((d, e))
+        return out
+    NE = min(len(e) for c_ in T.cores for _, e in sides(c_))
 
-    def send(pairs, sems, n):
+    def send(pairs, sem, us):
         s = "ls%d" % free["ls"]; free["ls"] += 1
-        deps("G", [p[0] for p in pairs], [])
-        tr = []
-        for side, d in (("A", prv), ("B", nxt)):
+        n, tr = NE // len(pairs), []
+        for side, (d, e) in zip("AB", sides(core)):
             rid, pid, _ = topo.addr(d)
             for i, p in enumerate(pairs):
-                tr.append(RemoteDMATransfer(dst_ids=[DstId(rid=rid, pnc=pid)], dma_engine_mask=sum(1 << e for e in eng[d][i * n:i * n + n]),
-                                            remote_sem=T.sem[sems[i] % side], src=p[0]["ap"], dst=p[1 if side == "A" else 2]["ap"]))
-        g.remote_dma_fused(tr, local_sem=T.sem[s])
-        note("G", s, n * len(tr), [p[0] for p in pairs], [])
+                tr.append(RemoteDMATransfer(dst_ids=[DstId(rid=rid, pnc=pid)], dma_engine_mask=sum(1 << k for k in e[i * n:i * n + n]),
+                                            remote_sem=T.sem[sem % side], src=p[0]["ap"], dst=p[1 if side == "A" else 2]["ap"]))
+        me = node("G", [lambda: g.remote_dma_fused(tr, local_sem=T.sem[s])], 1.0, [], [p[0] for p in pairs], lat=1.0, sem=(s, n * len(tr)))
+        for i, side in enumerate("AB"): node("R", [], 0.0, [p[1 + i] for p in pairs], [], lat=us, sem=(sem % side, n * len(pairs)), extra=[me])
 
-    def arrive(sem, val, writes):
-        snap[(sem, val)] = {}
-        for w in writes: hist.setdefault(w["n"], []).append((w["a"], w["b"], True, "R", sem, val))
+    def load(name, a, src, c0=0, c1=V, kb=256): dma(A(name, a + c0, a + c1)["ap"], src[:, c0:c1], [], [A(name, a + c0, a + c1)], kb * (c1 - c0) / V)
+    load("rb", DUM, T.reach, 0, G5); load("pb", 0, T.past, 0, G5)
+    load("ci", 0, T.cand, kb=512); load("xw", 0, T.x); load("xq", V, T.x)
+    load("rb", DUM, T.reach, G5, V); load("pb", 0, T.past, G5, V)
+    for o in (0, V): load("rq", o, T.reach)
+    for o in (0, V): load("pq", o, T.past)
+    load("si", 0, T.succ, kb=512); load("xq", 0, T.x)
+    dma(A("thi", 0, 1, p1=8)["ap"], T.th[:], [], [A("thi")], 1)
+    gh = {"ra": A("rb", DUM + V, DUM + V + G5), "rb": A("rb", DUM + V + G5, DUM + 2 * V), "pa": A("pb", V, V + G5), "pb": A("pb", V + G5, 2 * V)}
+    send([(A("rb", DUM, DUM + G5), gh["ra"], gh["rb"]), (A("pb", 0, G5), gh["pa"], gh["pb"])], "in%s", 5.0)
+    for n in ("pa", "pb", "ra", "rb"):
+        w = A(n[0] + "w" + n[1], 0, G5)
+        dma(w["ap"], gh[n]["ap"], [gh[n]], [w], 128)
 
-    RWb = lambda n: A(n, RAW, RAW + V)
-    own = lambda n: A(n, DUM, GH)
-    gA, gB = (GH, GH + G5), (GH + G5, GH + 2 * G5)
-    dma("D", RWb("rb")["ap"], T.reach[:], [], [RWb("rb")])
-    dma("S", RWb("pb")["ap"], T.past[:], [], [RWb("pb")])
-    dma("D", A("ci")["ap"], T.cand[:], [], [A("ci")])
-    dma("S", own("xb")["ap"], T.x[:], [], [own("xb")])
-    dma("D", RWb("xb")["ap"], T.x[:], [], [RWb("xb")])
-    dma("D", own("rb")["ap"], T.reach[:], [], [own("rb")])
-    dma("D", own("pb")["ap"], T.past[:], [], [own("pb")])
-    dma("D", A("si")["ap"], T.succ[:], [], [A("si")])
-    dma("D", A("thi", 0, 1, p1=8)["ap"], T.th[:], [], [A("thi")])
     c = lambda i: A("cc", i, i + 1)
-    ROW, P16, PF, ODD, SCL, RS, RG0, RG1, C1L, C1R, M12, M15, TH16, NG, LIM, EVR, W0, W1, W2, W3, W4 = range(21)
-    NRS, PM = 24, 28
+    ROW, P16, PF, ODD, RS, RG0, RG1, C1L, C1R, E12, E15, L10, M2, TH, NG, LIM, EVR, W0, W1, W2, W3, W4, W5, CA = range(24)
+    PM, EQ = 28, 32
     rw, pp = A("pc", 1, 2), A("pc", 0, 1)
     iota(pp, [[0, 1]], 0, 1)
-    iota(A("id_", 0, 16), [[32, 8], [-16, 2]], 16, 1)
-    iota(A("id_", 16, 32), [[1, 16]])
-    iota(A("ie"), [[1, 128]])
-    iota(A("ig", 0, 8), [[1, 8]])
-    iota(A("ia"), [[1, 16], [0, 16]])
-    iotf(A("xb", GH, RAW), [[0, RAW - GH]], int(PEN))
-    send([(A("rb", RAW, RAW + G5), A("rb", *gA), A("rb", *gB)), (A("pb", RAW, RAW + G5), A("pb", *gA), A("pb", *gB))], ["in%s", "in%s"], 4)
-    for n in ("rb", "pb"):
-        arrive("inA", 8, [A(n, *gA)]); arrive("inB", 8, [A(n, *gB)])
+    iota(A("id_", 0, 16), [[32, 8], [-16, 2]], 16, 1); iota(A("id_", 16, 32), [[1, 16]])
+    iota(A("ie"), [[1, 128]]); iota(A("ig", 0, 8), [[1, 8]]); iota(A("ik"), [[1, 8], [0, 16]])
+    iota(A("ib"), [[0, 16], [1, 16]]); iota(A("ic"), [[1, 256]])
+    iota(A("ih", 0, 16), [[1, 2], [2, 8]]); iota(A("ih", 16, 48), [[1, 32]])
+    iota(A("ij", 16, 32), [[16, 16]], 0, 1); iota(A("in_", 0, 96), [[-8, 2], [0, 3], [1, 16]]); iota(A("id_", 32, 64), [[16, 32]], 0, 1)
+    fill(A("xw", V, 2 * V), PEN); fill(A("rb", 0, DUM), 0.0); fill(A("bw", 0, DUM), 0.0); fill(A("bw", DUM + V, DUM + 2 * V), 0.0)
     ts(rw, pp, 15, O.bitwise_and)
     ts(A("pc", 2, 3), pp, 4, O.arith_shift_right)
     ts(A("pc", 3, 4), pp, 4, O.arith_shift_right, 1, O.bitwise_and)
     ts(A("pc", 4, 5), rw, 1, O.arith_shift_right)
     ts(A("pc", 5, 6), rw, 1, O.bitwise_and)
+    ts(A("pc", 6, 7), rw, 3, O.bitwise_and)
     cp(c(ROW), rw); cp(c(P16), A("pc", 2, 3)); cp(c(PF), pp); cp(c(RG1), A("pc", 3, 4)); cp(c(W0), A("pc", 4, 5)); cp(c(ODD), A("pc", 5, 6))
     ts(c(RG0), c(RG1), -1.0, O.mult, 1.0, O.add)
     ts(c(EVR), c(ODD), -1.0, O.mult, 1.0, O.add)
@@ -209,410 +253,322 @@ def rank_program(g, core, T, topo):
     tt(c(W1), c(ODD), c(RG1), O.not_equal)
     ts(c(W2), c(W0), 32.0, O.mult)
     ts(c(W1), c(W1), 256.0, O.mult, c(W2), O.add)
-    ts(c(W2), c(RG1), 16.0, O.mult, c(W1), O.add)
-    ts(A("ofin"), A("id_", 16, 32), c(W2), O.add)
-    def tables():
-        ts(A("g8"), A("ig", 0, 8), c(P16), O.is_equal)
-        fill(A("wm"), 0.0)
-        for m in range(16): act(A("wm", 128 * m + m, 128 * m + 128, 16), A("g8"))
-        ts(A("idm"), A("ie"), c(PF), O.is_equal)
-        ts(A("ngm"), A("idm"), -1.0, O.mult)
-        ts(A("kc"), A("ia"), 2.0 ** -23, O.mult)
-        fill(A("smx"), 0.0); fill(A("smx", 0, 1024, 16), 255.0)
-        fill(A("sg1"), 1.0); fill(A("sg1", 0, 256, 16), 0.0)
-        fill(A("nsm0"), 0.0)
-
-    def row_tables():
-        fill(c(SCL), 1.0)
-        for b in range(4):
-            ts(A("pc", 7, 8), rw, b, O.arith_shift_right, 1, O.bitwise_and)
-            ts(c(W3), A("pc", 7, 8), 2.0 ** -(2 ** b) - 1.0, O.mult, 1.0, O.add)
-            tt(c(SCL), c(SCL), c(W3), O.mult)
-        eq, lt = {}, {}
-        for lim in (10, 13):
-            lt[lim] = A("sc%d" % lim)
-            act(A("sw"), c(ROW), AF.Sign, bias=lim - 0.5, scale=-1.0)
-            act(lt[lim], A("sw"), AF.Relu)
-        for r in (10, 11, 12, 13, 14, 15):
-            eq[r] = A("se%d" % r)
-            act(A("sw"), c(ROW), AF.Abs, bias=-float(r))
-            act(eq[r], A("sw"), AF.Relu, bias=1.0, scale=-1.0)
-
-        def total(i, parts):
-            for n, (m, v) in enumerate(parts):
-                act(c(i), m, AF.Identity, bias=c(i) if n else 0.0, scale=float(v))
-        total(RS, [(lt[10], 2 ** 20), (eq[10], 2 ** 14), (eq[11], 2 ** 8), (eq[12], 1), (eq[13], -2 ** 14), (eq[14], -2 ** 8), (eq[15], -1)])
-        total(C1L, [(lt[10], -1), (eq[13], 1), (eq[14], 1), (eq[15], 1)])
-        total(C1R, [(lt[10], -2), (lt[13], 1)])
-        act(c(W4), lt[10], scale=2.0)
-        act(A("cll"), A("ic"), AF.Identity, bias=c(C1L), scale=eq[12])
-        act(A("clr"), A("ic"), AF.Identity, bias=c(C1R), scale=eq[15])
-        act(A("sb2m"), A("idm"), scale=c(W4))
-        act(A("idf"), A("idm"))
-
-    def turn_a(t):
-        cp(A("in12", 0, 256), A("ci", t, V, 4))
-        act(A("in12", 256, 512), ind(A("in12", 0, 256), A("o2")))
-
-    def turn_v(t): run("V", lambda: g.vector.transpose(A("tr12")["ap"], A("in12")["ap"]), [A("tr12")], [A("in12")])
-
-    def turn_s(t): act(A("ca%d" % t), ind(A("tr12"), A("ofin")))
-
-    def list_b(t): cp(A("ct%d" % t), A("ca%d" % t))
-
-    def copies(t, f):
-        f(A("xa%d" % t), A("xb", RAW + t, RAW + V, 4))
-        for n in ("r", "p"):
-            for i in range(4): f(A("%sr%d" % (n, t), 256 * i, 256 * i + 256), A(n + "b", RAW + t, RAW + V, 4))
-
-    def squeeze(n, i, w, last):
-        for m in range(16):
-            mm(A("p4", 32 * i, 32 * (i + w)), A("wm", 128 * m, 128 * m + 128), A(n, 512 * i + m, 512 * (i + w), 16), False, last and m == 15)
-
-    def x_gather(t, i): act(A("xg", 1024 * i, 1024 * i + 1024), ind(A("xb", DUM, RAW), A("ct%d" % t, 64 * i, 64 * i + 64)))
-
-    def x_sub(t, i):
-        for h in (2 * i, 2 * i + 1):
-            p = "p%d" % (h % 4)
-            mm(A(p), A("idm"), A("xg", 512 * h, 512 * h + 512), True, False)
-            mm(A(p, 0, 256), A("ngm"), A("xa%d" % t), False, False)
-            mm(A(p, 256, 512), A("ngm"), A("xa%d" % t), False, True)
-
-    def distances(t):
-        mm(A("p4", 0, 256), A("idm"), A("kc"), True, False)
-        x_sub(t, 0)
-        for i in range(4):
-            if i < 3: x_sub(t, i + 1)
-            for h in (2 * i, 2 * i + 1): act(A("ad", 512 * h, 512 * h + 512), A("p%d" % (h % 4)), AF.Abs, scale=2.0 ** -19)
-            squeeze("ad", 2 * i, 2, False)
-
-    def tests(t):
-        todo, tv, tg = [], 0.0, 0.0
-        plan = TESTS if t else TESTS0
-        for kind, i, n, who in plan:
-            if who == "V":
-                todo.append((tv, 0, kind, i, n)); tv += 0.8 * n; todo.append((tv, 3, kind, i, n))
-            else:
-                todo.append((tg, 1, kind, i, n)); tg += 0.8 * n
-        for kind, i, n, who in plan:
-            if who == "S":
-                todo.append((tg, 2, kind, i, n)); tg += 0.65 * n; todo.append((tg, 3, kind, i, n))
-        left = len(plan)
-        for _, step, kind, i, w in sorted(todo):
-            win = A("pb" if kind == "P" else "rb", DUM, RAW)
-            mine = ("rr%d" if kind == "P" else "pr%d") % t
-            n = {"P": "tp", "R": "tr"}[kind]
-            off = A("ct%d" % t, 32 * i, 32 * (i + w))
-            if step == 0:
-                tt(A(n, 512 * i, 512 * (i + w)), ind(win, off), A(mine, 0, 512 * w), O.is_ge if kind == "P" else O.is_le)
-            elif step == 1:
-                act(A("gp", 512 * i, 512 * (i + w)), ind(win, off))
-            elif step == 2:
-                for h in range(i, i + w):
-                    p = "p%d" % (h % 4)
-                    mm(A(p), A("idm"), A("gp", 512 * h, 512 * h + 512), True, False)
-                    mm(A(p), A("ngm"), A(mine, 0, 512), False, True)
-                    act(A(n, 512 * h, 512 * h + 512), A(p), AF.Relu, bias=1.0, scale=1.0 if kind == "P" else -1.0)
-            else:
-                left -= 1
-                squeeze(n, i, w, left == 0)
-
-    def tree(srcs, op):
-        for i in range(len(srcs) - 1):
-            w = 128 >> i
-            tt(A(srcs[i + 1]), A(srcs[i], 0, w), A(srcs[i], w, 2 * w), op)
-
-    def partner(t):
-        ts(A("key"), A("p4", 0, 256), 2.0 ** 23, O.mult, 2.0 ** 22, O.min)
-        tree(("key", "k8", "k4", "k2", "mk"), O.min)
-        tt(A("eq"), ind(A("mk"), A("oq")), A("key"), O.is_equal)
-        tt(A("prd"), A("eq"), A("ca%d" % t), O.mult)
-        ts(A("has"), A("mk"), 65536.0, O.is_lt)
-        tree(("prd", "s8", "s4", "s2", "s1"), O.add)
-        tt(A("nli"), A("s1"), A("has"), O.mult)
-        cp(A("nl"), A("nli"))
-        fw = A("fl", DUM, DUM + V)
-        ts(A("fsh"), ind(fw, A("nl")), c(SCL), O.mult, -0.5 + 2.0 ** -11, O.add)
-        ts(A("kl", 0, 16), A("mk"), 10, O.arith_shift_right, 63, O.bitwise_and)
-        ts(A("fbt"), A("fsh"), 1, O.bitwise_and)
-        ts(A("pen"), A("mk"), c(LIM), O.is_ge, 128.0, O.mult)
-        ts(A("kl", 16, 32), A("mk"), 4, O.arith_shift_right, 63, O.bitwise_and)
-        cp(A("bits"), A("fbt"))
-        tt(A("kl", 0, 16), A("kl", 0, 16), A("pen"), O.add)
-        tt(A("ke"), ind(A("kl"), A("oke")), A("dg"), O.mult)
-        for p, cl in (("p6", "clr"), ("p5", "cll")): mm(A(p, 0, 256), A("idm"), A(cl), True, False)
-        for p in ("p6", "p5"): mm(A(p, 0, 256), A("sb2m"), A("bits"), False, False)
-        for p, r in (("p6", 13), ("p5", 10)):
-            mm(A(p, 0, 256), A("wm", 128 * r, 128 * r + 128), A("ke", 0, 256), False, False)
-            mm(A(p, 0, 256), A("wm", 128 * r + 128, 128 * r + 256), A("ke", 256, 512), False, True)
-        act(A("fr"), A("p6", 0, 256), scale=c(RS))
-        act(A("fev"), A("p5", 0, 256), scale=c(RG0))
-        act(A("fod"), A("p5", 0, 256), scale=c(RG1))
-        tt(A("bm"), ind(fw, A("nl")), A("dg", 0, 256), O.mult)
-        scan(A("bs"), A("sg1"), A("bm"), 0.0, O.mult, O.add)
-        v3 = A("v3", 48 * t, 48 * t + 48)
-        cp(A("nb3", 0, 16), A("nli"))
-        ts(A("nb3", 16, 32), A("bs", 15, 256, 16), float(DUM), O.add)
-        cp(A("nb3", 32, 48), A("bs", 15, 256, 16))
-        tt(A("d3"), A("nb3"), v3, O.subtract)
-        ts(A("ask"), A("mk"), c(LIM), O.is_lt)
-        tt(A("bc"), A("d3", 32, 48), A("has"), O.mult)
-        tt(A("bc"), A("bc"), A("v3", 48 * t + 32, 48 * t + 48), O.add)
-        for i in range(3): tt(A("d3", 16 * i, 16 * i + 16), A("d3", 16 * i, 16 * i + 16), A("ask"), O.mult)
-        cp(A("bcu"), A("bc"))
-        if t + 1 < RO: list_b(t + 1)
-        seen = {"V": 0, "S": 0}
-        for a in range(16):
-            gr, h, who = a // 2, a % 2, PAIRS[a]
-            p = {"V": ("p0", "p2", "p5"), "S": ("p1", "p3", "p6")}[who][seen[who] % 3]
-            seen[who] += 1
-            lo = 32 * (gr // 2)
-            mm(A(p, 0, 256), A("fod" if gr % 2 else "fev", 128 * h, 128 * h + 128, p0=lo, p1=lo + 32), A("fr", p0=lo, p1=lo + 32), True, True)
-            if who == "V": reduce(A("mx", a, a + 1), A(p, 0, 256), O.max)
-            else: act(A("junk"), A(p, 0, 256), AF.Relu, bias=-B10, acc=A("mx", a, a + 1))
-        tt(A("we"), ind(A("mx"), A("omx")), A("thr"), O.is_le)
-        for h in range(2): mm(A("p7", 0, 48), A("we", 128 * h, 128 * h + 128), A("rq", 48 * h, 48 * h + 48), h == 0, h == 1)
-        tt(A("t3"), A("p7", 0, 48), A("d3"), O.mult)
-        tt(A("t3"), A("t3"), v3, O.add)
-        cp(A("l3"), A("t3"))
-
-    nl2, sc, sl = A("l3", 0, 16), A("l3", 16, 32), A("l3", 32, 48)
-
-    def selfmark(n, t, new, p, sign, op):
-        w = A(n, DUM + t, GH, 4)
-        mm(A(p, 0, 256), A("idm"), new, True, False)
-        mm(A(p, 0, 256), A(sign), A("nsm%d" % (t % 2)), False, True)
-        tt(w, w, A(p, 0, 256), op)
-
-    def merge(t):
-        tt(A("r2"), ind(A("rb", DUM, WID), nl2), A("rr%d" % t, 0, 256), O.min)
-        ts(A("sx"), ind(A("sb"), sl), c(ODD), O.mult)
-        scat(A("rb", 0, GH), sc, A("r2"))
-        tt(A("sb", t, V, 4), A("sx"), A("sev"), O.add)
-        cp(A("so"), A("sb", t, V, 4))
-        selfmark("rb", t, A("r2"), "p1", "idm", O.min)
-
-    def succ_gather(chunks):
-        for a, b in chunks: act(A("sg", a, b), ind(A("rb", DUM, RAW), A("so", a // 16, b // 16)))
-
-    def succ_min(t):
-        for a, b in SUCC: scan(A("sc", a, b), A("smx", 0, b - a), A("sg", a, b), 255.0, O.max, O.min)
-        tt(A("rn%d" % t), A("sc", 15, 4096, 16), A("r2"), O.min)
-
-    def pmerge(t): tt(A("pn%d" % t), ind(A("pb", DUM, WID), nl2), A("pr%d" % t, 0, 256), O.max)
-
-    def xmerge(t):
-        tt(A("xs"), ind(A("xb", DUM, WID), nl2), A("xa%d" % t), O.add)
-        ts(A("xh"), A("xs"), 1, O.arith_shift_right)
-        cp(A("xb", RAW + t, RAW + V, 4), A("xh"))
-
-    def c_flags():
-        for k in range(16): mm(A("p5", 0, 256), A("wm", 128 * k, 128 * k + 128), A("tp", 256 * k, 256 * k + 256), k == 0, False)
-        for k in range(16): mm(A("p5", 0, 256), A("wm", 128 * k, 128 * k + 128), A("tr", 256 * k, 256 * k + 256), False, k == 15)
-        act(A("os"), A("p5", 0, 256), AF.Sign)
-
-    def c_update(t):
-        tt(A("cd"), ind(A("cb"), A("bcu")), A("ci", t, V, 4), O.subtract)
-        tt(A("od"), A("os"), A("cd"), O.mult)
-        tt(A("cb", t, V, 4), A("cb", t, V, 4), A("od"), O.add)
-
-    def marks(u):
-        ns = A("nsm%d" % (u % 2))
-        mm(A("p2", 0, 256), A("idf"), A("fl", DUM + u, DUM + V, 4), True, False)
-        mm(A("p2", 0, 256), A("idf"), A("nv", DUM + u, DUM + V, 4), False, True)
-        act(ns, A("p2", 0, 256), AF.Abs, scale=PEN)
-        act(A("p3", 0, 256), ns, AF.Relu, bias=PEN, scale=-1.0)
-
-    def windows(t):
-        xr, u = A("xb", RAW + t, RAW + V, 4), t + 1
-        scat(A("xb", 0, GH), sc, xr)
-        selfmark("xb", t, xr, "p0", "idm", O.min)
-        f_changes(t)
-        tt(A("xb", DUM + u, GH, 4), A("xb", DUM + u, GH, 4), A("p3", 0, 256), O.max)
-
-    def f_list(t):
-        for m in range(16): mm(A("p6", 0, 32), A("em", 128 * m, 128 * m + 128), A("fl", DUM + m, DUM + G5, 16), m == 0, m == 15)
-
-    def f_changes(t):
-        cp(A("fli"), A("p6", 0, 32))
-        tt(A("dp"), A("pn%d" % t, 0, 128), A("pr%d" % t, 0, 128), O.not_equal)
-        ts(A("flt"), A("p6", 0, 32), float(G5), O.is_lt)
-        ts(A("fli"), A("fli"), 3, O.bitwise_and)
-        tt(A("dfl"), A("p6", 0, 32), A("fvs"), O.subtract)
-        ts(A("chf"), A("fli"), float(t), O.is_equal, c(NRS + t), O.mult)
-        tt(A("dfl"), A("dfl"), A("flt"), O.mult)
-        mm(A("p7", 128, 160), A("idm"), A("chf"), True, False)
-        changed("dp", t, False)
-
-    def changed(n, t, last):
-        for a in range(4):
-            m = 4 * a + t
-            mm(A("p7", 128, 160), A("wm", 128 * m, 128 * m + 128), A(n, a, 128, 4), False, last and a == 3)
-
-    def publish(t):
-        tt(A("dr"), A("rn%d" % t, 0, 128), A("rr%d" % t, 0, 128), O.not_equal)
-        changed("dr", t, True)
-        ts(A("ch"), A("p7", 128, 160), 0.0, O.is_gt)
-        scan(A("scq"), A("one"), A("ch"), 0.0, O.mult, O.add)
-        ts(A("c96"), A("ch"), float(CAP + 1), O.mult, -1.0, O.add)
-        mm(A("p7", 192, 224), A("ltm"), A("ch"), True, False)
-        mm(A("p7", 192, 224), A("bom"), A("scq"), False, True)
-        tt(A("go"), A("p7", 192, 224), A("c96"), O.is_le)
-        ts(A("ge"), A("go"), c(PM + t), O.mult)
-        tt(A("gf"), A("go"), A("dfl"), O.mult)
-        tt(A("e5"), A("e5"), A("ge"), O.max)
-        tt(A("fvs"), A("fvs"), A("gf"), O.add)
-        tt(A("zf"), A("e5"), A("fvs"), O.add)
-        cp(A("z%d" % t), A("zf"))
-        send([(A("z%d" % t), A("lz%d" % t, 0, 32), A("lz%d" % t, 32, 64))], ["az%%s%d" % t], 2)
-
-    def pwin(t):
-        scat(A("pb", 0, GH), sc, A("pn%d" % t))
-        selfmark("pb", t, A("pn%d" % t), "p2", "ngm", O.max)
-
-    def rwin(t):
-        scat(A("rb", 0, GH), sc, A("rn%d" % t))
-        selfmark("rb", t, A("rn%d" % t), "p1", "idm", O.min)
-        ts(A("sev"), A("si", t + 1, V, 4), c(EVR), O.mult)
-        act(A("rb", RAW + t, RAW + V, 4), A("rn%d" % t))
-
-    def count(t):
-        tt(A("wn"), A("p7", 0, 16), A("ask"), O.mult)
-        mm(A("p7", 256, 272), A("onm"), A("wn"), True, True)
-        reduce(A("mt", 0, 1), A("p7", 256, 272), O.add)
-        cp(A("mi", 0, 1), A("mt", 0, 1))
-        ts(A("mi", 1, 2), A("mi", 0, 1), 31, O.bitwise_and)
-        ts(c(LIM), A("mi", 1, 2), 16.0, O.mult, c(TH16), O.add)
-
-    def block(kind, t):
-        n = "%sn%d" % (kind, t)
-        send([(A(n, 0, 128), A("l%sa%d" % (kind, t)), A("l%sb%d" % (kind, t)))], ["a%s%%s%d" % (kind, t)], 2)
-        for s, S in (("a", "A"), ("b", "B")): arrive("a%s%s%d" % (kind, S, t), 2, [A("l%s%s%d" % (kind, s, t))])
-
-    def ghosts(t):
-        arrive("azA%d" % t, 2, [A("lz%d" % t, 0, 32)]); arrive("azB%d" % t, 2, [A("lz%d" % t, 32, 64)])
-        for s in "ab":
-            cp(A("rw" + s, G5 + t, 2 * G5, 4), A("lr%s%d" % (s, t)))
-            act(A("pw" + s, G5 + t, 2 * G5, 4), A("lp%s%d" % (s, t)))
-        cp(A("zi"), A("lz%d" % t))
-        ts(A("ei"), A("zi"), 512, O.bitwise_and)
-        ts(A("fi"), A("zi"), 511, O.bitwise_and)
-        tt(A("ei"), A("ei"), A("jl"), O.add)
-        cp(A("fu"), A("fi"))
-        cp(A("eu"), A("ei"))
-        for i, s in enumerate("ab"):
-            act(A("pv" + s), ind(A("pw" + s), A("eu", 32 * i, 32 * i + 32)))
-            cp(A("rv" + s), ind(A("rw" + s), A("eu", 32 * i, 32 * i + 32)))
-        for i, (s, w) in enumerate((("a", gA), ("b", gB))):
-            act(A("pb", *w), ind(A("pv" + s), A("fu", 32 * i, 32 * i + 32)))
-            cp(A("rb", *w), ind(A("rv" + s), A("fu", 32 * i, 32 * i + 32)))
-
-    turn_a(0)
-    tables()
-    turn_v(0)
-    turn_s(0)
-    fill(A("xb", DUM, GH, 4), PEN)
-    list_b(0)
-    turn_a(1)
-    copies(0, cp)
-    turn_v(1)
-    iota(A("ik"), [[1, 8], [0, 16]])
-    ts(A("b8"), A("ik"), c(PF), O.is_equal)
-    cp(A("thf", 0, 1, p1=8), A("thi", 0, 1, p1=8))
-    mm(A("p7", 0, 1), A("b8", p1=8), A("thf", 0, 1, p1=8), True, True)
-    ts(c(TH16), A("p7", 0, 1), 16.0, O.mult)
-    cp(c(LIM), c(TH16))
-    for i in range(4): x_gather(0, i)
-    distances(0)
-    iota(A("ib"), [[0, 16], [1, 16]])
-    iotf(A("ic"), [[1, 256]])
-    iota(A("ih", 0, 16), [[1, 2], [2, 8]]); iota(A("ih", 16, 48), [[1, 32]])
-    iota(A("ij", 0, 16), [[0, 16]], 0, 1); iota(A("ij", 16, 32), [[16, 16]], 0, 1)
-    iotf(A("vi"), [[1, DUM + V]], -DUM); iotf(A("fl"), [[1, DUM + V]], -DUM); iotf(A("nv"), [[-1, DUM + V]], DUM)
-    iota(A("in_", 0, 96), [[-8, 2], [0, 3], [1, 16]])
-    iota(A("id_", 32, 96), [[0, 2], [16, 32]], 0, 1)
-    iotf(A("em"), [[0, 2048]])
-    ts(A("dg", 0, 256), A("ib"), c(ROW), O.is_equal); ts(A("dg", 256, 512), A("ib"), c(ROW), O.is_equal)
+    ts(c(W3), c(RG1), 16.0, O.mult, c(W1), O.add)
+    ts(A("ofin"), A("id_", 16, 32), c(W3), O.add)
+    W = lambda n, m: A(n, 128 * m, 128 * m + 128)
+    ts(A("g8"), A("ig", 0, 8), c(P16), O.is_equal)
+    fill(A("wm"), 0.0)
+    for m in range(16): act(A("wm", 128 * m + m, 128 * m + 128, 16), A("g8"))
+    ts(A("idm"), A("ie"), c(PF), O.is_equal)
+    for n, v in (("ngm", -1.0), ("hm", 0.5), ("bgm", 4096.0), ("nbm", -4096.0), ("zm", 0.0), ("idf", 1.0)): act(A(n), A("idm"), scale=v)
+    ts(A("kc"), A("ic"), 2.0 ** -20, O.mult)
+    fill(A("smx"), 0.0); fill(A("smx", 0, 1024, 8), 255.0)
+    fill(A("sg1"), 1.0); fill(A("sg1", 0, 256, 16), 0.0); fill(A("mh"), -0.5)
+    ts(A("dg", 0, 256), A("ib"), c(ROW), O.is_equal); act(A("dg", 256, 512), A("dg", 0, 256))
+    ts(c(L10), c(ROW), 10.0, O.is_lt); ts(c(C1L), c(ROW), 13.0, O.is_ge); ts(c(E12), c(ROW), 12.0, O.is_equal); ts(c(E15), c(ROW), 15.0, O.is_equal)
+    ts(c(W4), c(ROW), 13.0, O.is_lt, c(L10), O.subtract); cp(c(C1R), c(W4))
+    ts(c(M2), c(C1R), c(E12), O.subtract)
+    for a, b, v in ((0, 10, 2.0 ** 20), (10, 11, 2.0 ** 14), (11, 12, 256.0), (12, 13, 1.0), (13, 14, -2.0 ** 14), (14, 15, -256.0), (15, 16, -1.0)): fill(A("wv", a, b), v)
+    tt(A("wx"), A("wv"), A("dg", 0, 16), O.mult); reduce(c(RS), A("wx"), O.add)
+    act(A("cll"), A("ic"), AF.Identity, bias=c(C1L), scale=c(E12)); act(A("clr"), A("ic"), AF.Identity, bias=c(C1R), scale=c(E15))
+    act(A("s10"), A("idm"), scale=c(L10))
+    ts(A("wm2"), A("wm"), c(M2), O.mult)
+    ts(A("bom"), A("ik"), c(P16), O.is_equal)
+    ts(A("lw"), A("dg", 0, 16), 1024.0, O.mult)
+    for m in range(16): act(W("wt", m), A("bom"), scale=A("lw", m, m + 1))
+    ts(A("lh"), A("ie"), c(PF), O.is_lt, -1.0, O.mult); tt(A("ltm"), A("lh"), A("bom"), O.mult)
+    fill(A("one"), 1.0); fill(A("onm"), 1.0); fill(A("e5"), 0.0)
+    cp(c(W5), A("pc", 6, 7))
+    for t in range(RO - 1): ts(c(PM + t), c(W5), float(t), O.is_le)
+    for r in range(5): iota(A("pat", 32 * r, 32 * r + 32), [[0, 16 >> r], [2, 2], [0, 1 << r]], -1)
+    iota(A("pat", 160, 192), [[1, 32]]); iota(A("pat", 192, 224), [[32, 32]])
+    pt = lambda i: A("pat", 32 * i, 32 * i + 32)
+    mms([(A("p6", 0, 32), W("wm", r), pt(r)) for r in range(5)] + [(A("p6", 0, 32), W("wm", 11), pt(5))])
+    mms([(A("p6", 32, 64), W("wm", r + 5), pt(r)) for r in range(5)] + [(A("p6", 32, 64), W("wm", 10), pt(6))])
+    act(A("tc"), A("p6", 0, 32), scale=1.0 / 16); act(A("ta"), A("p6", 32, 64), scale=1.0 / 16)
+    for a in range(32): act(A("bw", DUM + 32 * a, DUM + 32 * a + 32), A("tc"), AF.Identity, bias=A("ta", a, a + 1))
+    ts(A("bs"), A("bw", DUM, DUM + V), c(E12), O.add)
+    iota(A("pa"), [[0, 128], [128, 4]], 128); iota(A("pb_"), [[0, 128], [-1, 4]], 3); iota(A("pc_"), [[-1, 128], [0, 4]], 127)
+    mms([(A("p6"), W("wm", m), A(n)) for m, n in enumerate(("pa", "pb_", "pc_", "pc_", "pc_"))])
+    act(A("dig"), A("p6"), scale=1.0 / 16)
+    for par in range(2):
+        ts(c(CA + par), c(NG), -1.0, O.mult, c(W0), O.add)
+        if par: ts(c(CA + par), c(CA + par), 8.0, O.add)
+        ts(A("la%d" % par), A("ie"), c(CA + par), O.is_equal, c(ODD), O.mult); ts(A("lb_%d" % par), A("ie"), c(CA + par), O.is_equal, c(EVR), O.mult)
     cp(A("oke"), A("ih", 16, 48)); cp(A("omx"), A("ih", 0, 16))
-    ts(A("oq"), A("ij", 0, 16), c(NG), O.add)
     for a in range(16):
         o = 128 * (a % 2) + 16 * (a // 2)
         if a == 0: ts(A("thr"), A("dg", 0, 256), 1e9 + 0.5, O.mult, -1e9, O.add)
         if PAIRS[a] == "V": ts(A("thr", o, o + 16), A("dg", 0, 16), 1e9 + B10, O.mult, -1e9, O.add)
-    ts(A("rq"), A("in_", 0, 96), c(P16), O.is_equal)
-    ts(A("lw"), A("ij", 16, 32), c(NG), O.add)
+    ts(A("rs"), A("in_", 0, 96), c(P16), O.is_equal)
+    ts(A("wx"), A("ij", 16, 32), c(NG), O.add)
     for t in range(RO):
-        o = 48 * t
-        ts(A("v3", o, o + 16), A("lw"), 4.0, O.mult, float(2048 + t), O.add)
-        cp(A("v3", o + 16, o + 32), A("lw"))
-        ts(A("v3", o + 32, o + 48), A("lw"), 4.0, O.mult, float(t), O.add)
-    cp(A("sb"), A("si"))
-    ts(A("sev"), A("si", 0, V, 4), c(EVR), O.mult)
-    for n in ("r", "p"):
-        for s, w in (("a", gA), ("b", gB)):
-            for o in (0, G5):
-                dma("D", A(n + "w" + s, o, o + G5)["ap"], A(n + "b", *w)["ap"], [A(n + "b", *w)], [A(n + "w" + s, o, o + G5)])
+        for n, o in (("v3", 0.0), ("vm", -float(DUM))):
+            ts(A(n, 48 * t, 48 * t + 16), A("wx"), 4.0, O.mult, float(t), O.add)
+            ts(A(n, 48 * t + 16, 48 * t + 32), A("wx"), 4.0, O.mult, float(V + t), O.add)
+            ts(A(n, 48 * t + 32, 48 * t + 48), A("wx"), o, O.add)
+    ts(A("fvs"), A("id_", 32, 64), c(NG), O.add); ts(A("flo"), A("id_", 32, 64), c(NG), O.add)
+    ts(A("b8"), A("ik"), c(PF), O.is_equal)
+    cp(A("thf", 0, 1, p1=8), A("thi", 0, 1, p1=8))
+    mms([(A("p7", 0, 1), A("b8", p1=8), A("thf", 0, 1, p1=8))])
+    ts(c(TH), A("p7", 0, 1), 256.0, O.mult); cp(c(LIM), c(TH))
+    cp(A("cb"), A("ci")); cp(A("sb"), A("si"))
 
-    def border():
-        for m in range(16): act(A("em", 128 * m + m, 128 * m + 128, 16), A("idm", m, 128, 16))
-        ts(A("bom"), A("ik"), c(P16), O.is_equal)
-        ts(A("lh"), A("ie"), c(PF), O.is_lt, -1.0, O.mult)
-        tt(A("ltm"), A("lh"), A("bom"), O.mult)
-        ts(A("jl"), A("id_", 32, 96), c(NG), O.add)
-        cp(A("fvs"), A("jl", 0, 32)); fill(A("e5"), 0.0)
-        fill(A("one"), 1.0); fill(A("onm"), 1.0)
-        ts(A("pc", 7, 8), rw, 3, O.bitwise_and)
-        cp(c(W3), A("pc", 7, 8))
-        for t in range(RO - 1):
-            ts(c(NRS + t), c(W3), float(t), O.not_equal)
-            ts(c(PM + t), c(W3), float(t), O.is_le, 512.0, O.mult)
+    key = {}
 
+    def turn(t):
+        if t: act(A("in12", 0, 256), A("cb", t, V, 4))
+        else: cp(A("in12", 0, 256), A("ci", t, V, 4))
+        act(A("in12", 256, 512), ind(A("in12", 0, 256), A("o2")))
+        for h in range(2): turn32(A("tr12", 256 * h, 256 * h + 256), A("in12", 256 * h, 256 * h + 256))
+        if t:
+            act(A("ca%d" % t), ind(A("tr12"), A("ofin"))); cp(A("ct%d" % t), A("ca%d" % t))
+        else:
+            cp(A("ct0"), ind(A("tr12"), A("ofin"))); act(A("ca0"), ind(A("tr12"), A("ofin")))
+
+    def even_list(t):
+        mms([(A("p6", 0, 128), A("lb_%d" % par), A("sb", t + 4 * par, V, 8)) for par in range(2)])
+        cp(A("lb%d" % t), A("p6", 0, 128))
+
+    def squeeze(n, i, w):
+        p, o = "p%d" % (4 + i // 4), 32 * (i % 4)
+        mms([(A(p, o, o + 32 * w), W("wm", m), A(n, 512 * i + m, 512 * (i + w), 16)) for m in range(16)], key[p])
+
+    def distances(t):
+        for h in range(2):
+            p = "p%d" % (4 + h); key[p] = {}
+            mms([(A(p, 0, 128), A("idm"), A("kc", 128 * h, 128 * h + 128))], key[p])
+        mine = A("xq", V + t, 2 * V, 4)
+        for h in range(8):
+            p, x = "p%d" % (h % 2), A("xg", 512 * h, 512 * h + 512)
+            act(x, ind(A("xw"), A("ct%d" % t, 32 * h, 32 * h + 32)))
+            mms([(A(p), A("idm"), x), (A(p, 0, 256), A("ngm"), mine), (A(p, 256, 512), A("ngm"), mine)])
+            act(A("ad", 512 * h, 512 * h + 512), A(p), AF.Abs, scale=2.0 ** -12)
+            if h % 2: squeeze("ad", h - 1, 2)
+
+    def tests(t):
+        k = 0
+        for lo in (0, 4):
+            for kind in "PR":
+                win, mine, n = (A("pb"), A("rq", t, 2 * V, 4), "tp") if kind == "P" else (A("rb", DUM), A("pq", t, 2 * V, 4), "tr")
+                for h in range(lo, lo + 4):
+                    off, out = A("ct%d" % t, 32 * h, 32 * h + 32), A(n, 512 * h, 512 * h + 512)
+                    if (TESTS if t else TESTS0)[kind][h] == "V": tt(out, ind(win, off), mine, O.is_ge if kind == "P" else O.is_le)
+                    else:
+                        p, x = "p%d" % (2 + k % 2), A("gp", 512 * k, 512 * k + 512); k += 1
+                        act(x, ind(win, off))
+                        mms([(A(p), A("idm"), x), (A(p), A("ngm"), mine)])
+                        act(out, A(p), AF.Relu, bias=1.0, scale=1.0 if kind == "P" else -1.0)
+                    if lo and h >= 6: squeeze(n, h, 1)
+                    elif h % 2: squeeze(n, h - 1, 2)
+
+    sl, xl, sc = A("l3", 0, 16), A("l3", 16, 32), A("l3", 32, 48)
+
+    def partner(t):
+        act(A("klo"), A("p4", 0, 128))
+        tt(A("k8"), A("p5", 0, 128), A("klo"), O.min)
+        for a, b, w in (("k8", "k4", 64), ("k4", "k2", 32), ("k2", "k1", 16)): tt(A(b), A(a, 0, w), A(a, w, 2 * w), O.min)
+        ts(A("mk"), A("k1"), 2.0 ** 20, O.mult, 2.0 ** 21, O.min)
+        ts(A("kq"), A("mk"), 255, O.bitwise_and); cp(A("kqu"), A("kq"))
+        tt(A("cm"), ind(A("ca%d" % t), A("kqu")), A("dg", 0, 256), O.mult)
+        scan(A("cs"), A("sg1"), A("cm"), 0.0, O.mult, O.add)
+        cp(A("cu"), A("cs", 15, 256, 16))
+        act(A("bits"), ind(A("bw", DUM), A("cu")))
+        ts(A("kl", 0, 16), A("mk"), 14, O.arith_shift_right, 63, O.bitwise_and)
+        ts(A("pen"), A("mk"), c(LIM), O.is_ge, 128.0, O.mult)
+        ts(A("kl", 16, 32), A("mk"), 8, O.arith_shift_right, 63, O.bitwise_and)
+        tt(A("kl", 0, 16), A("kl", 0, 16), A("pen"), O.add)
+        tt(A("ke"), ind(A("kl"), A("oke")), A("dg"), O.mult)
+        for p, cl, r in (("p5", "clr", 13), ("p4", "cll", 10)):
+            grp, o = {}, A(p, 0, 256)
+            mms([(o, A("idm"), A(cl))], grp); mms([(o, A("s10"), A("bits"))], grp)
+            mms([(o, W("wm", r), A("ke", 0, 256)), (o, W("wm", r + 1), A("ke", 256, 512))], grp)
+        ts(A("fr"), A("p5", 0, 256), c(RS), O.mult)
+        act(A("fev"), A("p4", 0, 256), scale=c(RG0)); act(A("fod"), A("p4", 0, 256), scale=c(RG1))
+        mms([(A("p7", 0, 16), W("wm2", m), A("bits", m, 256, 16)) for m in range(16)])
+        for i in range(3): tt(A("d3", 16 * i, 16 * i + 16), A("p7", 0, 16), A("vm", 48 * t + 16 * i, 48 * t + 16 * i + 16), O.subtract)
+        ts(A("ask"), A("mk"), c(LIM), O.is_lt); ts(A("has"), A("mk"), 2.0 ** 20, O.is_lt)
+        tt(A("bc"), A("d3", 0, 16), A("has"), O.mult); tt(A("bc"), A("bc"), A("v3", 48 * t, 48 * t + 16), O.add); cp(A("bcu"), A("bc"))
+        for i in range(3): tt(A("d3", 16 * i, 16 * i + 16), A("d3", 16 * i, 16 * i + 16), A("ask"), O.mult)
+        seen = {"V": 0, "S": 0}
+        for a in range(16):
+            gr, h, who = a // 2, a % 2, PAIRS[a]
+            p = {"V": ("p0", "p2"), "S": ("p1", "p3")}[who][seen[who] % 2]
+            seen[who] += 1
+            lo = 32 * (gr // 2)
+            mms([(A(p, 0, 256), A("fod" if gr % 2 else "fev", 128 * h, 128 * h + 128, p0=lo, p1=lo + 32), A("fr", p0=lo, p1=lo + 32))])
+            if who == "V": reduce(A("mx", a, a + 1), A(p, 0, 256), O.max)
+            else: act(A("junk"), A(p, 0, 256), AF.Relu, bias=-B10, acc=A("mx", a, a + 1))
+        tt(A("we"), ind(A("mx"), A("omx")), A("thr"), O.is_le)
+        mms([(A("p7", 64, 112), A("we", 128 * h, 128 * h + 128), A("rs", 48 * h, 48 * h + 48)) for h in range(2)])
+        tt(A("t3"), A("p7", 64, 112), A("d3"), O.mult)
+        if t + 1 < RO: tt(A("wn"), A("p7", 64, 80), A("ask"), O.mult)
+        tt(A("t3"), A("t3"), A("v3", 48 * t, 48 * t + 48), O.add)
+        cp(A("l3"), A("t3"))
+
+    def merge(t):
+        grp, w = {}, A("rb", DUM + t, DUM + V, 4)
+        tt(A("r2"), ind(A("rq", 0, V), sl), A("rq", V + t, 2 * V, 4), O.min)
+        act(A("sx"), ind(A("sb"), sl))
+        scat(A("rb", 0, DUM + V), sc, A("r2"))
+        mms([(A("p6", 0, 256), W("wt", 12), A("bw", DUM + t, DUM + V, 4))], grp); mms([(A("p6", 0, 256), A("idm"), A("r2"))], grp)
+        tt(w, w, A("p6", 0, 256), O.min)
+        mms([(A("p5", 0, 128), A("la%d" % par), A("sx", par, 256, 2)) for par in range(2)])
+        cp(A("la"), A("p5", 0, 128))
+
+    def count():
+        mms([(A("p7", 448, 464), A("onm"), A("wn"))])
+        reduce(A("mt", 0, 1), A("p7", 448, 464), O.add)
+        cp(A("mi", 0, 1), A("mt", 0, 1)); ts(A("mi", 1, 2), A("mi", 0, 1), 31, O.bitwise_and)
+        ts(A("mt", 1, 2), A("mi", 1, 2), 256.0, O.mult, c(TH), O.add); ts(c(LIM), A("mt", 1, 2), 2.0 ** 20, O.min)
+
+    def names(t):
+        scat(A("bw", 0, DUM + V), sc, A("bs", t, V, 4))
+        mms([(A("p7", 128, 192), W("wm2", m), A("bw", DUM + m, DUM + V, 16)) for m in range(16)])
+        f = A("p7", 128, 160)
+        cp(A("flu"), A("p7", 128, 192))
+        tt(A("chf"), f, A("flo"), O.not_equal); cp(A("flo"), f)
+        ts(A("flt"), f, float(G5), O.is_lt); tt(A("dfl"), f, A("fvs"), O.subtract); tt(A("dfl"), A("dfl"), A("flt"), O.mult)
+
+    def block(kind, t):
+        o = G5 + 128 * t
+        send([(A("%sn%d" % (kind, t), 0, 128), A(kind + "wa", o, o + 128), A(kind + "wb", o, o + 128))], "a%s%%s%d" % (kind, t), 1.5)
+
+    def pmerge(t):
+        tt(A("pn%d" % t), ind(A("pq", 0, V), sl), A("pq", V + t, 2 * V, 4), O.max)
+        block("p", t)
+        cp(A("pq", t, V, 4), A("pn%d" % t))
+        tt(A("dp"), A("pn%d" % t, 0, 128), A("pq", V + t, V + G5, 4), O.not_equal)
+
+    def xmerge(t):
+        grp, o = {}, A("p6", 256, 512)
+        act(A("xp"), ind(A("xq"), xl))
+        mms([(o, A("hm"), A("xq", V + t, 2 * V, 4)), (o, A("hm"), A("mh"))], grp); mms([(o, A("hm"), A("xp"))], grp)
+        ts(A("xq", t, V, 4), o, MAGIC, O.add, MAGIC, O.subtract)
+
+    def successors(t, h):
+        for i in (2 * h, 2 * h + 1):
+            a, b = A("sga", 512 * i, 512 * i + 512), A("sgb", 512 * i, 512 * i + 512)
+            act(b, ind(A("rb", DUM), A("lb%d" % t, 32 * i, 32 * i + 32)))
+            tt(a, ind(A("rb", DUM), A("la", 32 * i, 32 * i + 32)), b, O.min)
+        o = 1024 * h
+        scan(A("sc", o, o + 1024), A("smx"), A("sga", o, o + 1024), 255.0, O.max, O.min)
+        tt(A("rn%d" % t, 128 * h, 128 * h + 128), A("sc", o + 7, o + 1024, 8), A("r2", 128 * h, 128 * h + 128), O.min)
+
+    def publish(t):
+        tt(A("dr"), A("rn%d" % t, 0, 128), A("rq", V + t, V + G5, 4), O.not_equal)
+        grp, o = {}, A("p7", 256, 288)
+        mms([(o, A("idm"), A("chf"))], grp)
+        for n in ("dp", "dr"): mms([(o, W("wm", 4 * a + t), A(n, a, 128, 4)) for a in range(4)], grp)
+        ts(A("ch"), o, 0.0, O.is_gt)
+        scan(A("scq"), A("one"), A("ch"), 0.0, O.mult, O.add)
+        ts(A("c96"), A("ch"), float(CAP + 1), O.mult, -1.0, O.add)
+        grp, o = {}, A("p7", 320, 352)
+        mms([(o, A("ltm"), A("ch"))], grp); mms([(o, A("bom"), A("scq"))], grp)
+        tt(A("go"), o, A("c96"), O.is_le)
+        grp, rows = {}, [m for m in range(16) if m % 4 <= t]
+        mms([(A("p6"), A("zm"), A("dig"))], grp)
+        if t: mms([(A("p6", m, G5, 16), W("wt", m), A("e5")) for m in rows], grp)
+        mms([(A("p6", m, G5, 16), W("wt", m), A("go")) for m in rows], grp)
+        tt(A("dt"), A("p6"), A("dig"), O.min)
+        tt(A("gf"), A("go"), A("dfl"), O.mult); tt(A("fvs"), A("fvs"), A("gf"), O.add); cp(A("fu"), A("fvs"))
+        cp(A("dgt"), ind(A("dt"), A("fu")))
+        grp, o = {}, A("p7", 384, 416)
+        mms([(o, A("idf"), A("fvs"))], grp); mms([(o, W("wm", m), A("dgt", m, G5, 16)) for m in range(16)], grp)
+        cp(A("z%d" % t), o)
+        send([(A("z%d" % t), A("lz%d" % t, 0, 32), A("lz%d" % t, 32, 64))], "az%%s%d" % t, 1.2)
+        if t + 2 < RO:
+            ts(A("ge"), A("go"), c(PM + t), O.mult); tt(A("e5"), A("e5"), A("ge"), O.add)
+
+    def candidates(t):
+        grp, own = {}, A("cb", t, V, 4)
+        for n in ("tp", "tr"):
+            for k0 in (0, 8): mms([(A("p2", 0, 256), W("wm", k), A(n, 256 * k, 256 * k + 256)) for k in range(k0, k0 + 8)], grp)
+        act(A("os"), A("p2", 0, 256), AF.Sign)
+        act(A("cx"), ind(A("cb"), A("bcu")))
+        for o, m in ((0, "bgm"), (256, "nbm")): mms([(A("p3", o, o + 256), A("idf"), own), (A("p3", o, o + 256), A(m), A("os"))])
+        tt(A("cy"), A("p3", 0, 256), A("cx"), O.min)
+        tt(own, A("p3", 256, 512), A("cy"), O.max)
+
+    def again(n, out, raw):
+        for h in range(2): copy(AGAIN[n], A(out[0], out[1] + G5 * h, out[1] + G5 * h + G5), ind(A(raw, 0, V), A("flu", 32 * h, 32 * h + 32)))
+
+    turn(0)
+    fill(A("xw", 0, V, 4), PEN)
+    distances(0)
+    even_list(0)
     for t in range(RO):
         last = t == RO - 1
         tests(t)
-        if t == 0: row_tables()
-        c_flags()
-        if not last:
-            turn_s(t + 1)
-            copies(t + 1, act)
-        if t == 0: border()
+        if not last: turn(t + 1)
         partner(t)
         merge(t)
-        if last:
-            succ_gather(SUCC[:3])
-            for a, b in SUCC[3:]: cp(A("sg", a, b), ind(A("rb", DUM, RAW), A("so", a // 16, b // 16)))
-        else:
-            scat(A("fl", 0, DUM + V), sc, A("vi", DUM + t, DUM + V, 4))
-            if t + 2 < RO: turn_a(t + 2)
-            succ_gather(SUCC[:2])
-            marks(t + 1)
-            succ_gather(SUCC[2:])
-            pmerge(t)
-            block("p", t)
-            f_list(t)
+        if not last:
+            names(t); pmerge(t)
         xmerge(t)
         if last:
-            dma("D", T.yx[:], RWb("xb")["ap"], [RWb("xb")], [])
-            c_update(t)
-            dma("D", T.yc[:], A("cb")["ap"], [A("cb")], [])
-            succ_min(t)
-            cp(A("rb", RAW + t, RAW + V, 4), A("rn%d" % t))
-            dma("D", T.yr[:], RWb("rb")["ap"], [RWb("rb")], [])
+            dma(T.yx[:], A("xq", 0, V)["ap"], [A("xq", 0, V)], [], 256)
+            candidates(t)
+            dma(T.yc[:], A("cb")["ap"], [A("cb")], [], 512)
+            for h in range(2):
+                successors(t, h)
+                o = G5 * h
+                cp(A("rq", o + t, o + G5, 4), A("rn%d" % t, 128 * h, 128 * h + 128))
+                dma(T.yr[:, o:o + G5], A("rq", o, o + G5)["ap"], [A("rq", o, o + G5)], [], 128)
             continue
-        windows(t)
-        for i in range(4): x_gather(t + 1, i)
-        succ_min(t)
+        act(A("sb", t, V, 4), A("sx"))
+        even_list(t + 1)
+        successors(t, 0)
         block("r", t)
         publish(t)
-        pwin(t)
-        rwin(t)
+        count()
+        successors(t, 1)
+        candidates(t)
+        fill(A("xq", t + 1, V, 4), PEN)
+        again("x", ("xw", 0), "xq")
         distances(t + 1)
-        if t == 0: cp(A("cb"), A("ci"))
-        c_update(t)
-        if t + 2 < RO: turn_v(t + 2)
-        ghosts(t)
-        count(t)
-    for i in range(free["ls"]):
-        for (s, v) in [k for k in snap if k[0] == "ls%d" % i]: wait("G", s, v)
+        again("p", ("pb", 0), "pq")
+        cp(A("rq", t, V, 4), A("rn%d" % t))
+        again("r", ("rb", DUM), "rq")
+        for n in ("pa", "pb", "ra", "rb"):
+            o = 32 * "ab".index(n[1])
+            copy(GHOST[n], gh[n], ind(A(n[0] + "w" + n[1], 0, G5 + 128 * (t + 1)), A("lz%d" % t, o, o + 32)))
+
+    if "order" not in ORDER: ORDER["order"] = plan(nodes)
+    queues = {"V": g.vector, "S": g.scalar, "P": g.tensor, "G": g, "D": g.sync}
+    cnt = {"qV": 0, "qS": 0, "qP": 0, "qG": 0}
+    know, snap, done = {q: {} for q in queues}, {}, {}
+
+    def wait(q, sem, val):
+        if know[q].get(sem, 0) < val:
+            queues[q].wait_ge(T.sem[sem], val)
+            for k, v in snap.get((sem, val), {}).items():
+                if know[q].get(k, 0) < v: know[q][k] = v
+            know[q][sem] = val
+
+    for i in ORDER["order"]:
+        d = nodes[i]
+        q = d["q"]
+        if q == "R":
+            done[i] = d["sem"]; continue
+        need = {}
+        for j, s in d["deps"].items():
+            if s and need.get(done[j][0], 0) < done[j][1]: need[done[j][0]] = done[j][1]
+        for s in sorted(need): wait(q, s, need[s])
+        if d["sem"] is not None:
+            r = d["calls"][0]()
+            if q == "D": r.then_inc(T.sem[d["sem"][0]], 16)
+            done[i] = d["sem"]
+        else:
+            s = "q" + q
+            if d["grp"] is not None: d["grp"]["n"] -= 1
+            for k, f in enumerate(d["calls"]):
+                if q == "P": r = g.tensor.matmul(f[0], f[1], f[2], f[3], k == len(d["calls"]) - 1 and (d["grp"] is None or d["grp"]["n"] == 0))
+                else: r = f()
+                r.then_inc(T.sem[s], 1); cnt[s] += 1
+            done[i] = (s, cnt[s])
+        snap[done[i]] = dict(know[q])
+    for i, d in enumerate(nodes):
+        if d["q"] == "G" and d["sem"] is not None: wait("G", *d["sem"])
     for s in sorted(cnt): wait("G", s, cnt[s])
     for i in range(free["d"]): wait("D", "d%d" % i, 16)

@@ -6,12 +6,15 @@ DUM = 256
 PEN = 16384.0
 B10 = 10.0 * 2 ** 20
 MAGIC = 1.5 * 2 ** 23
-TESTS = {"P": "VVVVVVVV", "R": "VVVSVVSS"}
-TESTS0 = {"P": "VVVVVVVV", "R": "VVVVVVVS"}
-AGAIN = {"x": "S", "p": "S", "r": "S"}
-GHOST = {"pa": "S", "pb": "V", "ra": "S", "rb": "V"}
+TESTS = {"P": "VVVVVSVV", "R": "VVSSVSVV"}
+TESTS0 = {"P": "VVVVVVVV", "R": "VSVSVSVV"}
+DIST, DIST0 = "SSSS", "SSSS"
+AGAIN, GHOST, ODDK, DGT = "SVV", "SVSV", "VVVV", "V"
+COPIES = "VSSVV"
 PAIRS = "SVSVSVSVSVSVSVSV"
-CYC, GA, SC, HOP, SELF, LOOK, SWEEPS = 0.9e-3, 1.56, 3.8, 0.1, 0.05, 1.0, 4
+CYC, HOP, SELF = 0.92e-3, 0.1, 0.05
+RATES = ((1.56, 3.8), (1.1, 2.0), (2.0, 5.5))
+STEPS = (6.0, 3.0, 1.5, 3.0, 0.7)
 
 SCRATCH, PLACE, ORDER = {}, {}, {}
 SIZE = {"bfloat16": 2, "uint16": 2, "float32": 4, "int32": 4}
@@ -31,7 +34,7 @@ def _b(names, cols, dtype, where="sbuf"):
 
 
 _b("rb bw", DUM + 2 * V, "bfloat16")
-_b("pb xw rq pq xq", 2 * V, "bfloat16")
+_b("pb xw rq pq wmx", 2 * V, "bfloat16"); _b("xq", 3 * V, "bfloat16")
 _b("bs", V, "bfloat16")
 _b("ci si", V, "int32"); _b("cb sb", V, "float32")
 for _t in range(RO):
@@ -44,64 +47,92 @@ _b("idm ngm hm bgm nbm zm bom ltm s10 onm lh", 128, "bfloat16"); _b("idf b8 la0 
 _b("ic thr sg1", 256, "float32"); _b("ib", 256, "int32"); _b("id_ ie ig ih ij ik in_", 128, "int32")
 _b("pc", 8, "int32"); _b("cc", 40, "float32"); _b("g8", 8, "bfloat16"); _b("lw wv wx", 16, "float32")
 _b("pat", 224, "bfloat16"); _b("tc", 32, "bfloat16"); _b("ta", 32, "float32"); _b("pa pb_ pc_ dig dt dgt", 512, "bfloat16")
-_b("dg", 512, "bfloat16"); _b("kc cll clr mh", 256, "bfloat16"); _b("rs", 96, "bfloat16"); _b("one", 32, "float32")
-_b("o2 ofin omx kqu cu bcu", 16, "uint16"); _b("oke", 32, "uint16")
+_b("dg", 256, "bfloat16"); _b("junk", 4096, "bfloat16"); _b("kc cll clr mh", 256, "bfloat16"); _b("rs", 96, "bfloat16"); _b("one", 32, "float32")
+_b("o2 ofin omx kqu cu bcu", 16, "uint16")
 _b("in12 tr12", 512, "float32")
-_b("klo k8", 128, "float32"); _b("k4", 64, "float32"); _b("k2", 32, "float32"); _b("k1 has ask bc pen", 16, "float32"); _b("mk kq", 16, "int32")
-_b("cm cs sx cx cy", 256, "float32"); _b("bits fev fod fr junk we os xp r2", 256, "bfloat16"); _b("kl", 32, "int32"); _b("ke", 512, "bfloat16")
+_b("klo k8", 128, "float32"); _b("k4", 64, "float32"); _b("k2", 32, "float32"); _b("k1 has bc oh", 16, "float32"); _b("pen", 32, "float32"); _b("klf", 48, "float32"); _b("mk kq", 16, "int32")
+_b("cm cs sx cx cy", 256, "float32"); _b("bits fev fod fr we os xp r2", 256, "bfloat16"); _b("kl", 32, "int32"); _b("ke", 768, "bfloat16")
 _b("mx", 16, "float32"); _b("d3 t3", 48, "float32"); _b("l3", 48, "uint16"); _b("v3 vm", 192, "float32"); _b("la", 128, "uint16")
 _b("wn", 16, "bfloat16"); _b("mt", 2, "float32"); _b("mi", 2, "int32"); _b("thi", 8, "int32"); _b("thf", 8, "float32")
 _b("dr dp", 128, "bfloat16")
 _b("fvs flo flt dfl c96 gf", 32, "float32"); _b("e5 ge go chf ch scq", 32, "bfloat16"); _b("fu", 32, "uint16"); _b("flu", 64, "uint16")
 _b("p0 p1 p2 p3 p4 p5 p6 p7", 512, "float32", "psum")
-SEMAPHORES = ["qV", "qS", "qP", "qG", "inA", "inB"] + ["d%d" % i for i in range(28)] + ["ls%d" % i for i in range(12)] + \
+_b("gate", 8, "float32")
+SEMAPHORES = ["qV", "qS", "qP", "qG", "ipA", "ipB", "irA", "irB", "go"] + ["d%d" % i for i in range(28)] + ["ls%d" % i for i in range(12)] + \
     ["%s%s%d" % (a, s, t) for a in ("ar", "ap", "az") for s in "AB" for t in range(RO - 1)]
 
 
 def plan(nodes):
     n = len(nodes)
-    after = [[] for _ in nodes]
+    Q, lat = [d["q"] for d in nodes], [d["lat"] for d in nodes]
+    costs = [[d["cost"] + (ga * d["ga"] + sc * d["sc"]) * CYC for d in nodes] for ga, sc in RATES]
+    c = costs[0]
+    after, before = [[] for _ in nodes], [[] for _ in nodes]
     for i, d in enumerate(nodes):
-        for j in d["deps"]: after[j].append(i)
-    hop = lambda j, i: 0.0 if not nodes[i]["deps"][j] else SELF if nodes[j]["q"] == nodes[i]["q"] else HOP
-    far = [0.0] * n
+        for j, w in d["deps"].items():
+            h = -lat[j] if not w else SELF if Q[j] == Q[i] else HOP
+            after[j].append((i, h)); before[i].append((j, h))
+    base = [0.0] * n
     for i in range(n - 1, -1, -1):
         run, most = {}, 0.0
-        for k in sorted(after[i], key=lambda k: nodes[k]["cost"] - far[k]):
-            q = nodes[k]["q"]
-            most = max(most, run.get(q, 0.0) + far[k] + hop(i, k))
-            run[q] = run.get(q, 0.0) + nodes[k]["cost"]
-        far[i] = nodes[i]["cost"] + nodes[i]["lat"] + most
-    before = [list(d["deps"]) for d in nodes]
+        for k, h in sorted(after[i], key=lambda e: c[e[0]] - base[e[0]]):
+            most = max(most, run.get(Q[k], 0.0) + base[k] + h)
+            run[Q[k]] = run.get(Q[k], 0.0) + c[k]
+        base[i] = c[i] + lat[i] + most
 
-    def sweep(far, back):
-        pre, post = (after, before) if back else (before, after)
-        left = [len(p) for p in pre]
-        end, est, free, ready, order = [0.0] * n, [0.0] * n, {}, {}, []
+    def sweep(far):
+        left, est, free, ready, order, last = [len(p) for p in before], [0.0] * n, {}, {}, [], 0.0
         for i in range(n):
-            if back: est[i] = nodes[i]["lat"]
-            if not left[i]: ready.setdefault(nodes[i]["q"], []).append(i)
+            if not left[i]: ready.setdefault(Q[i], []).append(i)
         while len(order) < n:
-            t, q = min((max(free.get(q, 0.0), min(est[i] for i in r)), q) for q, r in ready.items() if r)
-            a = max((i for i in ready[q] if est[i] <= t), key=lambda i: (far[i], -i))
-            for b in ready[q]:
-                if t < est[b] < t + nodes[a]["cost"] and far[b] > far[a]:
-                    if max(est[b] + far[b], est[b] + nodes[b]["cost"] + far[a]) + LOOK * (est[b] - t) < max(t + nodes[a]["cost"] + far[b], t + far[a]):
-                        a, t = b, est[b]
-            ready[q].remove(a); order.append(a)
-            if q != "R": free[q] = t + nodes[a]["cost"]
-            end[a] = t + nodes[a]["cost"] + (0.0 if back else nodes[a]["lat"])
-            for k in post[a]:
-                est[k] = max(est[k], end[a] + (hop(k, a) + nodes[k]["lat"] if back else hop(a, k))); left[k] -= 1
-                if not left[k]: ready.setdefault(nodes[k]["q"], []).append(k)
-        return order, end
+            t, q = 1e9, None
+            for k, r in ready.items():
+                if r:
+                    x = max(free.get(k, 0.0), min([est[i] for i in r]))
+                    if x < t: t, q = x, k
+            r, a = ready[q], -1
+            for i in r:
+                if est[i] <= t and (a < 0 or far[i] > far[a]): a = i
+            for b in r:
+                if t < est[b] < t + c[a] and far[b] > far[a]:
+                    if max(est[b] + far[b], est[b] + c[b] + far[a]) + est[b] - t < max(t + c[a] + far[b], t + far[a]): a, t = b, est[b]
+            r.remove(a); order.append(a)
+            if q != "R": free[q] = t + c[a]
+            e = t + c[a] + lat[a]
+            last = max(last, e)
+            for k, h in after[a]:
+                if e + h > est[k]: est[k] = e + h
+                left[k] -= 1
+                if not left[k]: ready.setdefault(Q[k], []).append(k)
+        return order, last
 
-    best = None
-    for _ in range(SWEEPS):
-        order, end = sweep(far, False)
-        if best is None or max(end) < best[0]: best = (max(end), order)
-        far = sweep(end, True)[1]
-    return best[1]
+    def replay(order, cost):
+        end, free = [0.0] * n, {}
+        for i in order:
+            t = free.get(Q[i], 0.0)
+            for j, h in before[i]:
+                if end[j] + h > t: t = end[j] + h
+            if Q[i] != "R": free[Q[i]] = t + cost[i]
+            end[i] = t + cost[i] + lat[i]
+        return max(end)
+
+    def length(move):
+        order, last = sweep([f + move.get(d["kind"], 0.0) for f, d in zip(base, nodes)])
+        return last + sum(replay(order, k) for k in costs[1:]) / (len(costs) - 1), order
+
+    kinds = sorted(set(d["kind"] for d in nodes))
+    kinds = [k for k in kinds if sum(d["kind"] == k for d in nodes) >= 3]
+    move = {}
+    best, order = length(move)
+    for step in STEPS:
+        for k in kinds:
+            for d in (step, -step):
+                trial = dict(move); trial[k] = trial.get(k, 0.0) + d
+                e, o = length(trial)
+                if e < best - 0.02:
+                    best, order, move = e, o, trial
+                    break
+    return order
 
 
 def rank_program(g, core, T, topo):
@@ -137,17 +168,21 @@ def rank_program(g, core, T, topo):
                 h[:] = keep + [(0, 512, w or any(e[2] for e in h if e[3] == me), me)]
             else:
                 for e in h:
-                    if e[3] != me and (w or e[2]) and x["a"] < e[1] and e[0] < x["b"]: deps[e[3]] = True
+                    if e[3] != me and (w or e[2]) and x["a"] < e[1] and e[0] < x["b"]:
+                        k = min(x["s"], e[4])
+                        if k == 1 or (x["a"] - e[0]) % k == 0 or q not in "VSP" or nodes[e[3]]["q"] not in "VSP": deps[e[3]] = True
         for x, w in acc:
             if not x["ps"]:
                 h = hist[x["n"]]
-                if w and x["s"] == 1: h[:] = [e for e in h if not (x["a"] <= e[0] and e[1] <= x["b"])]
-                h.append((x["a"], x["b"], w, me))
-        nodes.append({"q": q, "calls": calls, "cost": cost, "lat": lat, "deps": deps, "sem": sem, "grp": grp})
+                if w: h[:] = [e for e in h if not (x["a"] <= e[0] and e[1] <= x["b"] and e[4] % x["s"] == 0 and (x["a"] - e[0]) % x["s"] == 0)]
+                h.append((x["a"], x["b"], w, me, x["s"]))
+        nodes.append({"q": q, "calls": calls, "cost": cost, "lat": lat, "deps": deps, "sem": sem, "grp": grp, "ga": 0, "sc": 0,
+                      "kind": q + "".join(" " + x["n"].rstrip("0123456789") for x in writes[:1] + reads[:2])})
+        if isinstance(cost, tuple): nodes[-1].update({"cost": cost[0], cost[1]: cost[2]})
         return me
 
     def price(q, out, in_, rate):
-        if "o" in in_: return 0.06 + 16 * in_["o"]["k"] * GA * CYC
+        if "o" in in_: return (0.06, "ga", 16 * in_["o"]["k"])
         return max(64, in_["k"] * rate) * CYC
     def half(*x): return 0.5 if all(i["w"] == 2 for i in x) else 1.0
     def ind(win, off): return {"ap": win["ap"].indirect(off["ap"]), "win": win, "o": off, "w": win["w"], "ps": False}
@@ -155,7 +190,7 @@ def rank_program(g, core, T, topo):
     def ap(x): return x["ap"] if isinstance(x, dict) else x
     def cols(*x): return [i for i in x if isinstance(i, dict)]
     def cp(out, in_): node("V", [lambda: g.vector.tensor_copy(out["ap"], in_["ap"])], price("V", out, in_, half(out, in_)), [out], rd(in_))
-    def scat(win, off, in_): node("V", [lambda: g.vector.tensor_copy(win["ap"].indirect(off["ap"]), in_["ap"])], 0.05 + in_["k"] * SC * CYC, [win], [off, in_])
+    def scat(win, off, in_): node("V", [lambda: g.vector.tensor_copy(win["ap"].indirect(off["ap"]), in_["ap"])], (0.05, "sc", in_["k"]), [win], [off, in_])
     def tt(out, a, b, op):
         rate = 1.0 if a["ps"] or b["ps"] else 2.0 * half(out, a, b)
         node("V", [lambda: g.vector.tensor_tensor(out["ap"], a["ap"], b["ap"], op)], price("V", out, a, rate), [out], rd(a) + [b])
@@ -181,6 +216,9 @@ def rank_program(g, core, T, topo):
         calls = [(o["ap"], l["ap"], r["ap"], first and i == 0) for i, (o, l, r) in enumerate(parts)]
         cost = sum(max(64, r["k"]) * (4 if r["w"] == 4 else 1) * CYC / 2 for o, l, r in parts)
         node("P", calls, cost, [parts[0][0]], [x for o, l, r in parts for x in (l, r)], grp=grp)
+    def parts(all_, k, grp=None):
+        grp = {} if grp is None else grp
+        for i in range(0, len(all_), k): mms(all_[i:i + k], grp)
     def iota(out, pat, base=0, cm=0):
         if out["w"] == 4 and PLACE[out["n"]][0].endswith("int32"): f = lambda: g.iota(out["ap"], pat, base, cm)
         else: f = lambda: g.iota(out["ap"], pat, base, cm, allow_small_or_imprecise_dtypes=True)
@@ -188,7 +226,7 @@ def rank_program(g, core, T, topo):
     def dma(out, in_, reads, writes, kb, q="D"):
         s = "d%d" % free["d"]; free["d"] += 1
         f = g.sync if q == "D" else g.scalar
-        node("D", [lambda: f.dma_start(out, in_)], kb / 200.0, writes, reads, lat=2.0, sem=(s, 16))
+        free["last"] = [node("D", [lambda: f.dma_start(out, in_)], kb / 200.0, writes, reads, lat=2.0, sem=(s, 16), extra=free.get("last", ()))]
 
     def sides(c):
         r = T.rank_of(c)
@@ -203,7 +241,7 @@ def rank_program(g, core, T, topo):
         return out
     NE = min(len(e) for c_ in T.cores for _, e in sides(c_))
 
-    def send(pairs, sem, us):
+    def send(pairs, sem, us, once=0.0):
         s = "ls%d" % free["ls"]; free["ls"] += 1
         n, tr = NE // len(pairs), []
         for side, (d, e) in zip("AB", sides(core)):
@@ -211,19 +249,23 @@ def rank_program(g, core, T, topo):
             for i, p in enumerate(pairs):
                 tr.append(RemoteDMATransfer(dst_ids=[DstId(rid=rid, pnc=pid)], dma_engine_mask=sum(1 << k for k in e[i * n:i * n + n]),
                                             remote_sem=T.sem[sem % side], src=p[0]["ap"], dst=p[1 if side == "A" else 2]["ap"]))
-        me = node("G", [lambda: g.remote_dma_fused(tr, local_sem=T.sem[s])], 1.0, [], [p[0] for p in pairs], lat=1.0, sem=(s, n * len(tr)))
-        for i, side in enumerate("AB"): node("R", [], 0.0, [p[1 + i] for p in pairs], [], lat=us, sem=(sem % side, n * len(pairs)), extra=[me])
+        me = node("G", [lambda: g.remote_dma_fused(tr, local_sem=T.sem[s])], 1.0 + once, [], [p[0] for p in pairs], lat=1.0, sem=(s, n * len(tr)))
+        for i, side in enumerate("AB"): node("R", [], 0.0, [p[1 + i] for p in pairs], [], lat=us + 1.0, sem=(sem % side, n * len(pairs)), extra=[me])
+        return me
 
     def load(name, a, src, c0=0, c1=V, kb=256): dma(A(name, a + c0, a + c1)["ap"], src[:, c0:c1], [], [A(name, a + c0, a + c1)], kb * (c1 - c0) / V)
-    load("rb", DUM, T.reach, 0, G5); load("pb", 0, T.past, 0, G5)
-    load("ci", 0, T.cand, kb=512); load("xw", 0, T.x); load("xq", V, T.x)
+    load("pb", 0, T.past, 0, G5); load("rb", DUM, T.reach, 0, G5)
+    load("ci", 0, T.cand, kb=512); load("xw", 0, T.x)
     load("rb", DUM, T.reach, G5, V); load("pb", 0, T.past, G5, V)
-    for o in (0, V): load("rq", o, T.reach)
-    for o in (0, V): load("pq", o, T.past)
-    load("si", 0, T.succ, kb=512); load("xq", 0, T.x)
     dma(A("thi", 0, 1, p1=8)["ap"], T.th[:], [], [A("thi")], 1)
     gh = {"ra": A("rb", DUM + V, DUM + V + G5), "rb": A("rb", DUM + V + G5, DUM + 2 * V), "pa": A("pb", V, V + G5), "pb": A("pb", V + G5, 2 * V)}
-    send([(A("rb", DUM, DUM + G5), gh["ra"], gh["rb"]), (A("pb", 0, G5), gh["pa"], gh["pb"])], "in%s", 5.0)
+    send([(A("pb", 0, G5), gh["pa"], gh["pb"])], "ip%s", 2.5, 2.0)
+    sent = send([(A("rb", DUM, DUM + G5), gh["ra"], gh["rb"])], "ir%s", 2.5)
+    node("G", [lambda: g.sem_inc(T.sem["go"], 1)], 0.05, [A("gate")], [], sem=("go", 1), extra=[sent])
+    dma(A("si")["ap"], T.succ[:], [A("gate")], [A("si")], 512)
+    dma(A("xq", 0, V)["ap"], T.x[:], [A("gate")], [A("xq", 0, V)], 256)
+    for who, (n, o, w) in zip(COPIES, (("xq", V, A("xw", 0, V)), ("rq", 0, A("rb", DUM, DUM + V)), ("rq", V, A("rb", DUM, DUM + V)),
+                                       ("pq", 0, A("pb", 0, V)), ("pq", V, A("pb", 0, V)))): copy(who, A(n, o, o + V), w)
     for n in ("pa", "pb", "ra", "rb"):
         w = A(n[0] + "w" + n[1], 0, G5)
         dma(w["ap"], gh[n]["ap"], [gh[n]], [w], 128)
@@ -236,9 +278,9 @@ def rank_program(g, core, T, topo):
     iota(A("id_", 0, 16), [[32, 8], [-16, 2]], 16, 1); iota(A("id_", 16, 32), [[1, 16]])
     iota(A("ie"), [[1, 128]]); iota(A("ig", 0, 8), [[1, 8]]); iota(A("ik"), [[1, 8], [0, 16]])
     iota(A("ib"), [[0, 16], [1, 16]]); iota(A("ic"), [[1, 256]])
-    iota(A("ih", 0, 16), [[1, 2], [2, 8]]); iota(A("ih", 16, 48), [[1, 32]])
+    iota(A("ih", 0, 16), [[1, 2], [2, 8]])
     iota(A("ij", 16, 32), [[16, 16]], 0, 1); iota(A("in_", 0, 96), [[-8, 2], [0, 3], [1, 16]]); iota(A("id_", 32, 64), [[16, 32]], 0, 1)
-    fill(A("xw", V, 2 * V), PEN); fill(A("rb", 0, DUM), 0.0); fill(A("bw", 0, DUM), 0.0); fill(A("bw", DUM + V, DUM + 2 * V), 0.0)
+    fill(A("xw", V, 2 * V), PEN); fill(A("rb", 0, DUM), 0.0); fill(A("bw", 0, DUM), 0.0); fill(A("bw", DUM + V, DUM + 2 * V), 1.0)
     ts(rw, pp, 15, O.bitwise_and)
     ts(A("pc", 2, 3), pp, 4, O.arith_shift_right)
     ts(A("pc", 3, 4), pp, 4, O.arith_shift_right, 1, O.bitwise_and)
@@ -264,7 +306,7 @@ def rank_program(g, core, T, topo):
     ts(A("kc"), A("ic"), 2.0 ** -20, O.mult)
     fill(A("smx"), 0.0); fill(A("smx", 0, 1024, 8), 255.0)
     fill(A("sg1"), 1.0); fill(A("sg1", 0, 256, 16), 0.0); fill(A("mh"), -0.5)
-    ts(A("dg", 0, 256), A("ib"), c(ROW), O.is_equal); act(A("dg", 256, 512), A("dg", 0, 256))
+    ts(A("dg", 0, 256), A("ib"), c(ROW), O.is_equal)
     ts(c(L10), c(ROW), 10.0, O.is_lt); ts(c(C1L), c(ROW), 13.0, O.is_ge); ts(c(E12), c(ROW), 12.0, O.is_equal); ts(c(E15), c(ROW), 15.0, O.is_equal)
     ts(c(W4), c(ROW), 13.0, O.is_lt, c(L10), O.subtract); cp(c(C1R), c(W4))
     ts(c(M2), c(C1R), c(E12), O.subtract)
@@ -273,6 +315,9 @@ def rank_program(g, core, T, topo):
     act(A("cll"), A("ic"), AF.Identity, bias=c(C1L), scale=c(E12)); act(A("clr"), A("ic"), AF.Identity, bias=c(C1R), scale=c(E15))
     act(A("s10"), A("idm"), scale=c(L10))
     ts(A("wm2"), A("wm"), c(M2), O.mult)
+    if "V" in DIST + DIST0:
+        ts(A("wmx"), A("wm"), -2.0 ** -12, O.mult)
+        dma(A("xq", 2 * V, 3 * V)["ap"], T.x[:], [A("gate")], [A("xq", 2 * V, 3 * V)], 256)
     ts(A("bom"), A("ik"), c(P16), O.is_equal)
     ts(A("lw"), A("dg", 0, 16), 1024.0, O.mult)
     for m in range(16): act(W("wt", m), A("bom"), scale=A("lw", m, m + 1))
@@ -295,7 +340,7 @@ def rank_program(g, core, T, topo):
         ts(c(CA + par), c(NG), -1.0, O.mult, c(W0), O.add)
         if par: ts(c(CA + par), c(CA + par), 8.0, O.add)
         ts(A("la%d" % par), A("ie"), c(CA + par), O.is_equal, c(ODD), O.mult); ts(A("lb_%d" % par), A("ie"), c(CA + par), O.is_equal, c(EVR), O.mult)
-    cp(A("oke"), A("ih", 16, 48)); cp(A("omx"), A("ih", 0, 16))
+    cp(A("oh"), A("dg", 0, 16)); fill(A("pen"), 0.0); cp(A("omx"), A("ih", 0, 16))
     for a in range(16):
         o = 128 * (a % 2) + 16 * (a // 2)
         if a == 0: ts(A("thr"), A("dg", 0, 256), 1e9 + 0.5, O.mult, -1e9, O.add)
@@ -330,9 +375,9 @@ def rank_program(g, core, T, topo):
         mms([(A("p6", 0, 128), A("lb_%d" % par), A("sb", t + 4 * par, V, 8)) for par in range(2)])
         cp(A("lb%d" % t), A("p6", 0, 128))
 
-    def squeeze(n, i, w):
+    def squeeze(n, i, w, by="wm"):
         p, o = "p%d" % (4 + i // 4), 32 * (i % 4)
-        mms([(A(p, o, o + 32 * w), W("wm", m), A(n, 512 * i + m, 512 * (i + w), 16)) for m in range(16)], key[p])
+        parts([(A(p, o, o + 32 * w), W(by, m), A(n, 512 * i + m, 512 * (i + w), 16)) for m in range(16)], 8, key[p])
 
     def distances(t):
         for h in range(2):
@@ -341,6 +386,11 @@ def rank_program(g, core, T, topo):
         mine = A("xq", V + t, 2 * V, 4)
         for h in range(8):
             p, x = "p%d" % (h % 2), A("xg", 512 * h, 512 * h + 512)
+            if (DIST if t else DIST0)[h // 2] == "V":
+                tt(x, ind(A("xw"), A("ct%d" % t, 32 * h, 32 * h + 32)), A("xq", V + t, 3 * V, 4), O.subtract)
+                ts(A("ad", 512 * h, 512 * h + 512), x, 0.0, O.max, 2.0 ** -11, O.mult)
+                if h % 2: squeeze("xg", h - 1, 2, "wmx"); squeeze("ad", h - 1, 2)
+                continue
             act(x, ind(A("xw"), A("ct%d" % t, 32 * h, 32 * h + 32)))
             mms([(A(p), A("idm"), x), (A(p, 0, 256), A("ngm"), mine), (A(p, 256, 512), A("ngm"), mine)])
             act(A("ad", 512 * h, 512 * h + 512), A(p), AF.Abs, scale=2.0 ** -12)
@@ -359,7 +409,7 @@ def rank_program(g, core, T, topo):
                         act(x, ind(win, off))
                         mms([(A(p), A("idm"), x), (A(p), A("ngm"), mine)])
                         act(out, A(p), AF.Relu, bias=1.0, scale=1.0 if kind == "P" else -1.0)
-                    if lo and h >= 6: squeeze(n, h, 1)
+                    if h >= 6 and kind == "R": squeeze(n, h, 1)
                     elif h % 2: squeeze(n, h - 1, 2)
 
     sl, xl, sc = A("l3", 0, 16), A("l3", 16, 32), A("l3", 32, 48)
@@ -373,23 +423,23 @@ def rank_program(g, core, T, topo):
         tt(A("cm"), ind(A("ca%d" % t), A("kqu")), A("dg", 0, 256), O.mult)
         scan(A("cs"), A("sg1"), A("cm"), 0.0, O.mult, O.add)
         cp(A("cu"), A("cs", 15, 256, 16))
-        act(A("bits"), ind(A("bw", DUM), A("cu")))
+        cp(A("bits"), ind(A("bw", DUM), A("cu")))
         ts(A("kl", 0, 16), A("mk"), 14, O.arith_shift_right, 63, O.bitwise_and)
-        ts(A("pen"), A("mk"), c(LIM), O.is_ge, 128.0, O.mult)
         ts(A("kl", 16, 32), A("mk"), 8, O.arith_shift_right, 63, O.bitwise_and)
-        tt(A("kl", 0, 16), A("kl", 0, 16), A("pen"), O.add)
-        tt(A("ke"), ind(A("kl"), A("oke")), A("dg"), O.mult)
+        ts(A("pen", 0, 16), A("mk"), c(LIM), O.is_ge, 128.0, O.mult)
+        tt(A("klf", 0, 32), A("kl"), A("pen"), O.add)
+        ts(A("klf", 32, 48), A("mk"), c(LIM), O.is_ge, 4096.0, O.mult)
+        for m in range(16): act(A("ke", m, 768, 16), A("klf"), scale=A("oh", m, m + 1))
         for p, cl, r in (("p5", "clr", 13), ("p4", "cll", 10)):
             grp, o = {}, A(p, 0, 256)
             mms([(o, A("idm"), A(cl))], grp); mms([(o, A("s10"), A("bits"))], grp)
-            mms([(o, W("wm", r), A("ke", 0, 256)), (o, W("wm", r + 1), A("ke", 256, 512))], grp)
+            mms([(o, W("wm", r), A("ke", 0, 256)), (o, W("wm", r + 1), A("ke", 256, 512))] + [(o, W("wm", 12), A("ke", 512, 768))][:r == 10], grp)
         ts(A("fr"), A("p5", 0, 256), c(RS), O.mult)
         act(A("fev"), A("p4", 0, 256), scale=c(RG0)); act(A("fod"), A("p4", 0, 256), scale=c(RG1))
-        mms([(A("p7", 0, 16), W("wm2", m), A("bits", m, 256, 16)) for m in range(16)])
+        parts([(A("p7", 0, 16), W("wm2", m), A("bits", m, 256, 16)) for m in range(16)], 4)
         for i in range(3): tt(A("d3", 16 * i, 16 * i + 16), A("p7", 0, 16), A("vm", 48 * t + 16 * i, 48 * t + 16 * i + 16), O.subtract)
-        ts(A("ask"), A("mk"), c(LIM), O.is_lt); ts(A("has"), A("mk"), 2.0 ** 20, O.is_lt)
+        ts(A("has"), A("mk"), 2.0 ** 20, O.is_lt)
         tt(A("bc"), A("d3", 0, 16), A("has"), O.mult); tt(A("bc"), A("bc"), A("v3", 48 * t, 48 * t + 16), O.add); cp(A("bcu"), A("bc"))
-        for i in range(3): tt(A("d3", 16 * i, 16 * i + 16), A("d3", 16 * i, 16 * i + 16), A("ask"), O.mult)
         seen = {"V": 0, "S": 0}
         for a in range(16):
             gr, h, who = a // 2, a % 2, PAIRS[a]
@@ -398,11 +448,11 @@ def rank_program(g, core, T, topo):
             lo = 32 * (gr // 2)
             mms([(A(p, 0, 256), A("fod" if gr % 2 else "fev", 128 * h, 128 * h + 128, p0=lo, p1=lo + 32), A("fr", p0=lo, p1=lo + 32))])
             if who == "V": reduce(A("mx", a, a + 1), A(p, 0, 256), O.max)
-            else: act(A("junk"), A(p, 0, 256), AF.Relu, bias=-B10, acc=A("mx", a, a + 1))
+            else: act(A("junk", 256 * a, 256 * a + 256), A(p, 0, 256), AF.Relu, bias=-B10, acc=A("mx", a, a + 1))
         tt(A("we"), ind(A("mx"), A("omx")), A("thr"), O.is_le)
         mms([(A("p7", 64, 112), A("we", 128 * h, 128 * h + 128), A("rs", 48 * h, 48 * h + 48)) for h in range(2)])
         tt(A("t3"), A("p7", 64, 112), A("d3"), O.mult)
-        if t + 1 < RO: tt(A("wn"), A("p7", 64, 80), A("ask"), O.mult)
+        if t + 1 < RO: cp(A("wn"), A("p7", 64, 80))
         tt(A("t3"), A("t3"), A("v3", 48 * t, 48 * t + 48), O.add)
         cp(A("l3"), A("t3"))
 
@@ -411,8 +461,8 @@ def rank_program(g, core, T, topo):
         tt(A("r2"), ind(A("rq", 0, V), sl), A("rq", V + t, 2 * V, 4), O.min)
         act(A("sx"), ind(A("sb"), sl))
         scat(A("rb", 0, DUM + V), sc, A("r2"))
-        mms([(A("p6", 0, 256), W("wt", 12), A("bw", DUM + t, DUM + V, 4))], grp); mms([(A("p6", 0, 256), A("idm"), A("r2"))], grp)
-        tt(w, w, A("p6", 0, 256), O.min)
+        mms([(A("p2", 0, 256), W("wt", 12), A("bw", DUM + t, DUM + V, 4))], grp); mms([(A("p2", 0, 256), A("idm"), A("r2"))], grp)
+        tt(w, w, A("p2", 0, 256), O.min)
         mms([(A("p5", 0, 128), A("la%d" % par), A("sx", par, 256, 2)) for par in range(2)])
         cp(A("la"), A("p5", 0, 128))
 
@@ -441,8 +491,8 @@ def rank_program(g, core, T, topo):
         tt(A("dp"), A("pn%d" % t, 0, 128), A("pq", V + t, V + G5, 4), O.not_equal)
 
     def xmerge(t):
-        grp, o = {}, A("p6", 256, 512)
-        act(A("xp"), ind(A("xq"), xl))
+        grp, o = {}, A("p3", 0, 256)
+        act(A("xp"), ind(A("xq", 0, 2 * V), xl))
         mms([(o, A("hm"), A("xq", V + t, 2 * V, 4)), (o, A("hm"), A("mh"))], grp); mms([(o, A("hm"), A("xp"))], grp)
         ts(A("xq", t, V, 4), o, MAGIC, O.add, MAGIC, O.subtract)
 
@@ -472,7 +522,7 @@ def rank_program(g, core, T, topo):
         mms([(A("p6", m, G5, 16), W("wt", m), A("go")) for m in rows], grp)
         tt(A("dt"), A("p6"), A("dig"), O.min)
         tt(A("gf"), A("go"), A("dfl"), O.mult); tt(A("fvs"), A("fvs"), A("gf"), O.add); cp(A("fu"), A("fvs"))
-        cp(A("dgt"), ind(A("dt"), A("fu")))
+        copy(DGT, A("dgt"), ind(A("dt"), A("fu")))
         grp, o = {}, A("p7", 384, 416)
         mms([(o, A("idf"), A("fvs"))], grp); mms([(o, W("wm", m), A("dgt", m, G5, 16)) for m in range(16)], grp)
         cp(A("z%d" % t), o)
@@ -483,15 +533,15 @@ def rank_program(g, core, T, topo):
     def candidates(t):
         grp, own = {}, A("cb", t, V, 4)
         for n in ("tp", "tr"):
-            for k0 in (0, 8): mms([(A("p2", 0, 256), W("wm", k), A(n, 256 * k, 256 * k + 256)) for k in range(k0, k0 + 8)], grp)
-        act(A("os"), A("p2", 0, 256), AF.Sign)
+            parts([(A("p6", 0, 256), W("wm", k), A(n, 256 * k, 256 * k + 256)) for k in range(16)], 2, grp)
+        act(A("os"), A("p6", 0, 256), AF.Sign)
         act(A("cx"), ind(A("cb"), A("bcu")))
-        for o, m in ((0, "bgm"), (256, "nbm")): mms([(A("p3", o, o + 256), A("idf"), own), (A("p3", o, o + 256), A(m), A("os"))])
-        tt(A("cy"), A("p3", 0, 256), A("cx"), O.min)
-        tt(own, A("p3", 256, 512), A("cy"), O.max)
+        for o, m in ((0, "bgm"), (256, "nbm")): mms([(A("p6", o, o + 256), A("idf"), own), (A("p6", o, o + 256), A(m), A("os"))])
+        tt(A("cy"), A("p6", 0, 256), A("cx"), O.min)
+        tt(own, A("p6", 256, 512), A("cy"), O.max)
 
     def again(n, out, raw):
-        for h in range(2): copy(AGAIN[n], A(out[0], out[1] + G5 * h, out[1] + G5 * h + G5), ind(A(raw, 0, V), A("flu", 32 * h, 32 * h + 32)))
+        for h in range(2): copy(AGAIN["xpr".index(n)], A(out[0], out[1] + G5 * h, out[1] + G5 * h + G5), ind(A(raw, 0, V), A("flu", 32 * h, 32 * h + 32)))
 
     turn(0)
     fill(A("xw", 0, V, 4), PEN)
@@ -500,16 +550,17 @@ def rank_program(g, core, T, topo):
     for t in range(RO):
         last = t == RO - 1
         tests(t)
-        if not last: turn(t + 1)
+        if not last:
+            turn(t + 1); even_list(t + 1)
         partner(t)
+        candidates(t)
         merge(t)
         if not last:
             names(t); pmerge(t)
         xmerge(t)
         if last:
-            dma(T.yx[:], A("xq", 0, V)["ap"], [A("xq", 0, V)], [], 256)
-            candidates(t)
             dma(T.yc[:], A("cb")["ap"], [A("cb")], [], 512)
+            dma(T.yx[:], A("xq", 0, V)["ap"], [A("xq", 0, V)], [], 256)
             for h in range(2):
                 successors(t, h)
                 o = G5 * h
@@ -517,22 +568,20 @@ def rank_program(g, core, T, topo):
                 dma(T.yr[:, o:o + G5], A("rq", o, o + G5)["ap"], [A("rq", o, o + G5)], [], 128)
             continue
         act(A("sb", t, V, 4), A("sx"))
-        even_list(t + 1)
         successors(t, 0)
         block("r", t)
         publish(t)
         count()
         successors(t, 1)
-        candidates(t)
         fill(A("xq", t + 1, V, 4), PEN)
         again("x", ("xw", 0), "xq")
         distances(t + 1)
         again("p", ("pb", 0), "pq")
         cp(A("rq", t, V, 4), A("rn%d" % t))
         again("r", ("rb", DUM), "rq")
-        for n in ("pa", "pb", "ra", "rb"):
+        for who, n in zip(GHOST, ("pa", "pb", "ra", "rb")):
             o = 32 * "ab".index(n[1])
-            copy(GHOST[n], gh[n], ind(A(n[0] + "w" + n[1], 0, G5 + 128 * (t + 1)), A("lz%d" % t, o, o + 32)))
+            copy(who, gh[n], ind(A(n[0] + "w" + n[1], 0, G5 + 128 * (t + 1)), A("lz%d" % t, o, o + 32)))
 
     if "order" not in ORDER: ORDER["order"] = plan(nodes)
     queues = {"V": g.vector, "S": g.scalar, "P": g.tensor, "G": g, "D": g.sync}

@@ -2,19 +2,21 @@ from concourse.bass import DstId, RemoteDMATransfer
 from concourse.mybir import AluOpType, AxisListType, ActivationFunctionType as AF
 
 V, G5, RO, CAP = 1024, 512, 4, 96
-DUM = 256
+DUM, WID = 0, 2304
 PEN = 16384.0
 B10 = 10.0 * 2 ** 20
 MAGIC = 1.5 * 2 ** 23
+XW = 2
 TESTS = {"P": "VVVVVSVV", "R": "VVSSVSVV"}
 TESTS0 = {"P": "VVVVVVVV", "R": "VSVSVSVV"}
 DIST, DIST0 = "SSSS", "SSSS"
-AGAIN, GHOST, ODDK, DGT = "SVV", "SVSV", "VVVV", "V"
-COPIES = "VSSVV"
-PAIRS = "SVSVSVSVSVSVSVSV"
-CYC, HOP, SELF = 0.92e-3, 0.1, 0.05
-RATES = ((1.56, 3.8), (1.1, 2.0), (2.0, 5.5))
-STEPS = (6.0, 3.0, 1.5, 3.0, 0.7)
+AGAIN, GHOST, ODDK, DGT = "SXX", "SVSV", "VVVV", "V"
+COPIES = "VVVVV"
+PAIRS = "VVVVSSSSVVVVSSSS"
+CYC, HOP, SELF = 0.83e-3, 0.22, 0.11
+CALL = {"V": 0.01, "S": 0.03, "P": 0.004}
+RATES = ((1.56, 3.8, 1.0), (1.15, 2.2, 1.3), (2.0, 5.4, 1.3))
+TRIES, SLACK = 4500, 0.25
 
 SCRATCH, PLACE, ORDER = {}, {}, {}
 SIZE = {"bfloat16": 2, "uint16": 2, "float32": 4, "int32": 4}
@@ -33,26 +35,26 @@ def _b(names, cols, dtype, where="sbuf"):
             PLACE[name] = (name, 0, cols)
 
 
-_b("rb bw", DUM + 2 * V, "bfloat16")
-_b("pb xw rq pq wmx", 2 * V, "bfloat16"); _b("xq", 3 * V, "bfloat16")
-_b("bs", V, "bfloat16")
-_b("ci si", V, "int32"); _b("cb sb", V, "float32")
+_b("rb pb xw bw", WID, "bfloat16"); _b("nw", 128, "bfloat16")
+_b("rq pq wmx", 2 * V, "bfloat16"); _b("xq", 3 * V, "bfloat16")
+_b("bs p0_", V, "bfloat16")
+_b("ci si", V, "int32"); _b("cb sb", 2 * V, "float32")
 for _t in range(RO):
     _b("ct%d" % _t, 256, "uint16"); _b("ca%d" % _t, 256, "float32"); _b("lb%d" % _t, 128, "uint16")
     _b("rn%d pn%d" % (_t, _t), 256, "bfloat16"); _b("z%d" % _t, 32, "uint16"); _b("lz%d" % _t, 64, "uint16")
 _b("xg ad tp tr gp", 4096, "bfloat16"); _b("sga sgb sc", 2048, "bfloat16")
 _b("rwa rwb pwa pwb", 896, "bfloat16")
-_b("wm wm2 wt", 2048, "bfloat16"); _b("smx", 1024, "bfloat16")
+_b("wm wm2 wmn wt", 2048, "bfloat16"); _b("smx", 1024, "bfloat16")
 _b("idm ngm hm bgm nbm zm bom ltm s10 onm lh", 128, "bfloat16"); _b("idf b8 la0 la1 lb_0 lb_1", 128, "float32")
 _b("ic thr sg1", 256, "float32"); _b("ib", 256, "int32"); _b("id_ ie ig ih ij ik in_", 128, "int32")
 _b("pc", 8, "int32"); _b("cc", 40, "float32"); _b("g8", 8, "bfloat16"); _b("lw wv wx", 16, "float32")
 _b("pat", 224, "bfloat16"); _b("tc", 32, "bfloat16"); _b("ta", 32, "float32"); _b("pa pb_ pc_ dig dt dgt", 512, "bfloat16")
-_b("dg", 256, "bfloat16"); _b("junk", 4096, "bfloat16"); _b("kc cll clr mh", 256, "bfloat16"); _b("rs", 96, "bfloat16"); _b("one", 32, "float32")
+_b("dg", 256, "bfloat16"); _b("junk", 4096, "bfloat16"); _b("kc cll clr mh", 256, "bfloat16"); _b("rs", 32, "bfloat16"); _b("nh", 16, "bfloat16"); _b("r2s rbv", 256, "bfloat16"); _b("one", 32, "float32")
 _b("o2 ofin omx kqu cu bcu", 16, "uint16")
 _b("in12 tr12", 512, "float32")
-_b("klo k8", 128, "float32"); _b("k4", 64, "float32"); _b("k2", 32, "float32"); _b("k1 has bc oh", 16, "float32"); _b("pen", 32, "float32"); _b("klf", 48, "float32"); _b("mk kq", 16, "int32")
+_b("klo k8", 128, "float32"); _b("k4", 64, "float32"); _b("k2", 32, "float32"); _b("k1 bc oh vd", 16, "float32"); _b("pen klf", 32, "float32"); _b("mk kq", 16, "int32")
 _b("cm cs sx cx cy", 256, "float32"); _b("bits fev fod fr we os xp r2", 256, "bfloat16"); _b("kl", 32, "int32"); _b("ke", 768, "bfloat16")
-_b("mx", 16, "float32"); _b("d3 t3", 48, "float32"); _b("l3", 48, "uint16"); _b("v3 vm", 192, "float32"); _b("la", 128, "uint16")
+_b("mx", 16, "float32"); _b("t3", 32, "float32"); _b("l3", 32, "uint16"); _b("vs", 64, "float32"); _b("la", 128, "uint16")
 _b("wn", 16, "bfloat16"); _b("mt", 2, "float32"); _b("mi", 2, "int32"); _b("thi", 8, "int32"); _b("thf", 8, "float32")
 _b("dr dp", 128, "bfloat16")
 _b("fvs flo flt dfl c96 gf", 32, "float32"); _b("e5 ge go chf ch scq", 32, "bfloat16"); _b("fu", 32, "uint16"); _b("flu", 64, "uint16")
@@ -65,7 +67,8 @@ SEMAPHORES = ["qV", "qS", "qP", "qG", "ipA", "ipB", "irA", "irB", "go"] + ["d%d"
 def plan(nodes):
     n = len(nodes)
     Q, lat = [d["q"] for d in nodes], [d["lat"] for d in nodes]
-    costs = [[d["cost"] + (ga * d["ga"] + sc * d["sc"]) * CYC for d in nodes] for ga, sc in RATES]
+    costs = [[(f if d["q"] in CALL else 1.0) * (d["cost"] + (ga * d["ga"] + sc * d["sc"]) * CYC) + (0.0 if d["ga"] or d["sc"] else CALL.get(d["q"], 0.0) * len(d["calls"]))
+              for d in nodes] for ga, sc, f in RATES]
     c = costs[0]
     after, before = [[] for _ in nodes], [[] for _ in nodes]
     for i, d in enumerate(nodes):
@@ -120,19 +123,43 @@ def plan(nodes):
         order, last = sweep([f + move.get(d["kind"], 0.0) for f, d in zip(base, nodes)])
         return last + sum(replay(order, k) for k in costs[1:]) / (len(costs) - 1), order
 
-    kinds = sorted(set(d["kind"] for d in nodes))
-    kinds = [k for k in kinds if sum(d["kind"] == k for d in nodes) >= 3]
-    move = {}
-    best, order = length(move)
-    for step in STEPS:
-        for k in kinds:
-            for d in (step, -step):
-                trial = dict(move); trial[k] = trial.get(k, 0.0) + d
-                e, o = length(trial)
-                if e < best - 0.02:
-                    best, order, move = e, o, trial
-                    break
-    return order
+    def holdups(order, cost):
+        end, free, why, ran, was = [0.0] * n, {}, [-1] * n, {}, [0.0] * n
+        for i in order:
+            t, w = 0.0, -1
+            for j, h in before[i]:
+                if end[j] + h > t: t, w = end[j] + h, j
+            was[i] = t
+            if free.get(Q[i], 0.0) > t: t, w = free[Q[i]], ran[Q[i]][-1]
+            if Q[i] != "R": free[Q[i]] = t + cost[i]; ran.setdefault(Q[i], []).append(i)
+            end[i], why[i] = t + cost[i] + lat[i], w
+        i, pairs = max(range(n), key=lambda k: end[k]), {}
+        while i >= 0:
+            for j, h in [(i, 0)] + before[i]:
+                r = ran.get(Q[j], [])
+                k = r.index(j) - 1 if r else -1
+                while k >= 0 and end[r[k]] - lat[r[k]] > was[j] + 0.05:
+                    if kind[r[k]] != kind[j]: pairs[(kind[j], kind[r[k]])] = (j, r[k])
+                    k -= 1
+            i = why[i]
+        return list(pairs.values())
+
+    kind, move = [d["kind"] for d in nodes], {}
+    now, order = length(move)
+    best, seed = (now, order), 1
+    for it in range(TRIES):
+        if it % 8 == 0: pairs = holdups(order, costs[it // 8 % len(costs)])
+        seed = (seed * 1103515245 + 12345) % 2 ** 31
+        a, b = pairs[(seed >> 8) % len(pairs)]
+        gap = base[b] + move.get(kind[b], 0.0) - base[a] - move.get(kind[a], 0.0) + 0.3
+        trial = dict(move)
+        if seed >> 7 & 1: trial[kind[a]] = trial.get(kind[a], 0.0) + max(gap, 0.5)
+        else: trial[kind[b]] = trial.get(kind[b], 0.0) - max(gap, 0.5)
+        e, o = length(trial)
+        if e < now + SLACK * (1.0 - it / TRIES):
+            now, order, move = e, o, trial
+            if e < best[0]: best = (e, o)
+    return best[1]
 
 
 def rank_program(g, core, T, topo):
@@ -140,7 +167,7 @@ def rank_program(g, core, T, topo):
     if rank is None:
         return
     O = AluOpType
-    nodes, hist, free = [], {}, {"d": 0, "ls": 0}
+    nodes, hist, free = [], {}, {"d": 0, "ls": 0, "part": "0"}
 
     def A(name, a=None, b=None, s=1, p0=0, p1=128):
         buf, at, cols = PLACE[name]
@@ -177,7 +204,7 @@ def rank_program(g, core, T, topo):
                 if w: h[:] = [e for e in h if not (x["a"] <= e[0] and e[1] <= x["b"] and e[4] % x["s"] == 0 and (x["a"] - e[0]) % x["s"] == 0)]
                 h.append((x["a"], x["b"], w, me, x["s"]))
         nodes.append({"q": q, "calls": calls, "cost": cost, "lat": lat, "deps": deps, "sem": sem, "grp": grp, "ga": 0, "sc": 0,
-                      "kind": q + "".join(" " + x["n"].rstrip("0123456789") for x in writes[:1] + reads[:2])})
+                      "kind": q + free["part"] + "".join(" " + x["n"].rstrip("0123456789") for x in writes[:1] + reads[:2])})
         if isinstance(cost, tuple): nodes[-1].update({"cost": cost[0], cost[1]: cost[2]})
         return me
 
@@ -264,6 +291,7 @@ def rank_program(g, core, T, topo):
     node("G", [lambda: g.sem_inc(T.sem["go"], 1)], 0.05, [A("gate")], [], sem=("go", 1), extra=[sent])
     dma(A("si")["ap"], T.succ[:], [A("gate")], [A("si")], 512)
     dma(A("xq", 0, V)["ap"], T.x[:], [A("gate")], [A("xq", 0, V)], 256)
+    dma(A("p0_")["ap"], T.past[:], [A("gate")], [A("p0_")], 256)
     for who, (n, o, w) in zip(COPIES, (("xq", V, A("xw", 0, V)), ("rq", 0, A("rb", DUM, DUM + V)), ("rq", V, A("rb", DUM, DUM + V)),
                                        ("pq", 0, A("pb", 0, V)), ("pq", V, A("pb", 0, V)))): copy(who, A(n, o, o + V), w)
     for n in ("pa", "pb", "ra", "rb"):
@@ -272,15 +300,15 @@ def rank_program(g, core, T, topo):
 
     c = lambda i: A("cc", i, i + 1)
     ROW, P16, PF, ODD, RS, RG0, RG1, C1L, C1R, E12, E15, L10, M2, TH, NG, LIM, EVR, W0, W1, W2, W3, W4, W5, CA = range(24)
-    PM, EQ = 28, 32
+    PM, CL = 28, 32
     rw, pp = A("pc", 1, 2), A("pc", 0, 1)
     iota(pp, [[0, 1]], 0, 1)
     iota(A("id_", 0, 16), [[32, 8], [-16, 2]], 16, 1); iota(A("id_", 16, 32), [[1, 16]])
     iota(A("ie"), [[1, 128]]); iota(A("ig", 0, 8), [[1, 8]]); iota(A("ik"), [[1, 8], [0, 16]])
     iota(A("ib"), [[0, 16], [1, 16]]); iota(A("ic"), [[1, 256]])
     iota(A("ih", 0, 16), [[1, 2], [2, 8]])
-    iota(A("ij", 16, 32), [[16, 16]], 0, 1); iota(A("in_", 0, 96), [[-8, 2], [0, 3], [1, 16]]); iota(A("id_", 32, 64), [[16, 32]], 0, 1)
-    fill(A("xw", V, 2 * V), PEN); fill(A("rb", 0, DUM), 0.0); fill(A("bw", 0, DUM), 0.0); fill(A("bw", DUM + V, DUM + 2 * V), 1.0)
+    iota(A("ij", 0, 64), [[1, 4], [64, 16]], V, 4); iota(A("in_", 0, 32), [[-8, 2], [1, 16]]); iota(A("id_", 32, 64), [[16, 32]], 0, 1)
+    fill(A("xw", V, 2 * V), PEN); fill(A("bw", V, 2 * V), 1.0)
     ts(rw, pp, 15, O.bitwise_and)
     ts(A("pc", 2, 3), pp, 4, O.arith_shift_right)
     ts(A("pc", 3, 4), pp, 4, O.arith_shift_right, 1, O.bitwise_and)
@@ -303,25 +331,29 @@ def rank_program(g, core, T, topo):
     for m in range(16): act(A("wm", 128 * m + m, 128 * m + 128, 16), A("g8"))
     ts(A("idm"), A("ie"), c(PF), O.is_equal)
     for n, v in (("ngm", -1.0), ("hm", 0.5), ("bgm", 4096.0), ("nbm", -4096.0), ("zm", 0.0), ("idf", 1.0)): act(A(n), A("idm"), scale=v)
-    ts(A("kc"), A("ic"), 2.0 ** -20, O.mult)
+    ts(A("kc"), A("ic"), 2.0 ** -21, O.mult)
     fill(A("smx"), 0.0); fill(A("smx", 0, 1024, 8), 255.0)
     fill(A("sg1"), 1.0); fill(A("sg1", 0, 256, 16), 0.0); fill(A("mh"), -0.5)
     ts(A("dg", 0, 256), A("ib"), c(ROW), O.is_equal)
     ts(c(L10), c(ROW), 10.0, O.is_lt); ts(c(C1L), c(ROW), 13.0, O.is_ge); ts(c(E12), c(ROW), 12.0, O.is_equal); ts(c(E15), c(ROW), 15.0, O.is_equal)
     ts(c(W4), c(ROW), 13.0, O.is_lt, c(L10), O.subtract); cp(c(C1R), c(W4))
     ts(c(M2), c(C1R), c(E12), O.subtract)
+    ts(c(CL), c(ROW), 13.0, O.not_equal, -2.0 ** 22, O.mult); ts(c(CL), c(CL), -100.0 * 2 ** 14, O.add)
     for a, b, v in ((0, 10, 2.0 ** 20), (10, 11, 2.0 ** 14), (11, 12, 256.0), (12, 13, 1.0), (13, 14, -2.0 ** 14), (14, 15, -256.0), (15, 16, -1.0)): fill(A("wv", a, b), v)
     tt(A("wx"), A("wv"), A("dg", 0, 16), O.mult); reduce(c(RS), A("wx"), O.add)
     act(A("cll"), A("ic"), AF.Identity, bias=c(C1L), scale=c(E12)); act(A("clr"), A("ic"), AF.Identity, bias=c(C1R), scale=c(E15))
     act(A("s10"), A("idm"), scale=c(L10))
     ts(A("wm2"), A("wm"), c(M2), O.mult)
+    for m in range(16):
+        if m % 4 < RO - 1: act(W("wmn", m), W("wm", m), scale=-1.0)
     if "V" in DIST + DIST0:
-        ts(A("wmx"), A("wm"), -2.0 ** -12, O.mult)
+        ts(A("wmx"), A("wm"), -2.0 ** -13, O.mult)
         dma(A("xq", 2 * V, 3 * V)["ap"], T.x[:], [A("gate")], [A("xq", 2 * V, 3 * V)], 256)
     ts(A("bom"), A("ik"), c(P16), O.is_equal)
     ts(A("lw"), A("dg", 0, 16), 1024.0, O.mult)
     for m in range(16): act(W("wt", m), A("bom"), scale=A("lw", m, m + 1))
-    ts(A("lh"), A("ie"), c(PF), O.is_lt, -1.0, O.mult); tt(A("ltm"), A("lh"), A("bom"), O.mult)
+    act(A("nw"), W("wt", 12), scale=-PEN / 1024)
+    ts(A("lh"), A("ie"), c(PF), O.is_lt, -1.0, O.mult); tt(A("lh"), A("lh"), A("bom"), O.mult); tt(A("ltm"), A("lh"), A("nbm"), O.add)
     fill(A("one"), 1.0); fill(A("onm"), 1.0); fill(A("e5"), 0.0)
     cp(c(W5), A("pc", 6, 7))
     for t in range(RO - 1): ts(c(PM + t), c(W5), float(t), O.is_le)
@@ -343,21 +375,18 @@ def rank_program(g, core, T, topo):
     cp(A("oh"), A("dg", 0, 16)); fill(A("pen"), 0.0); cp(A("omx"), A("ih", 0, 16))
     for a in range(16):
         o = 128 * (a % 2) + 16 * (a // 2)
-        if a == 0: ts(A("thr"), A("dg", 0, 256), 1e9 + 0.5, O.mult, -1e9, O.add)
-        if PAIRS[a] == "V": ts(A("thr", o, o + 16), A("dg", 0, 16), 1e9 + B10, O.mult, -1e9, O.add)
-    ts(A("rs"), A("in_", 0, 96), c(P16), O.is_equal)
-    ts(A("wx"), A("ij", 16, 32), c(NG), O.add)
-    for t in range(RO):
-        for n, o in (("v3", 0.0), ("vm", -float(DUM))):
-            ts(A(n, 48 * t, 48 * t + 16), A("wx"), 4.0, O.mult, float(t), O.add)
-            ts(A(n, 48 * t + 16, 48 * t + 32), A("wx"), 4.0, O.mult, float(V + t), O.add)
-            ts(A(n, 48 * t + 32, 48 * t + 48), A("wx"), o, O.add)
+        if a == 0: ts(A("thr"), A("dg", 0, 256), -1e9, O.mult, 1e9, O.add)
+        if PAIRS[a] == "V": ts(A("thr", o, o + 16), A("dg", 0, 16), B10 - 1e9, O.mult, 1e9, O.add)
+    ts(A("rs"), A("in_", 0, 32), c(P16), O.is_equal, 4096.0, O.mult)
+    ts(c(CL + 1), c(NG), 4.0, O.mult); ts(A("vs"), A("ij", 0, 64), c(CL + 1), O.add)
+    ts(A("vd"), A("id_", 32, 48), c(NG), O.add, 2.0 * V, O.add)
     ts(A("fvs"), A("id_", 32, 64), c(NG), O.add); ts(A("flo"), A("id_", 32, 64), c(NG), O.add)
     ts(A("b8"), A("ik"), c(PF), O.is_equal)
     cp(A("thf", 0, 1, p1=8), A("thi", 0, 1, p1=8))
     mms([(A("p7", 0, 1), A("b8", p1=8), A("thf", 0, 1, p1=8))])
     ts(c(TH), A("p7", 0, 1), 256.0, O.mult); cp(c(LIM), c(TH))
-    cp(A("cb"), A("ci")); cp(A("sb"), A("si"))
+    for n, i in (("cb", "ci"), ("sb", "si")):
+        cp(A(n, 0, V), A(i)); dma(A(n, V, 2 * V)["ap"], A(n, 0, V)["ap"], [A(n, 0, V)], [A(n, V, 2 * V)], 512)
 
     key = {}
 
@@ -377,7 +406,7 @@ def rank_program(g, core, T, topo):
 
     def squeeze(n, i, w, by="wm"):
         p, o = "p%d" % (4 + i // 4), 32 * (i % 4)
-        parts([(A(p, o, o + 32 * w), W(by, m), A(n, 512 * i + m, 512 * (i + w), 16)) for m in range(16)], 8, key[p])
+        parts([(A(p, o, o + 32 * w), W(by, m), A(n, 512 * i + m, 512 * (i + w), 16)) for m in range(16)], 16 // max(w, 2), key[p])
 
     def distances(t):
         for h in range(2):
@@ -387,20 +416,20 @@ def rank_program(g, core, T, topo):
         for h in range(8):
             p, x = "p%d" % (h % 2), A("xg", 512 * h, 512 * h + 512)
             if (DIST if t else DIST0)[h // 2] == "V":
-                tt(x, ind(A("xw"), A("ct%d" % t, 32 * h, 32 * h + 32)), A("xq", V + t, 3 * V, 4), O.subtract)
-                ts(A("ad", 512 * h, 512 * h + 512), x, 0.0, O.max, 2.0 ** -11, O.mult)
+                tt(x, ind(A("xw", 0, 2 * V), A("ct%d" % t, 32 * h, 32 * h + 32)), A("xq", V + t, 3 * V, 4), O.subtract)
+                ts(A("ad", 512 * h, 512 * h + 512), x, 0.0, O.max, 2.0 ** -12, O.mult)
                 if h % 2: squeeze("xg", h - 1, 2, "wmx"); squeeze("ad", h - 1, 2)
                 continue
-            act(x, ind(A("xw"), A("ct%d" % t, 32 * h, 32 * h + 32)))
+            if h % XW == 0: act(A("xg", 512 * h, 512 * (h + XW)), ind(A("xw", 0, 2 * V), A("ct%d" % t, 32 * h, 32 * (h + XW))))
             mms([(A(p), A("idm"), x), (A(p, 0, 256), A("ngm"), mine), (A(p, 256, 512), A("ngm"), mine)])
-            act(A("ad", 512 * h, 512 * h + 512), A(p), AF.Abs, scale=2.0 ** -12)
-            if h % 2: squeeze("ad", h - 1, 2)
+            act(A("ad", 512 * h, 512 * h + 512), A(p), AF.Abs, scale=2.0 ** -13)
+            if h % 4 == 3: squeeze("ad", h - 3, 4)
 
     def tests(t):
         k = 0
         for lo in (0, 4):
             for kind in "PR":
-                win, mine, n = (A("pb"), A("rq", t, 2 * V, 4), "tp") if kind == "P" else (A("rb", DUM), A("pq", t, 2 * V, 4), "tr")
+                win, mine, n = (A("pb", 0, 2 * V), A("rq", t, 2 * V, 4), "tp") if kind == "P" else (A("rb", 0, 2 * V), A("pq", t, 2 * V, 4), "tr")
                 for h in range(lo, lo + 4):
                     off, out = A("ct%d" % t, 32 * h, 32 * h + 32), A(n, 512 * h, 512 * h + 512)
                     if (TESTS if t else TESTS0)[kind][h] == "V": tt(out, ind(win, off), mine, O.is_ge if kind == "P" else O.is_le)
@@ -409,60 +438,61 @@ def rank_program(g, core, T, topo):
                         act(x, ind(win, off))
                         mms([(A(p), A("idm"), x), (A(p), A("ngm"), mine)])
                         act(out, A(p), AF.Relu, bias=1.0, scale=1.0 if kind == "P" else -1.0)
-                    if h >= 6 and kind == "R": squeeze(n, h, 1)
-                    elif h % 2: squeeze(n, h - 1, 2)
+                    if lo and kind == "R":
+                        if h > 4: squeeze(n, h - (h == 5), 1 + (h == 5))
+                    elif h % 4 == 3: squeeze(n, h - 3, 4)
 
-    sl, xl, sc = A("l3", 0, 16), A("l3", 16, 32), A("l3", 32, 48)
+    sl, sc = A("l3", 0, 16), A("l3", 16, 32)
 
     def partner(t):
         act(A("klo"), A("p4", 0, 128))
         tt(A("k8"), A("p5", 0, 128), A("klo"), O.min)
         for a, b, w in (("k8", "k4", 64), ("k4", "k2", 32), ("k2", "k1", 16)): tt(A(b), A(a, 0, w), A(a, w, 2 * w), O.min)
-        ts(A("mk"), A("k1"), 2.0 ** 20, O.mult, 2.0 ** 21, O.min)
+        ts(A("mk"), A("k1"), 2.0 ** 21, O.mult, 2.0 ** 22, O.min)
         ts(A("kq"), A("mk"), 255, O.bitwise_and); cp(A("kqu"), A("kq"))
         tt(A("cm"), ind(A("ca%d" % t), A("kqu")), A("dg", 0, 256), O.mult)
         scan(A("cs"), A("sg1"), A("cm"), 0.0, O.mult, O.add)
         cp(A("cu"), A("cs", 15, 256, 16))
-        cp(A("bits"), ind(A("bw", DUM), A("cu")))
+        cp(A("bits"), ind(A("bw", 0, 2 * V), A("cu")))
+        tt(A("r2s"), ind(A("rb", 0, 2 * V), A("cu")), A("rq", V + t, 2 * V, 4), O.min)
         ts(A("kl", 0, 16), A("mk"), 14, O.arith_shift_right, 63, O.bitwise_and)
         ts(A("kl", 16, 32), A("mk"), 8, O.arith_shift_right, 63, O.bitwise_and)
         ts(A("pen", 0, 16), A("mk"), c(LIM), O.is_ge, 128.0, O.mult)
         tt(A("klf", 0, 32), A("kl"), A("pen"), O.add)
-        ts(A("klf", 32, 48), A("mk"), c(LIM), O.is_ge, 4096.0, O.mult)
-        for m in range(16): act(A("ke", m, 768, 16), A("klf"), scale=A("oh", m, m + 1))
-        for p, cl, r in (("p5", "clr", 13), ("p4", "cll", 10)):
+        for m in range(16): act(A("ke", m, 512, 16), A("klf", 0, 32), scale=A("oh", m, m + 1))
+        for p, cl, r in (("p4", "cll", 10), ("p5", "clr", 13)):
             grp, o = {}, A(p, 0, 256)
             mms([(o, A("idm"), A(cl))], grp); mms([(o, A("s10"), A("bits"))], grp)
-            mms([(o, W("wm", r), A("ke", 0, 256)), (o, W("wm", r + 1), A("ke", 256, 512))] + [(o, W("wm", 12), A("ke", 512, 768))][:r == 10], grp)
-        ts(A("fr"), A("p5", 0, 256), c(RS), O.mult)
+            mms([(o, W("wm", r), A("ke", 0, 256)), (o, W("wm", r + 1), A("ke", 256, 512))], grp)
+        ts(A("fr"), A("p5", 0, 256), c(RS), O.mult, c(CL), O.max)
         act(A("fev"), A("p4", 0, 256), scale=c(RG0)); act(A("fod"), A("p4", 0, 256), scale=c(RG1))
-        parts([(A("p7", 0, 16), W("wm2", m), A("bits", m, 256, 16)) for m in range(16)], 4)
-        for i in range(3): tt(A("d3", 16 * i, 16 * i + 16), A("p7", 0, 16), A("vm", 48 * t + 16 * i, 48 * t + 16 * i + 16), O.subtract)
-        ts(A("has"), A("mk"), 2.0 ** 20, O.is_lt)
-        tt(A("bc"), A("d3", 0, 16), A("has"), O.mult); tt(A("bc"), A("bc"), A("v3", 48 * t, 48 * t + 16), O.add); cp(A("bcu"), A("bc"))
         seen = {"V": 0, "S": 0}
-        for a in range(16):
-            gr, h, who = a // 2, a % 2, PAIRS[a]
-            p = {"V": ("p0", "p2"), "S": ("p1", "p3")}[who][seen[who] % 2]
+        for gr in (0, 2, 4, 6, 1, 3, 5, 7):
+            who = PAIRS[2 * gr]
+            p = {"V": ("p0", "p2", "p5"), "S": ("p1", "p3", "p4")}[who][seen[who] % 3]
             seen[who] += 1
             lo = 32 * (gr // 2)
-            mms([(A(p, 0, 256), A("fod" if gr % 2 else "fev", 128 * h, 128 * h + 128, p0=lo, p1=lo + 32), A("fr", p0=lo, p1=lo + 32))])
-            if who == "V": reduce(A("mx", a, a + 1), A(p, 0, 256), O.max)
-            else: act(A("junk", 256 * a, 256 * a + 256), A(p, 0, 256), AF.Relu, bias=-B10, acc=A("mx", a, a + 1))
-        tt(A("we"), ind(A("mx"), A("omx")), A("thr"), O.is_le)
-        mms([(A("p7", 64, 112), A("we", 128 * h, 128 * h + 128), A("rs", 48 * h, 48 * h + 48)) for h in range(2)])
-        tt(A("t3"), A("p7", 64, 112), A("d3"), O.mult)
-        if t + 1 < RO: cp(A("wn"), A("p7", 64, 80))
-        tt(A("t3"), A("t3"), A("v3", 48 * t, 48 * t + 48), O.add)
+            for h in range(2):
+                mms([(A(p, 256 * h, 256 * h + 256), A("fod" if gr % 2 else "fev", 128 * h, 128 * h + 128, p0=lo, p1=lo + 32), A("fr", p0=lo, p1=lo + 32))])
+            for a in (2 * gr, 2 * gr + 1):
+                o = A(p, 256 * (a % 2), 256 * (a % 2) + 256)
+                if who == "V": reduce(A("mx", a, a + 1), o, O.max)
+                else: act(A("junk", 256 * a, 256 * a + 256), o, AF.Relu, bias=-B10, acc=A("mx", a, a + 1))
+        tt(A("we"), ind(A("mx"), A("omx")), A("thr"), O.is_gt)
+        grp, o = {}, A("p7", 0, 16)
+        parts([(o, W("wm2", m), A("bits", m, 256, 16)) for m in range(16)], 4, grp)
+        mms([(o, A("we", 128 * h, 128 * h + 128), A("rs", 16 * h, 16 * h + 16)) for h in range(2)], grp)
+        tt(A("t3", 16, 32), o, A("vd"), O.min); tt(A("t3", 0, 16), o, A("vs", 16 * t, 16 * t + 16), O.min)
         cp(A("l3"), A("t3"))
+        if t + 1 < RO: ts(A("wn"), o, float(V), O.is_lt)
 
     def merge(t):
-        grp, w = {}, A("rb", DUM + t, DUM + V, 4)
-        tt(A("r2"), ind(A("rq", 0, V), sl), A("rq", V + t, 2 * V, 4), O.min)
-        act(A("sx"), ind(A("sb"), sl))
-        scat(A("rb", 0, DUM + V), sc, A("r2"))
-        mms([(A("p2", 0, 256), W("wt", 12), A("bw", DUM + t, DUM + V, 4))], grp); mms([(A("p2", 0, 256), A("idm"), A("r2"))], grp)
+        grp, w = {}, A("rb", t, V, 4)
+        scat(A("rb"), sc, A("r2s"))
+        act(A("rbv"), ind(A("rq"), sl)); act(A("sx"), ind(A("sb"), sl))
+        mms([(A("p2", 0, 256), W("wt", 12), A("bw", t, V, 4))], grp); mms([(A("p2", 0, 256), A("idm"), A("rbv"))], grp)
         tt(w, w, A("p2", 0, 256), O.min)
+        tt(A("r2"), A("rbv"), A("rq", V + t, 2 * V, 4), O.min)
         mms([(A("p5", 0, 128), A("la%d" % par), A("sx", par, 256, 2)) for par in range(2)])
         cp(A("la"), A("p5", 0, 128))
 
@@ -470,13 +500,13 @@ def rank_program(g, core, T, topo):
         mms([(A("p7", 448, 464), A("onm"), A("wn"))])
         reduce(A("mt", 0, 1), A("p7", 448, 464), O.add)
         cp(A("mi", 0, 1), A("mt", 0, 1)); ts(A("mi", 1, 2), A("mi", 0, 1), 31, O.bitwise_and)
-        ts(A("mt", 1, 2), A("mi", 1, 2), 256.0, O.mult, c(TH), O.add); ts(c(LIM), A("mt", 1, 2), 2.0 ** 20, O.min)
+        ts(c(LIM), A("mi", 1, 2), 256.0, O.mult, c(TH), O.add)
 
     def names(t):
-        scat(A("bw", 0, DUM + V), sc, A("bs", t, V, 4))
+        scat(A("bw"), sc, A("bs", t, V, 4))
         mms([(A("p7", 128, 192), W("wm2", m), A("bw", DUM + m, DUM + V, 16)) for m in range(16)])
         f = A("p7", 128, 160)
-        cp(A("flu"), A("p7", 128, 192))
+        if AGAIN != "XXX": cp(A("flu"), A("p7", 128, 192))
         tt(A("chf"), f, A("flo"), O.not_equal); cp(A("flo"), f)
         ts(A("flt"), f, float(G5), O.is_lt); tt(A("dfl"), f, A("fvs"), O.subtract); tt(A("dfl"), A("dfl"), A("flt"), O.mult)
 
@@ -485,37 +515,36 @@ def rank_program(g, core, T, topo):
         send([(A("%sn%d" % (kind, t), 0, 128), A(kind + "wa", o, o + 128), A(kind + "wb", o, o + 128))], "a%s%%s%d" % (kind, t), 1.5)
 
     def pmerge(t):
-        tt(A("pn%d" % t), ind(A("pq", 0, V), sl), A("pq", V + t, 2 * V, 4), O.max)
+        tt(A("pn%d" % t), ind(A("pq"), sl), A("p0_", t, V, 4), O.max)
         block("p", t)
         cp(A("pq", t, V, 4), A("pn%d" % t))
-        tt(A("dp"), A("pn%d" % t, 0, 128), A("pq", V + t, V + G5, 4), O.not_equal)
 
     def xmerge(t):
         grp, o = {}, A("p3", 0, 256)
-        act(A("xp"), ind(A("xq", 0, 2 * V), xl))
+        act(A("xp"), ind(A("xq", 0, 2 * V), sl))
         mms([(o, A("hm"), A("xq", V + t, 2 * V, 4)), (o, A("hm"), A("mh"))], grp); mms([(o, A("hm"), A("xp"))], grp)
         ts(A("xq", t, V, 4), o, MAGIC, O.add, MAGIC, O.subtract)
 
     def successors(t, h):
+        free["part"] = free["part"][:last] + "ab"[h]
         for i in (2 * h, 2 * h + 1):
             a, b = A("sga", 512 * i, 512 * i + 512), A("sgb", 512 * i, 512 * i + 512)
-            act(b, ind(A("rb", DUM), A("lb%d" % t, 32 * i, 32 * i + 32)))
-            tt(a, ind(A("rb", DUM), A("la", 32 * i, 32 * i + 32)), b, O.min)
+            act(b, ind(A("rb", 0, 2 * V), A("lb%d" % t, 32 * i, 32 * i + 32)))
+            tt(a, ind(A("rb", 0, 2 * V), A("la", 32 * i, 32 * i + 32)), b, O.min)
         o = 1024 * h
         scan(A("sc", o, o + 1024), A("smx"), A("sga", o, o + 1024), 255.0, O.max, O.min)
         tt(A("rn%d" % t, 128 * h, 128 * h + 128), A("sc", o + 7, o + 1024, 8), A("r2", 128 * h, 128 * h + 128), O.min)
 
     def publish(t):
-        tt(A("dr"), A("rn%d" % t, 0, 128), A("rq", V + t, V + G5, 4), O.not_equal)
         grp, o = {}, A("p7", 256, 288)
         mms([(o, A("idm"), A("chf"))], grp)
-        for n in ("dp", "dr"): mms([(o, W("wm", 4 * a + t), A(n, a, 128, 4)) for a in range(4)], grp)
+        for by, n in (("wm", "rq"), ("wmn", "pq")): mms([(o, W(by, 4 * a + t), A(n, V + t + 4 * a, V + G5, 16)) for a in range(4)], grp)
+        for by, n in (("wm", "pn"), ("wmn", "rn")): mms([(o, W(by, 4 * a + t), A(n + str(t), a, 128, 4)) for a in range(4)], grp)
         ts(A("ch"), o, 0.0, O.is_gt)
         scan(A("scq"), A("one"), A("ch"), 0.0, O.mult, O.add)
-        ts(A("c96"), A("ch"), float(CAP + 1), O.mult, -1.0, O.add)
         grp, o = {}, A("p7", 320, 352)
         mms([(o, A("ltm"), A("ch"))], grp); mms([(o, A("bom"), A("scq"))], grp)
-        tt(A("go"), o, A("c96"), O.is_le)
+        ts(A("go"), o, CAP - 4096.0, O.is_le)
         grp, rows = {}, [m for m in range(16) if m % 4 <= t]
         mms([(A("p6"), A("zm"), A("dig"))], grp)
         if t: mms([(A("p6", m, G5, 16), W("wt", m), A("e5")) for m in rows], grp)
@@ -535,13 +564,30 @@ def rank_program(g, core, T, topo):
         for n in ("tp", "tr"):
             parts([(A("p6", 0, 256), W("wm", k), A(n, 256 * k, 256 * k + 256)) for k in range(16)], 2, grp)
         act(A("os"), A("p6", 0, 256), AF.Sign)
+        grp, o = {}, A("p6", 256, 272)
+        ts(A("nh"), A("mk"), 2.0 ** 21, O.is_ge, 4096.0, O.mult)
+        parts([(o, A("idm"), A("nh"))] + [(o, W("wm2", m), A("bits", m, 256, 16)) for m in range(16)], 6, grp)
+        tt(A("bc"), o, A("vs", 16 * t, 16 * t + 16), O.min); cp(A("bcu"), A("bc"))
         act(A("cx"), ind(A("cb"), A("bcu")))
         for o, m in ((0, "bgm"), (256, "nbm")): mms([(A("p6", o, o + 256), A("idf"), own), (A("p6", o, o + 256), A(m), A("os"))])
         tt(A("cy"), A("p6", 0, 256), A("cx"), O.min)
         tt(own, A("p6", 256, 512), A("cy"), O.max)
 
-    def again(n, out, raw):
-        for h in range(2): copy(AGAIN["xpr".index(n)], A(out[0], out[1] + G5 * h, out[1] + G5 * h + G5), ind(A(raw, 0, V), A("flu", 32 * h, 32 * h + 32)))
+    def again(n, win, t):
+        who = AGAIN["xpr".index(n)]
+        if who != "X":
+            if n == "x": fill(A("xq", t + 1, V, 4), PEN)
+            copy(who, A(win, 0, V), ind(A(n + "q", 0, V), A("flu")))
+            return
+        new = A("xq", t, V, 4) if n == "x" else A("%sn%d" % (n, t))
+        o, w, grp = A({"x": "p0", "p": "p3", "r": "p2"}[n], 0, 256), A(win, t, V, 4), {}
+        scat(A(win), sc, new)
+        mms([(o, A("nw") if n == "p" else W("wt", 12), A("bw", t, V, 4))], grp); mms([(o, A("idm"), new)], grp)
+        tt(w, w, o, O.max if n == "p" else O.min)
+        if n == "x":
+            o, w = A("p1", 0, 256), A(win, t + 1, V, 4)
+            mms([(o, A("idm"), A("xw", V, V + 256)), (o, A("nw"), A("bw", t + 1, V, 4))])
+            tt(w, w, o, O.max)
 
     turn(0)
     fill(A("xw", 0, V, 4), PEN)
@@ -550,6 +596,7 @@ def rank_program(g, core, T, topo):
     for t in range(RO):
         last = t == RO - 1
         tests(t)
+        free["part"] = "3" if last else ""
         if not last:
             turn(t + 1); even_list(t + 1)
         partner(t)
@@ -559,7 +606,7 @@ def rank_program(g, core, T, topo):
             names(t); pmerge(t)
         xmerge(t)
         if last:
-            dma(T.yc[:], A("cb")["ap"], [A("cb")], [], 512)
+            dma(T.yc[:], A("cb", 0, V)["ap"], [A("cb", 0, V)], [], 512)
             dma(T.yx[:], A("xq", 0, V)["ap"], [A("xq", 0, V)], [], 256)
             for h in range(2):
                 successors(t, h)
@@ -573,12 +620,11 @@ def rank_program(g, core, T, topo):
         publish(t)
         count()
         successors(t, 1)
-        fill(A("xq", t + 1, V, 4), PEN)
-        again("x", ("xw", 0), "xq")
+        again("x", "xw", t)
         distances(t + 1)
-        again("p", ("pb", 0), "pq")
+        again("p", "pb", t)
         cp(A("rq", t, V, 4), A("rn%d" % t))
-        again("r", ("rb", DUM), "rq")
+        again("r", "rb", t)
         for who, n in zip(GHOST, ("pa", "pb", "ra", "rb")):
             o = 32 * "ab".index(n[1])
             copy(who, gh[n], ind(A(n[0] + "w" + n[1], 0, G5 + 128 * (t + 1)), A("lz%d" % t, o, o + 32)))

from concourse.bass import DstId, RemoteDMATransfer
from concourse.mybir import AluOpType, AxisListType, ActivationFunctionType as AF

V, G5, RO, CAP = 1024, 512, 4, 96
DUM, WID = 0, 2304
PEN = 16384.0
B10 = 10.0 * 2 ** 20
MAGIC = 1.5 * 2 ** 23
XW = 2
TESTS = {"P": "VVVVVSVV", "R": "VVSSVSVV"}
TESTS0 = {"P": "VVVVVVVV", "R": "VSVSVSVV"}
DIST, DIST0 = "SSSS", "SSSS"
AGAIN, GHOST, ODDK, DGT = "SXX", "SVSV", "VVVV", "V"
COPIES = "VVVVV"
PAIRS = "VVVVSSSSVVVVSSSS"
CYC, HOP, SELF = 0.83e-3, 0.22, 0.11
CALL = {"V": 0.01, "S": 0.03, "P": 0.004}
RATES = ((1.56, 3.8, 1.0), (1.15, 2.2, 1.3), (2.0, 5.4, 1.3))
TRIES, SLACK = 4500, 0.25

SCRATCH, PLACE, ORDER = {}, {}, {}
SIZE = {"bfloat16": 2, "uint16": 2, "float32": 4, "int32": 4}


def _b(names, cols, dtype, where="sbuf"):
    for name in names.split():
        if where == "sbuf" and cols <= 512:
            pool = "pool_" + dtype
            at = SCRATCH.get(pool, (where, [128, 0], dtype))[1][1]
            step = 32 // SIZE[dtype]
            SCRATCH[pool] = (where, [128, at + -(-cols // step) * step], dtype)
            PLACE[name] = (pool, at, cols)
        else:
            SCRATCH[name] = (where, [128, cols], dtype)
            PLACE[name] = (name, 0, cols)


_b("rb pb xw bw", WID, "bfloat16"); _b("nw", 128, "bfloat16")
_b("rq pq wmx", 2 * V, "bfloat16"); _b("xq", 3 * V, "bfloat16")
_b("bs p0_", V, "bfloat16")
_b("ci si", V, "int32"); _b("cb sb", 2 * V, "float32")
for _t in range(RO):
    _b("ct%d" % _t, 256, "uint16"); _b("ca%d" % _t, 256, "float32"); _b("lb%d" % _t, 128, "uint16")
    _b("rn%d pn%d" % (_t, _t), 256, "bfloat16"); _b("z%d" % _t, 32, "uint16"); _b("lz%d" % _t, 64, "uint16")
_b("xg ad tp tr gp", 4096, "bfloat16"); _b("sga sgb sc", 2048, "bfloat16")
_b("rwa rwb pwa pwb", 896, "bfloat16")
_b("wm wm2 wmn wt", 2048, "bfloat16"); _b("smx", 1024, "bfloat16")
_b("idm ngm hm bgm nbm zm bom ltm s10 onm lh", 128, "bfloat16"); _b("idf b8 la0 la1 lb_0 lb_1", 128, "float32")
_b("ic thr sg1", 256, "float32"); _b("ib", 256, "int32"); _b("id_ ie ig ih ij ik in_", 128, "int32")
_b("pc", 8, "int32"); _b("cc", 40, "float32"); _b("g8", 8, "bfloat16"); _b("lw wv wx", 16, "float32")
_b("pat", 224, "bfloat16"); _b("tc", 32, "bfloat16"); _b("ta", 32, "float32"); _b("pa pb_ pc_ dig dt dgt", 512, "bfloat16")
_b("dg", 256, "bfloat16"); _b("junk", 4096, "bfloat16"); _b("kc cll clr mh", 256, "bfloat16"); _b("rs", 32, "bfloat16"); _b("nh", 16, "bfloat16"); _b("r2s rbv", 256, "bfloat16"); _b("one", 32, "float32")
_b("o2 ofin omx kqu cu bcu", 16, "uint16")
_b("in12 tr12", 512, "float32")
_b("klo k8", 128, "float32"); _b("k4", 64, "float32"); _b("k2", 32, "float32"); _b("k1 bc oh vd", 16, "float32"); _b("pen klf", 32, "float32"); _b("mk kq", 16, "int32")
_b("cm cs sx cx cy", 256, "float32"); _b("bits fev fod fr we os xp r2", 256, "bfloat16"); _b("kl", 32, "int32"); _b("ke", 768, "bfloat16")
_b("mx", 16, "float32"); _b("t3", 32, "float32"); _b("l3", 32, "uint16"); _b("vs", 64, "float32"); _b("la", 128, "uint16")
_b("wn", 16, "bfloat16"); _b("mt", 2, "float32"); _b("mi", 2, "int32"); _b("thi", 8, "int32"); _b("thf", 8, "float32")
_b("dr dp", 128, "bfloat16")
_b("fvs flo flt dfl c96 gf", 32, "float32"); _b("e5 ge go chf ch scq", 32, "bfloat16"); _b("fu", 32, "uint16"); _b("flu", 64, "uint16")
_b("p0 p1 p2 p3 p4 p5 p6 p7", 512, "float32", "psum")
_b("gate", 8, "float32")
SEMAPHORES = ["qV", "qS", "qP", "qG", "ipA", "ipB", "irA", "irB", "go"] + ["d%d" % i for i in range(28)] + ["ls%d" % i for i in range(12)] + \
    ["%s%s%d" % (a, s, t) for a in ("ar", "ap", "az") for s in "AB" for t in range(RO - 1)]


def plan(nodes):
    n = len(nodes)
    Q, lat = [d["q"] for d in nodes], [d["lat"] for d in nodes]
    costs = [[(f if d["q"] in CALL else 1.0) * (d["cost"] + (ga * d["ga"] + sc * d["sc"]) * CYC) + (0.0 if d["ga"] or d["sc"] else CALL.get(d["q"], 0.0) * len(d["calls"]))
              for d in nodes] for ga, sc, f in RATES]
    c = costs[0]
    after, before = [[] for _ in nodes], [[] for _ in nodes]
    for i, d in enumerate(nodes):
        for j, w in d["deps"].items():
            h = -lat[j] if not w else SELF if Q[j] == Q[i] else HOP
            after[j].append((i, h)); before[i].append((j, h))
    base = [0.0] * n
    for i in range(n - 1, -1, -1):
        run, most = {}, 0.0
        for k, h in sorted(after[i], key=lambda e: c[e[0]] - base[e[0]]):
            most = max(most, run.get(Q[k], 0.0) + base[k] + h)
            run[Q[k]] = run.get(Q[k], 0.0) + c[k]
        base[i] = c[i] + lat[i] + most

    def sweep(far):
        left, est, free, ready, order, last = [len(p) for p in before], [0.0] * n, {}, {}, [], 0.0
        for i in range(n):
            if not left[i]: ready.setdefault(Q[i], []).append(i)
        while len(order) < n:
            t, q = 1e9, None
            for k, r in ready.items():
                if r:
                    x = max(free.get(k, 0.0), min([est[i] for i in r]))
                    if x < t: t, q = x, k
            r, a = ready[q], -1
            for i in r:
                if est[i] <= t and (a < 0 or far[i] > far[a]): a = i
            for b in r:
                if t < est[b] < t + c[a] and far[b] > far[a]:
                    if max(est[b] + far[b], est[b] + c[b] + far[a]) + est[b] - t < max(t + c[a] + far[b], t + far[a]): a, t = b, est[b]
            r.remove(a); order.append(a)
            if q != "R": free[q] = t + c[a]
            e = t + c[a] + lat[a]
            last = max(last, e)
            for k, h in after[a]:
                if e + h > est[k]: est[k] = e + h
                left[k] -= 1
                if not left[k]: ready.setdefault(Q[k], []).append(k)
        return order, last

    def replay(order, cost):
        end, free = [0.0] * n, {}
        for i in order:
            t = free.get(Q[i], 0.0)
            for j, h in before[i]:
                if end[j] + h > t: t = end[j] + h
            if Q[i] != "R": free[Q[i]] = t + cost[i]
            end[i] = t + cost[i] + lat[i]
        return max(end)

    def length(move):
        order, last = sweep([f + move.get(d["kind"], 0.0) for f, d in zip(base, nodes)])
        return last + sum(replay(order, k) for k in costs[1:]) / (len(costs) - 1), order

    def holdups(order, cost):
        end, free, why, ran, was = [0.0] * n, {}, [-1] * n, {}, [0.0] * n
        for i in order:
            t, w = 0.0, -1
            for j, h in before[i]:
                if end[j] + h > t: t, w = end[j] + h, j
            was[i] = t
            if free.get(Q[i], 0.0) > t: t, w = free[Q[i]], ran[Q[i]][-1]
            if Q[i] != "R": free[Q[i]] = t + cost[i]; ran.setdefault(Q[i], []).append(i)
            end[i], why[i] = t + cost[i] + lat[i], w
        i, pairs = max(range(n), key=lambda k: end[k]), {}
        while i >= 0:
            for j, h in [(i, 0)] + before[i]:
                r = ran.get(Q[j], [])
                k = r.index(j) - 1 if r else -1
                while k >= 0 and end[r[k]] - lat[r[k]] > was[j] + 0.05:
                    if kind[r[k]] != kind[j]: pairs[(kind[j], kind[r[k]])] = (j, r[k])
                    k -= 1
            i = why[i]
        return list(pairs.values())

    kind, move = [d["kind"] for d in nodes], {}
    now, order = length(move)
    best, seed = (now, order), 1
    for it in range(TRIES):
        if it % 8 == 0: pairs = holdups(order, costs[it // 8 % len(costs)])
        seed = (seed * 1103515245 + 12345) % 2 ** 31
        a, b = pairs[(seed >> 8) % len(pairs)]
        gap = base[b] + move.get(kind[b], 0.0) - base[a] - move.get(kind[a], 0.0) + 0.3
        trial = dict(move)
        if seed >> 7 & 1: trial[kind[a]] = trial.get(kind[a], 0.0) + max(gap, 0.5)
        else: trial[kind[b]] = trial.get(kind[b], 0.0) - max(gap, 0.5)
        e, o = length(trial)
        if e < now + SLACK * (1.0 - it / TRIES):
            now, order, move = e, o, trial
            if e < best[0]: best = (e, o)
    return best[1]


def rank_program(g, core, T, topo):
    rank = T.rank_of(core)
    if rank is None:
        return
    O = AluOpType
    nodes, hist, free = [], {}, {"d": 0, "ls": 0, "part": "0"}

    def A(name, a=None, b=None, s=1, p0=0, p1=128):
        buf, at, cols = PLACE[name]
        t = T[buf]
        a = 0 if a is None else a
        b = cols if b is None else b
        return {"n": name, "a": a, "b": b, "s": s, "k": len(range(a, b, s)), "w": SIZE[SCRATCH[buf][2]], "ps": SCRATCH[buf][0] == "psum",
                "ap": t[p0:p1, at + a:at + b:s] if s != 1 else t[p0:p1, at + a:at + b]}

    def node(q, calls, cost, writes, reads, lat=0.0, sem=None, grp=None, extra=()):
        me, deps = len(nodes), {j: False for j in extra}
        acc = [(r, False) for r in reads] + [(r, True) for r in writes]
        for x, w in acc:
            h = hist.setdefault(x["n"], [])
            if x["ps"]:
                keep = []
                for e in h:
                    if e[3] == me: continue
                    o = nodes[e[3]]
                    if grp is not None and o["grp"] is grp and e[3] != grp["first"]: keep.append(e)
                    elif o["q"] == q and not (w or e[2]): keep.append(e)
                    else:
                        deps[e[3]] = deps.get(e[3], False) or not (q == o["q"] == "P")
                        if (grp is not None and o["grp"] is grp) or (e[2] and not w): keep.append(e)
                h[:] = keep + [(0, 512, w or any(e[2] for e in h if e[3] == me), me)]
            else:
                for e in h:
                    if e[3] != me and (w or e[2]) and x["a"] < e[1] and e[0] < x["b"]:
                        k = min(x["s"], e[4])
                        if k == 1 or (x["a"] - e[0]) % k == 0 or q not in "VSP" or nodes[e[3]]["q"] not in "VSP": deps[e[3]] = True
        for x, w in acc:
            if not x["ps"]:
                h = hist[x["n"]]
                if w: h[:] = [e for e in h if not (x["a"] <= e[0] and e[1] <= x["b"] and e[4] % x["s"] == 0 and (x["a"] - e[0]) % x["s"] == 0)]
                h.append((x["a"], x["b"], w, me, x["s"]))
        nodes.append({"q": q, "calls": calls, "cost": cost, "lat": lat, "deps": deps, "sem": sem, "grp": grp, "ga": 0, "sc": 0,
                      "kind": q + free["part"] + "".join(" " + x["n"].rstrip("0123456789") for x in writes[:1] + reads[:2])})
        if isinstance(cost, tuple): nodes[-1].update({"cost": cost[0], cost[1]: cost[2]})
        return me

    def price(q, out, in_, rate):
        if "o" in in_: return (0.06, "ga", 16 * in_["o"]["k"])
        return max(64, in_["k"] * rate) * CYC
    def half(*x): return 0.5 if all(i["w"] == 2 for i in x) else 1.0
    def ind(win, off): return {"ap": win["ap"].indirect(off["ap"]), "win": win, "o": off, "w": win["w"], "ps": False}
    def rd(x): return [x["win"], x["o"]] if "o" in x else [x]
    def ap(x): return x["ap"] if isinstance(x, dict) else x
    def cols(*x): return [i for i in x if isinstance(i, dict)]
    def cp(out, in_): node("V", [lambda: g.vector.tensor_copy(out["ap"], in_["ap"])], price("V", out, in_, half(out, in_)), [out], rd(in_))
    def scat(win, off, in_): node("V", [lambda: g.vector.tensor_copy(win["ap"].indirect(off["ap"]), in_["ap"])], (0.05, "sc", in_["k"]), [win], [off, in_])
    def tt(out, a, b, op):
        rate = 1.0 if a["ps"] or b["ps"] else 2.0 * half(out, a, b)
        node("V", [lambda: g.vector.tensor_tensor(out["ap"], a["ap"], b["ap"], op)], price("V", out, a, rate), [out], rd(a) + [b])
    def ts(out, a, s1, op0, s2=None, op1=None):
        f = (lambda: g.vector.tensor_scalar(out["ap"], a["ap"], ap(s1), None, op0)) if op1 is None else \
            (lambda: g.vector.tensor_scalar(out["ap"], a["ap"], ap(s1), ap(s2), op0, op1))
        node("V", [f], price("V", out, a, half(out, a)), [out], rd(a) + cols(s1, s2))
    def scan(out, d0, d1, init, op0, op1):
        node("V", [lambda: g.vector.tensor_tensor_scan(out["ap"], d0["ap"], d1["ap"], init, op0, op1)], price("V", out, d1, half(out, d0, d1)), [out], [d0, d1])
    def fill(out, v): node("V", [lambda: g.vector.memset(out["ap"], v)], price("V", out, out, half(out)), [out], [])
    def reduce(out, in_, op): node("V", [lambda: g.vector.tensor_reduce(out["ap"], in_["ap"], AxisListType.X, op)], price("V", out, in_, 1.0), [out], [in_])
    def turn32(out, in_): node("V", [lambda: g.vector.transpose(out["ap"], in_["ap"])], price("V", out, in_, 1.0), [out], [in_])
    def act(out, in_, func=AF.Copy, bias=0.0, scale=1.0, acc=None):
        r = rd(in_) + cols(bias, scale)
        if acc is None: node("S", [lambda: g.scalar.activation(out["ap"], in_["ap"], func, bias=ap(bias), scale=ap(scale))], price("S", out, in_, 1.0), [out], r)
        else: node("S", [lambda: g.scalar.activation(out["ap"], in_["ap"], func, bias=bias, scale=ap(scale), accum_out=acc["ap"])], price("S", out, in_, 1.0) + 0.02, [out, acc], r)
    def copy(who, out, in_): (cp if who == "V" else act)(out, in_)
    def mms(parts, grp=None):
        first = grp is None or "first" not in grp
        if grp is not None:
            if first: grp["first"] = len(nodes); grp["n"] = 0
            grp["n"] += 1
        calls = [(o["ap"], l["ap"], r["ap"], first and i == 0) for i, (o, l, r) in enumerate(parts)]
        cost = sum(max(64, r["k"]) * (4 if r["w"] == 4 else 1) * CYC / 2 for o, l, r in parts)
        node("P", calls, cost, [parts[0][0]], [x for o, l, r in parts for x in (l, r)], grp=grp)
    def parts(all_, k, grp=None):
        grp = {} if grp is None else grp
        for i in range(0, len(all_), k): mms(all_[i:i + k], grp)
    def iota(out, pat, base=0, cm=0):
        if out["w"] == 4 and PLACE[out["n"]][0].endswith("int32"): f = lambda: g.iota(out["ap"], pat, base, cm)
        else: f = lambda: g.iota(out["ap"], pat, base, cm, allow_small_or_imprecise_dtypes=True)
        node("G", [f], 0.13 + 2 * out["k"] * CYC, [out], [])
    def dma(out, in_, reads, writes, kb, q="D"):
        s = "d%d" % free["d"]; free["d"] += 1
        f = g.sync if q == "D" else g.scalar
        free["last"] = [node("D", [lambda: f.dma_start(out, in_)], kb / 200.0, writes, reads, lat=2.0, sem=(s, 16), extra=free.get("last", ()))]

    def sides(c):
        r = T.rank_of(c)
        two = (T.cores[(r - 1) % 8], T.cores[(r + 1) % 8])
        far = [d for d in two if topo.chip(d) != topo.chip(c)]
        out = []
        for d in two:
            e = topo.engines(c, d)
            if d not in far: e = [i for i in e if not far or i not in topo.engines(c, far[0])] or e
            elif len(far) == 2: e = e[:len(e) // 2] if d == far[0] else e[len(e) // 2:]
            out.append((d, e))
        return out
    NE = min(len(e) for c_ in T.cores for _, e in sides(c_))

    def send(pairs, sem, us, once=0.0):
        s = "ls%d" % free["ls"]; free["ls"] += 1
        n, tr = NE // len(pairs), []
        for side, (d, e) in zip("AB", sides(core)):
            rid, pid, _ = topo.addr(d)
            for i, p in enumerate(pairs):
                tr.append(RemoteDMATransfer(dst_ids=[DstId(rid=rid, pnc=pid)], dma_engine_mask=sum(1 << k for k in e[i * n:i * n + n]),
                                            remote_sem=T.sem[sem % side], src=p[0]["ap"], dst=p[1 if side == "A" else 2]["ap"]))
        me = node("G", [lambda: g.remote_dma_fused(tr, local_sem=T.sem[s])], 1.0 + once, [], [p[0] for p in pairs], lat=1.0, sem=(s, n * len(tr)))
        for i, side in enumerate("AB"): node("R", [], 0.0, [p[1 + i] for p in pairs], [], lat=us + 1.0, sem=(sem % side, n * len(pairs)), extra=[me])
        return me

    def load(name, a, src, c0=0, c1=V, kb=256): dma(A(name, a + c0, a + c1)["ap"], src[:, c0:c1], [], [A(name, a + c0, a + c1)], kb * (c1 - c0) / V)
    load("pb", 0, T.past, 0, G5); load("rb", DUM, T.reach, 0, G5)
    load("ci", 0, T.cand, kb=512); load("xw", 0, T.x)
    load("rb", DUM, T.reach, G5, V); load("pb", 0, T.past, G5, V)
    dma(A("thi", 0, 1, p1=8)["ap"], T.th[:], [], [A("thi")], 1)
    gh = {"ra": A("rb", DUM + V, DUM + V + G5), "rb": A("rb", DUM + V + G5, DUM + 2 * V), "pa": A("pb", V, V + G5), "pb": A("pb", V + G5, 2 * V)}
    send([(A("pb", 0, G5), gh["pa"], gh["pb"])], "ip%s", 2.5, 2.0)
    sent = send([(A("rb", DUM, DUM + G5), gh["ra"], gh["rb"])], "ir%s", 2.5)
    node("G", [lambda: g.sem_inc(T.sem["go"], 1)], 0.05, [A("gate")], [], sem=("go", 1), extra=[sent])
    dma(A("si")["ap"], T.succ[:], [A("gate")], [A("si")], 512)
    dma(A("xq", 0, V)["ap"], T.x[:], [A("gate")], [A("xq", 0, V)], 256)
    dma(A("p0_")["ap"], T.past[:], [A("gate")], [A("p0_")], 256)
    for who, (n, o, w) in zip(COPIES, (("xq", V, A("xw", 0, V)), ("rq", 0, A("rb", DUM, DUM + V)), ("rq", V, A("rb", DUM, DUM + V)),
                                       ("pq", 0, A("pb", 0, V)), ("pq", V, A("pb", 0, V)))): copy(who, A(n, o, o + V), w)
    for n in ("pa", "pb", "ra", "rb"):
        w = A(n[0] + "w" + n[1], 0, G5)
        dma(w["ap"], gh[n]["ap"], [gh[n]], [w], 128)

    c = lambda i: A("cc", i, i + 1)
    ROW, P16, PF, ODD, RS, RG0, RG1, C1L, C1R, E12, E15, L10, M2, TH, NG, LIM, EVR, W0, W1, W2, W3, W4, W5, CA = range(24)
    PM, CL = 28, 32
    rw, pp = A("pc", 1, 2), A("pc", 0, 1)
    iota(pp, [[0, 1]], 0, 1)
    iota(A("id_", 0, 16), [[32, 8], [-16, 2]], 16, 1); iota(A("id_", 16, 32), [[1, 16]])
    iota(A("ie"), [[1, 128]]); iota(A("ig", 0, 8), [[1, 8]]); iota(A("ik"), [[1, 8], [0, 16]])
    iota(A("ib"), [[0, 16], [1, 16]]); iota(A("ic"), [[1, 256]])
    iota(A("ih", 0, 16), [[1, 2], [2, 8]])
    iota(A("ij", 0, 64), [[1, 4], [64, 16]], V, 4); iota(A("in_", 0, 32), [[-8, 2], [1, 16]]); iota(A("id_", 32, 64), [[16, 32]], 0, 1)
    fill(A("xw", V, 2 * V), PEN); fill(A("bw", V, 2 * V), 1.0)
    ts(rw, pp, 15, O.bitwise_and)
    ts(A("pc", 2, 3), pp, 4, O.arith_shift_right)
    ts(A("pc", 3, 4), pp, 4, O.arith_shift_right, 1, O.bitwise_and)
    ts(A("pc", 4, 5), rw, 1, O.arith_shift_right)
    ts(A("pc", 5, 6), rw, 1, O.bitwise_and)
    ts(A("pc", 6, 7), rw, 3, O.bitwise_and)
    cp(c(ROW), rw); cp(c(P16), A("pc", 2, 3)); cp(c(PF), pp); cp(c(RG1), A("pc", 3, 4)); cp(c(W0), A("pc", 4, 5)); cp(c(ODD), A("pc", 5, 6))
    ts(c(RG0), c(RG1), -1.0, O.mult, 1.0, O.add)
    ts(c(EVR), c(ODD), -1.0, O.mult, 1.0, O.add)
    ts(c(NG), c(P16), -16.0, O.mult)
    ts(A("o2"), A("id_", 0, 16), c(NG), O.add)
    tt(c(W1), c(ODD), c(RG1), O.not_equal)
    ts(c(W2), c(W0), 32.0, O.mult)
    ts(c(W1), c(W1), 256.0, O.mult, c(W2), O.add)
    ts(c(W3), c(RG1), 16.0, O.mult, c(W1), O.add)
    ts(A("ofin"), A("id_", 16, 32), c(W3), O.add)
    W = lambda n, m: A(n, 128 * m, 128 * m + 128)
    ts(A("g8"), A("ig", 0, 8), c(P16), O.is_equal)
    fill(A("wm"), 0.0)
    for m in range(16): act(A("wm", 128 * m + m, 128 * m + 128, 16), A("g8"))
    ts(A("idm"), A("ie"), c(PF), O.is_equal)
    for n, v in (("ngm", -1.0), ("hm", 0.5), ("bgm", 4096.0), ("nbm", -4096.0), ("zm", 0.0), ("idf", 1.0)): act(A(n), A("idm"), scale=v)
    ts(A("kc"), A("ic"), 2.0 ** -21, O.mult)
    fill(A("smx"), 0.0); fill(A("smx", 0, 1024, 8), 255.0)
    fill(A("sg1"), 1.0); fill(A("sg1", 0, 256, 16), 0.0); fill(A("mh"), -0.5)
    ts(A("dg", 0, 256), A("ib"), c(ROW), O.is_equal)
    ts(c(L10), c(ROW), 10.0, O.is_lt); ts(c(C1L), c(ROW), 13.0, O.is_ge); ts(c(E12), c(ROW), 12.0, O.is_equal); ts(c(E15), c(ROW), 15.0, O.is_equal)
    ts(c(W4), c(ROW), 13.0, O.is_lt, c(L10), O.subtract); cp(c(C1R), c(W4))
    ts(c(M2), c(C1R), c(E12), O.subtract)
    ts(c(CL), c(ROW), 13.0, O.not_equal, -2.0 ** 22, O.mult); ts(c(CL), c(CL), -100.0 * 2 ** 14, O.add)
    for a, b, v in ((0, 10, 2.0 ** 20), (10, 11, 2.0 ** 14), (11, 12, 256.0), (12, 13, 1.0), (13, 14, -2.0 ** 14), (14, 15, -256.0), (15, 16, -1.0)): fill(A("wv", a, b), v)
    tt(A("wx"), A("wv"), A("dg", 0, 16), O.mult); reduce(c(RS), A("wx"), O.add)
    act(A("cll"), A("ic"), AF.Identity, bias=c(C1L), scale=c(E12)); act(A("clr"), A("ic"), AF.Identity, bias=c(C1R), scale=c(E15))
    act(A("s10"), A("idm"), scale=c(L10))
    ts(A("wm2"), A("wm"), c(M2), O.mult)
    for m in range(16):
        if m % 4 < RO - 1: act(W("wmn", m), W("wm", m), scale=-1.0)
    if "V" in DIST + DIST0:
        ts(A("wmx"), A("wm"), -2.0 ** -13, O.mult)
        dma(A("xq", 2 * V, 3 * V)["ap"], T.x[:], [A("gate")], [A("xq", 2 * V, 3 * V)], 256)
    ts(A("bom"), A("ik"), c(P16), O.is_equal)
    ts(A("lw"), A("dg", 0, 16), 1024.0, O.mult)
    for m in range(16): act(W("wt", m), A("bom"), scale=A("lw", m, m + 1))
    act(A("nw"), W("wt", 12), scale=-PEN / 1024)
    ts(A("lh"), A("ie"), c(PF), O.is_lt, -1.0, O.mult); tt(A("lh"), A("lh"), A("bom"), O.mult); tt(A("ltm"), A("lh"), A("nbm"), O.add)
    fill(A("one"), 1.0); fill(A("onm"), 1.0); fill(A("e5"), 0.0)
    cp(c(W5), A("pc", 6, 7))
    for t in range(RO - 1): ts(c(PM + t), c(W5), float(t), O.is_le)
    for r in range(5): iota(A("pat", 32 * r, 32 * r + 32), [[0, 16 >> r], [2, 2], [0, 1 << r]], -1)
    iota(A("pat", 160, 192), [[1, 32]]); iota(A("pat", 192, 224), [[32, 32]])
    pt = lambda i: A("pat", 32 * i, 32 * i + 32)
    mms([(A("p6", 0, 32), W("wm", r), pt(r)) for r in range(5)] + [(A("p6", 0, 32), W("wm", 11), pt(5))])
    mms([(A("p6", 32, 64), W("wm", r + 5), pt(r)) for r in range(5)] + [(A("p6", 32, 64), W("wm", 10), pt(6))])
    act(A("tc"), A("p6", 0, 32), scale=1.0 / 16); act(A("ta"), A("p6", 32, 64), scale=1.0 / 16)
    for a in range(32): act(A("bw", DUM + 32 * a, DUM + 32 * a + 32), A("tc"), AF.Identity, bias=A("ta", a, a + 1))
    ts(A("bs"), A("bw", DUM, DUM + V), c(E12), O.add)
    iota(A("pa"), [[0, 128], [128, 4]], 128); iota(A("pb_"), [[0, 128], [-1, 4]], 3); iota(A("pc_"), [[-1, 128], [0, 4]], 127)
    mms([(A("p6"), W("wm", m), A(n)) for m, n in enumerate(("pa", "pb_", "pc_", "pc_", "pc_"))])
    act(A("dig"), A("p6"), scale=1.0 / 16)
    for par in range(2):
        ts(c(CA + par), c(NG), -1.0, O.mult, c(W0), O.add)
        if par: ts(c(CA + par), c(CA + par), 8.0, O.add)
        ts(A("la%d" % par), A("ie"), c(CA + par), O.is_equal, c(ODD), O.mult); ts(A("lb_%d" % par), A("ie"), c(CA + par), O.is_equal, c(EVR), O.mult)
    cp(A("oh"), A("dg", 0, 16)); fill(A("pen"), 0.0); cp(A("omx"), A("ih", 0, 16))
    for a in range(16):
        o = 128 * (a % 2) + 16 * (a // 2)
        if a == 0: ts(A("thr"), A("dg", 0, 256), -1e9, O.mult, 1e9, O.add)
        if PAIRS[a] == "V": ts(A("thr", o, o + 16), A("dg", 0, 16), B10 - 1e9, O.mult, 1e9, O.add)
    ts(A("rs"), A("in_", 0, 32), c(P16), O.is_equal, 4096.0, O.mult)
    ts(c(CL + 1), c(NG), 4.0, O.mult); ts(A("vs"), A("ij", 0, 64), c(CL + 1), O.add)
    ts(A("vd"), A("id_", 32, 48), c(NG), O.add, 2.0 * V, O.add)
    ts(A("fvs"), A("id_", 32, 64), c(NG), O.add); ts(A("flo"), A("id_", 32, 64), c(NG), O.add)
    ts(A("b8"), A("ik"), c(PF), O.is_equal)
    cp(A("thf", 0, 1, p1=8), A("thi", 0, 1, p1=8))
    mms([(A("p7", 0, 1), A("b8", p1=8), A("thf", 0, 1, p1=8))])
    ts(c(TH), A("p7", 0, 1), 256.0, O.mult); cp(c(LIM), c(TH))
    for n, i in (("cb", "ci"), ("sb", "si")):
        cp(A(n, 0, V), A(i)); dma(A(n, V, 2 * V)["ap"], A(n, 0, V)["ap"], [A(n, 0, V)], [A(n, V, 2 * V)], 512)

    key = {}

    def turn(t):
        if t: act(A("in12", 0, 256), A("cb", t, V, 4))
        else: cp(A("in12", 0, 256), A("ci", t, V, 4))
        act(A("in12", 256, 512), ind(A("in12", 0, 256), A("o2")))
        for h in range(2): turn32(A("tr12", 256 * h, 256 * h + 256), A("in12", 256 * h, 256 * h + 256))
        if t:
            act(A("ca%d" % t), ind(A("tr12"), A("ofin"))); cp(A("ct%d" % t), A("ca%d" % t))
        else:
            cp(A("ct0"), ind(A("tr12"), A("ofin"))); act(A("ca0"), ind(A("tr12"), A("ofin")))

    def even_list(t):
        mms([(A("p6", 0, 128), A("lb_%d" % par), A("sb", t + 4 * par, V, 8)) for par in range(2)])
        cp(A("lb%d" % t), A("p6", 0, 128))

    def squeeze(n, i, w, by="wm"):
        p, o = "p%d" % (4 + i // 4), 32 * (i % 4)
        parts([(A(p, o, o + 32 * w), W(by, m), A(n, 512 * i + m, 512 * (i + w), 16)) for m in range(16)], 16 // max(w, 2), key[p])

    def distances(t):
        for h in range(2):
            p = "p%d" % (4 + h); key[p] = {}
            mms([(A(p, 0, 128), A("idm"), A("kc", 128 * h, 128 * h + 128))], key[p])
        mine = A("xq", V + t, 2 * V, 4)
        for h in range(8):
            p, x = "p%d" % (h % 2), A("xg", 512 * h, 512 * h + 512)
            if (DIST if t else DIST0)[h // 2] == "V":
                tt(x, ind(A("xw", 0, 2 * V), A("ct%d" % t, 32 * h, 32 * h + 32)), A("xq", V + t, 3 * V, 4), O.subtract)
                ts(A("ad", 512 * h, 512 * h + 512), x, 0.0, O.max, 2.0 ** -12, O.mult)
                if h % 2: squeeze("xg", h - 1, 2, "wmx"); squeeze("ad", h - 1, 2)
                continue
            if h % XW == 0: act(A("xg", 512 * h, 512 * (h + XW)), ind(A("xw", 0, 2 * V), A("ct%d" % t, 32 * h, 32 * (h + XW))))
            mms([(A(p), A("idm"), x), (A(p, 0, 256), A("ngm"), mine), (A(p, 256, 512), A("ngm"), mine)])
            act(A("ad", 512 * h, 512 * h + 512), A(p), AF.Abs, scale=2.0 ** -13)
            if h % 4 == 3: squeeze("ad", h - 3, 4)

    def tests(t):
        k = 0
        for lo in (0, 4):
            for kind in "PR":
                win, mine, n = (A("pb", 0, 2 * V), A("rq", t, 2 * V, 4), "tp") if kind == "P" else (A("rb", 0, 2 * V), A("pq", t, 2 * V, 4), "tr")
                for h in range(lo, lo + 4):
                    off, out = A("ct%d" % t, 32 * h, 32 * h + 32), A(n, 512 * h, 512 * h + 512)
                    if (TESTS if t else TESTS0)[kind][h] == "V": tt(out, ind(win, off), mine, O.is_ge if kind == "P" else O.is_le)
                    else:
                        p, x = "p%d" % (2 + k % 2), A("gp", 512 * k, 512 * k + 512); k += 1
                        act(x, ind(win, off))
                        mms([(A(p), A("idm"), x), (A(p), A("ngm"), mine)])
                        act(out, A(p), AF.Relu, bias=1.0, scale=1.0 if kind == "P" else -1.0)
                    if lo and kind == "R":
                        if h > 4: squeeze(n, h - (h == 5), 1 + (h == 5))
                    elif h % 4 == 3: squeeze(n, h - 3, 4)

    sl, sc = A("l3", 0, 16), A("l3", 16, 32)

    def partner(t):
        act(A("klo"), A("p4", 0, 128))
        tt(A("k8"), A("p5", 0, 128), A("klo"), O.min)
        for a, b, w in (("k8", "k4", 64), ("k4", "k2", 32), ("k2", "k1", 16)): tt(A(b), A(a, 0, w), A(a, w, 2 * w), O.min)
        ts(A("mk"), A("k1"), 2.0 ** 21, O.mult, 2.0 ** 22, O.min)
        ts(A("kq"), A("mk"), 255, O.bitwise_and); cp(A("kqu"), A("kq"))
        tt(A("cm"), ind(A("ca%d" % t), A("kqu")), A("dg", 0, 256), O.mult)
        scan(A("cs"), A("sg1"), A("cm"), 0.0, O.mult, O.add)
        cp(A("cu"), A("cs", 15, 256, 16))
        cp(A("bits"), ind(A("bw", 0, 2 * V), A("cu")))
        tt(A("r2s"), ind(A("rb", 0, 2 * V), A("cu")), A("rq", V + t, 2 * V, 4), O.min)
        ts(A("kl", 0, 16), A("mk"), 14, O.arith_shift_right, 63, O.bitwise_and)
        ts(A("kl", 16, 32), A("mk"), 8, O.arith_shift_right, 63, O.bitwise_and)
        ts(A("pen", 0, 16), A("mk"), c(LIM), O.is_ge, 128.0, O.mult)
        tt(A("klf", 0, 32), A("kl"), A("pen"), O.add)
        for m in range(16): act(A("ke", m, 512, 16), A("klf", 0, 32), scale=A("oh", m, m + 1))
        for p, cl, r in (("p4", "cll", 10), ("p5", "clr", 13)):
            grp, o = {}, A(p, 0, 256)
            mms([(o, A("idm"), A(cl))], grp); mms([(o, A("s10"), A("bits"))], grp)
            mms([(o, W("wm", r), A("ke", 0, 256)), (o, W("wm", r + 1), A("ke", 256, 512))], grp)
        ts(A("fr"), A("p5", 0, 256), c(RS), O.mult, c(CL), O.max)
        act(A("fev"), A("p4", 0, 256), scale=c(RG0)); act(A("fod"), A("p4", 0, 256), scale=c(RG1))
        seen = {"V": 0, "S": 0}
        for gr in (0, 2, 4, 6, 1, 3, 5, 7):
            who = PAIRS[2 * gr]
            p = {"V": ("p0", "p2", "p5"), "S": ("p1", "p3", "p4")}[who][seen[who] % 3]
            seen[who] += 1
            lo = 32 * (gr // 2)
            for h in range(2):
                mms([(A(p, 256 * h, 256 * h + 256), A("fod" if gr % 2 else "fev", 128 * h, 128 * h + 128, p0=lo, p1=lo + 32), A("fr", p0=lo, p1=lo + 32))])
            for a in (2 * gr, 2 * gr + 1):
                o = A(p, 256 * (a % 2), 256 * (a % 2) + 256)
                if who == "V": reduce(A("mx", a, a + 1), o, O.max)
                else: act(A("junk", 256 * a, 256 * a + 256), o, AF.Relu, bias=-B10, acc=A("mx", a, a + 1))
        tt(A("we"), ind(A("mx"), A("omx")), A("thr"), O.is_gt)
        grp, o = {}, A("p7", 0, 16)
        parts([(o, W("wm2", m), A("bits", m, 256, 16)) for m in range(16)], 4, grp)
        mms([(o, A("we", 128 * h, 128 * h + 128), A("rs", 16 * h, 16 * h + 16)) for h in range(2)], grp)
        tt(A("t3", 16, 32), o, A("vd"), O.min); tt(A("t3", 0, 16), o, A("vs", 16 * t, 16 * t + 16), O.min)
        cp(A("l3"), A("t3"))
        if t + 1 < RO: ts(A("wn"), o, float(V), O.is_lt)

    def merge(t):
        grp, w = {}, A("rb", t, V, 4)
        scat(A("rb"), sc, A("r2s"))
        act(A("rbv"), ind(A("rq"), sl)); act(A("sx"), ind(A("sb"), sl))
        mms([(A("p2", 0, 256), W("wt", 12), A("bw", t, V, 4))], grp); mms([(A("p2", 0, 256), A("idm"), A("rbv"))], grp)
        tt(w, w, A("p2", 0, 256), O.min)
        tt(A("r2"), A("rbv"), A("rq", V + t, 2 * V, 4), O.min)
        mms([(A("p5", 0, 128), A("la%d" % par), A("sx", par, 256, 2)) for par in range(2)])
        cp(A("la"), A("p5", 0, 128))

    def count():
        mms([(A("p7", 448, 464), A("onm"), A("wn"))])
        reduce(A("mt", 0, 1), A("p7", 448, 464), O.add)
        cp(A("mi", 0, 1), A("mt", 0, 1)); ts(A("mi", 1, 2), A("mi", 0, 1), 31, O.bitwise_and)
        ts(c(LIM), A("mi", 1, 2), 256.0, O.mult, c(TH), O.add)

    def names(t):
        scat(A("bw"), sc, A("bs", t, V, 4))
        mms([(A("p7", 128, 192), W("wm2", m), A("bw", DUM + m, DUM + V, 16)) for m in range(16)])
        f = A("p7", 128, 160)
        if AGAIN != "XXX": cp(A("flu"), A("p7", 128, 192))
        tt(A("chf"), f, A("flo"), O.not_equal); cp(A("flo"), f)
        ts(A("flt"), f, float(G5), O.is_lt); tt(A("dfl"), f, A("fvs"), O.subtract); tt(A("dfl"), A("dfl"), A("flt"), O.mult)

    def block(kind, t):
        o = G5 + 128 * t
        send([(A("%sn%d" % (kind, t), 0, 128), A(kind + "wa", o, o + 128), A(kind + "wb", o, o + 128))], "a%s%%s%d" % (kind, t), 1.5)

    def pmerge(t):
        tt(A("pn%d" % t), ind(A("pq"), sl), A("p0_", t, V, 4), O.max)
        block("p", t)
        cp(A("pq", t, V, 4), A("pn%d" % t))

    def xmerge(t):
        grp, o = {}, A("p3", 0, 256)
        act(A("xp"), ind(A("xq", 0, 2 * V), sl))
        mms([(o, A("hm"), A("xq", V + t, 2 * V, 4)), (o, A("hm"), A("mh"))], grp); mms([(o, A("hm"), A("xp"))], grp)
        ts(A("xq", t, V, 4), o, MAGIC, O.add, MAGIC, O.subtract)

    def successors(t, h):
        free["part"] = free["part"][:last] + "ab"[h]
        for i in (2 * h, 2 * h + 1):
            a, b = A("sga", 512 * i, 512 * i + 512), A("sgb", 512 * i, 512 * i + 512)
            act(b, ind(A("rb", 0, 2 * V), A("lb%d" % t, 32 * i, 32 * i + 32)))
            tt(a, ind(A("rb", 0, 2 * V), A("la", 32 * i, 32 * i + 32)), b, O.min)
        o = 1024 * h
        scan(A("sc", o, o + 1024), A("smx"), A("sga", o, o + 1024), 255.0, O.max, O.min)
        tt(A("rn%d" % t, 128 * h, 128 * h + 128), A("sc", o + 7, o + 1024, 8), A("r2", 128 * h, 128 * h + 128), O.min)

    def publish(t):
        grp, o = {}, A("p7", 256, 288)
        mms([(o, A("idm"), A("chf"))], grp)
        for by, n in (("wm", "rq"), ("wmn", "pq")): mms([(o, W(by, 4 * a + t), A(n, V + t + 4 * a, V + G5, 16)) for a in range(4)], grp)
        for by, n in (("wm", "pn"), ("wmn", "rn")): mms([(o, W(by, 4 * a + t), A(n + str(t), a, 128, 4)) for a in range(4)], grp)
        ts(A("ch"), o, 0.0, O.is_gt)
        scan(A("scq"), A("one"), A("ch"), 0.0, O.mult, O.add)
        grp, o = {}, A("p7", 320, 352)
        mms([(o, A("ltm"), A("ch"))], grp); mms([(o, A("bom"), A("scq"))], grp)
        ts(A("go"), o, CAP - 4096.0, O.is_le)
        grp, rows = {}, [m for m in range(16) if m % 4 <= t]
        mms([(A("p6"), A("zm"), A("dig"))], grp)
        if t: mms([(A("p6", m, G5, 16), W("wt", m), A("e5")) for m in rows], grp)
        mms([(A("p6", m, G5, 16), W("wt", m), A("go")) for m in rows], grp)
        tt(A("dt"), A("p6"), A("dig"), O.min)
        tt(A("gf"), A("go"), A("dfl"), O.mult); tt(A("fvs"), A("fvs"), A("gf"), O.add); cp(A("fu"), A("fvs"))
        copy(DGT, A("dgt"), ind(A("dt"), A("fu")))
        grp, o = {}, A("p7", 384, 416)
        mms([(o, A("idf"), A("fvs"))], grp); mms([(o, W("wm", m), A("dgt", m, G5, 16)) for m in range(16)], grp)
        cp(A("z%d" % t), o)
        send([(A("z%d" % t), A("lz%d" % t, 0, 32), A("lz%d" % t, 32, 64))], "az%%s%d" % t, 1.2)
        if t + 2 < RO:
            ts(A("ge"), A("go"), c(PM + t), O.mult); tt(A("e5"), A("e5"), A("ge"), O.add)

    def candidates(t):
        grp, own = {}, A("cb", t, V, 4)
        for n in ("tp", "tr"):
            parts([(A("p6", 0, 256), W("wm", k), A(n, 256 * k, 256 * k + 256)) for k in range(16)], 2, grp)
        act(A("os"), A("p6", 0, 256), AF.Sign)
        grp, o = {}, A("p6", 256, 272)
        ts(A("nh"), A("mk"), 2.0 ** 21, O.is_ge, 4096.0, O.mult)
        parts([(o, A("idm"), A("nh"))] + [(o, W("wm2", m), A("bits", m, 256, 16)) for m in range(16)], 6, grp)
        tt(A("bc"), o, A("vs", 16 * t, 16 * t + 16), O.min); cp(A("bcu"), A("bc"))
        act(A("cx"), ind(A("cb"), A("bcu")))
        for o, m in ((0, "bgm"), (256, "nbm")): mms([(A("p6", o, o + 256), A("idf"), own), (A("p6", o, o + 256), A(m), A("os"))])
        tt(A("cy"), A("p6", 0, 256), A("cx"), O.min)
        tt(own, A("p6", 256, 512), A("cy"), O.max)

    def again(n, win, t):
        who = AGAIN["xpr".index(n)]
        if who != "X":
            if n == "x": fill(A("xq", t + 1, V, 4), PEN)
            copy(who, A(win, 0, V), ind(A(n + "q", 0, V), A("flu")))
            return
        new = A("xq", t, V, 4) if n == "x" else A("%sn%d" % (n, t))
        o, w, grp = A({"x": "p0", "p": "p3", "r": "p2"}[n], 0, 256), A(win, t, V, 4), {}
        scat(A(win), sc, new)
        mms([(o, A("nw") if n == "p" else W("wt", 12), A("bw", t, V, 4))], grp); mms([(o, A("idm"), new)], grp)
        tt(w, w, o, O.max if n == "p" else O.min)
        if n == "x":
            o, w = A("p1", 0, 256), A(win, t + 1, V, 4)
            mms([(o, A("idm"), A("xw", V, V + 256)), (o, A("nw"), A("bw", t + 1, V, 4))])
            tt(w, w, o, O.max)

    turn(0)
    fill(A("xw", 0, V, 4), PEN)
    distances(0)
    even_list(0)
    for t in range(RO):
        last = t == RO - 1
        tests(t)
        free["part"] = "3" if last else ""
        if not last:
            turn(t + 1); even_list(t + 1)
        partner(t)
        candidates(t)
        merge(t)
        if not last:
            names(t); pmerge(t)
        xmerge(t)
        if last:
            dma(T.yc[:], A("cb", 0, V)["ap"], [A("cb", 0, V)], [], 512)
            dma(T.yx[:], A("xq", 0, V)["ap"], [A("xq", 0, V)], [], 256)
            for h in range(2):
                successors(t, h)
                o = G5 * h
                cp(A("rq", o + t, o + G5, 4), A("rn%d" % t, 128 * h, 128 * h + 128))
                dma(T.yr[:, o:o + G5], A("rq", o, o + G5)["ap"], [A("rq", o, o + G5)], [], 128)
            continue
        act(A("sb", t, V, 4), A("sx"))
        successors(t, 0)
        block("r", t)
        publish(t)
        count()
        successors(t, 1)
        again("x", "xw", t)
        distances(t + 1)
        again("p", "pb", t)
        cp(A("rq", t, V, 4), A("rn%d" % t))
        again("r", "rb", t)
        for who, n in zip(GHOST, ("pa", "pb", "ra", "rb")):
            o = 32 * "ab".index(n[1])
            copy(who, gh[n], ind(A(n[0] + "w" + n[1], 0, G5 + 128 * (t + 1)), A("lz%d" % t, o, o + 32)))

    if "order" not in ORDER: ORDER["order"] = plan(nodes)
    queues = {"V": g.vector, "S": g.scalar, "P": g.tensor, "G": g, "D": g.sync}
    cnt = {"qV": 0, "qS": 0, "qP": 0, "qG": 0}
    know, snap, done = {q: {} for q in queues}, {}, {}

    def wait(q, sem, val):
        if know[q].get(sem, 0) < val:
            queues[q].wait_ge(T.sem[sem], val)
            for k, v in snap.get((sem, val), {}).items():
                if know[q].get(k, 0) < v: know[q][k] = v
            know[q][sem] = val

    for i in ORDER["order"]:
        d = nodes[i]
        q = d["q"]
        if q == "R":
            done[i] = d["sem"]; continue
        need = {}
        for j, s in d["deps"].items():
            if s and need.get(done[j][0], 0) < done[j][1]: need[done[j][0]] = done[j][1]
        for s in sorted(need): wait(q, s, need[s])
        if d["sem"] is not None:
            r = d["calls"][0]()
            if q == "D": r.then_inc(T.sem[d["sem"][0]], 16)
            done[i] = d["sem"]
        else:
            s = "q" + q
            if d["grp"] is not None: d["grp"]["n"] -= 1
            for k, f in enumerate(d["calls"]):
                if q == "P": r = g.tensor.matmul(f[0], f[1], f[2], f[3], k == len(d["calls"]) - 1 and (d["grp"] is None or d["grp"]["n"] == 0))
                else: r = f()
                r.then_inc(T.sem[s], 1); cnt[s] += 1
            done[i] = (s, cnt[s])
        snap[done[i]] = dict(know[q])
    for i, d in enumerate(nodes):
        if d["q"] == "G" and d["sem"] is not None: wait("G", *d["sem"])
    for s in sorted(cnt): wait("G", s, cnt[s])
    for i in range(free["d"]): wait("D", "d%d" % i, 16)
